import numpy as np
import ml_dtypes


def mxq(x, axis, fmt="e4m3"):
    dtype, down = {"e4m3": (ml_dtypes.float8_e4m3fn, 7), "e5m2": (ml_dtypes.float8_e5m2, 14)}[fmt]
    v = np.moveaxis(np.asarray(x, np.float32).astype(ml_dtypes.bfloat16).astype(np.float64), axis, -1)
    blocks = v.reshape(v.shape[:-1] + (-1, 32))
    amax = np.abs(blocks).max(-1, keepdims=True)
    byte = np.maximum(np.where(amax > 0, np.frexp(amax)[1] - 1 + 127, 0) - down, 1)
    scale = np.exp2(byte - 127.0)
    codes = (blocks / scale).astype(np.float32).astype(dtype).astype(np.float64)
    return np.moveaxis((codes * scale).reshape(v.shape), -1, axis)


WIDE = False


def mx_kscale(k):
    if not WIDE:
        return np.ones(k)
    levels = np.array([10, -10, 5, -5, 0])
    if k % 512:
        return np.exp2(np.random.permutation(np.resize(levels, k // 32))).repeat(32)
    a = np.empty((k // 512, 16))
    for p in range(k // 512):
        a[p, :8] = np.random.permutation(np.resize(levels, 8))
        for g in range(8):
            far = levels[np.abs(levels - a[p, g]) >= 10]
            a[p, g + 8] = far[np.random.randint(len(far))]
    return np.exp2(a.ravel()).repeat(32)


BF16 = ml_dtypes.bfloat16


def bf(x):
    return np.asarray(x, np.float32).astype(BF16)


def f64(x):
    return np.asarray(x).astype(np.float64)


E2M1 = np.array([0.0, 0.5, 1.0, 1.5, 2.0, 3.0, 4.0, 6.0, -0.0, -0.5, -1.0, -1.5, -2.0, -3.0, -4.0, -6.0])


def pack_weight(w, fmt):
    k, n = w.shape
    w = f64(bf(w)).reshape(k // 32, 32, n)
    amax = np.abs(w).max(1)
    if fmt == "e4m3":
        byte = np.frexp(amax)[1] - 1 + 127 - 7
    else:
        mant, ex = np.frexp(amax / 6.0)
        byte = np.where(mant > 0.5, ex, ex - 1) + 127
    byte = np.clip(np.where(amax > 0, byte, 1), 1, 254)
    scaled = (w * np.exp2(127.0 - byte)[:, None, :]).reshape(k, n).astype(np.float32)
    by_word = np.ascontiguousarray(scaled.reshape(k // 512, 128, 4, n).transpose(0, 1, 3, 2))
    if fmt == "e4m3":
        words = by_word.astype(ml_dtypes.float8_e4m3fn).view(np.uint8)
    else:
        c = by_word.astype(ml_dtypes.float4_e2m1fn).view(np.uint8) & 0xF
        words = c[..., 0::2] | (c[..., 1::2] << 4)
    return np.ascontiguousarray(words), np.ascontiguousarray(byte.astype(np.uint8).reshape(k // 512, 16, n))


def unpack_weight(words, scales, fmt):
    g, p, n, _ = words.shape
    if fmt == "e4m3":
        vals = np.ascontiguousarray(words).view(ml_dtypes.float8_e4m3fn).astype(np.float64)
    else:
        nib = np.empty((g, p, n, 4), np.uint8)
        nib[..., 0::2] = words & 0xF
        nib[..., 1::2] = words >> 4
        vals = E2M1[nib]
    vals = vals * np.repeat(np.exp2(scales.astype(np.float64) - 127.0), 8, axis=1)[..., None]
    return vals.transpose(0, 1, 3, 2).reshape(g * 512, n)

E4M3FN = np.array([(-1.0 if i & 128 else 1.0) * ((1.0 + (i & 7) / 8.0) * 2.0 ** (((i >> 3) & 15) - 7) if i & 120 else (i & 7) * 2.0 ** -9) for i in range(256)])


def e4m3fn_bytes(y):
    return np.clip(np.asarray(y, np.float64), -448.0, 448.0).astype(np.float32).astype(ml_dtypes.float8_e4m3fn).view(np.uint8)


def e4m3fn_values(b):
    return E4M3FN[b]


T, D, F, E, R = 1024, 1024, 1024, 128, 512


def softmax_last(l):
    m = np.max(l, axis=-1, keepdims=True)
    p = np.exp(l - m)
    return p / np.sum(p, axis=-1, keepdims=True)


def draw0():
    s, t = mx_kscale(D), mx_kscale(R)
    sd, sr = np.sqrt(D), np.sqrt(R)
    x = bf(np.random.standard_normal((T, D)) * s)
    w0_words, w0_scales = pack_weight(np.random.standard_normal((D, F)) / sd / s[:, None], "e4m3")
    wr_words, wr_scales = pack_weight(np.random.standard_normal((D, E)) / sd / s[:, None], "e4m3")
    br = bf(np.random.standard_normal(E) * 0.5)
    a_words, a_scales = pack_weight(np.random.standard_normal((D, R)) / sd / s[:, None] * t, "e4m3")
    b_words, b_scales = pack_weight(np.random.standard_normal((R, F)) * 0.6 / sr / t[:, None], "e4m3")
    return {
        "x": x,
        "w0_words": w0_words,
        "w0_scales": w0_scales,
        "wr_words": wr_words,
        "wr_scales": wr_scales,
        "br": br,
        "a_words": a_words,
        "a_scales": a_scales,
        "b_words": b_words,
        "b_scales": b_scales,
    }


def core(x, w0_words, w0_scales, wr_words, wr_scales, br, a_words, a_scales, b_words, b_scales):
    w0 = unpack_weight(w0_words, w0_scales, "e4m3")
    wr = unpack_weight(wr_words, wr_scales, "e4m3")
    a = unpack_weight(a_words, a_scales, "e4m3")
    b = unpack_weight(b_words, b_scales, "e4m3")
    n_tok = x.shape[0]
    n_exp = wr.shape[1]
    rank = a.shape[1]
    per_exp = rank // n_exp
    xq = mxq(f64(x), 1, "e4m3")
    l = (xq @ wr) + f64(br)
    g = float(n_exp) * softmax_last(l)
    u = xq @ a
    z = u.reshape(n_tok, n_exp, per_exp) * g[:, :, None]
    z = z.reshape(n_tok, rank)
    y = (xq @ w0) + (mxq(z, 1, "e4m3") @ b)
    return y


def setup_inputs():
    drawn = draw0()
    full = np.asarray(drawn['x']).astype(np.float64)
    scale = (np.abs(full).reshape(8, 128, 8, 128).max(axis=(1, 3)) / 448.0).astype(np.float32)
    given = {}
    for key, value in drawn.items():
        if key == 'x':
            given['x_bytes'] = e4m3fn_bytes(full / np.repeat(np.repeat(scale.astype(np.float64), 128, axis=0), 128, axis=1))
            given['x_scale'] = scale
        else:
            given[key] = value
    return given


def reference(x_bytes, x_scale, w0_words, w0_scales, wr_words, wr_scales, br, a_words, a_scales, b_words, b_scales):
    return core(e4m3fn_values(x_bytes) * np.repeat(np.repeat(x_scale.astype(np.float64), 128, axis=0), 128, axis=1), w0_words, w0_scales, wr_words, wr_scales, br, a_words, a_scales, b_words, b_scales)

@@ -1,0 +1,450 @@
+from contextlib import ExitStack
+
+import concourse.mybir as mybir
+from concourse.masks import make_identity
+
+T, D, F, E, R = 1024, 1024, 1024, 128, 512
+FLOPS = 2 * T * D * (F + E + R) + 2 * T * R * F
+
+F32 = mybir.dt.float32
+BF16 = mybir.dt.bfloat16
+I32 = mybir.dt.int32
+U32 = mybir.dt.uint32
+U8 = mybir.dt.uint8
+FP8 = mybir.dt.float8_e4m3fn
+FP8X4 = mybir.dt.float8_e4m3fn_x4
+MULT = mybir.AluOpType.mult
+ADD = mybir.AluOpType.add
+MAX = mybir.AluOpType.max
+AX = mybir.AxisListType.X
+ACT = mybir.ActivationFunctionType
+
+P = 128
+TILES = 8
+PAIRS = 4
+S_BLOCKS = ((3, 6, 7), (3, 6, 7), (1, 3, 5, 7), (1, 3, 5, 7), (3, 7), (3, 7), (3, 7), (3, 7))
+CONTIG = ()
+Y_V = ((2, 512), (4, 512), (6, 512), (7, 512))
+
+
+def tile_rankwisemoloradenserouter_d2p_kernel(
+    tc, x_bytes, x_scale, w0_words, w0_scales, wr_words, wr_scales, br, a_words, a_scales, b_words, b_scales, out
+):
+    nc = tc.nc
+    with ExitStack() as ctx:
+        keep = ctx.enter_context(tc.tile_pool(name="keep", bufs=1))
+        psum = ctx.enter_context(tc.psum_pool(name="psum", bufs=1))
+        ctx.enter_context(tc.manual_schedule())
+
+        a_sc_raw = keep.tile([P, 2 * R], U8, align_bytes=64, name="a_sc_raw")
+        wr_sc = keep.tile([P, 2, E], U8, align_bytes=64, name="wr_sc")
+        w0_sc = keep.tile([P, F], U8, align_bytes=64, name="w0_sc")
+        b_sc = keep.tile([P, F], U8, align_bytes=64, name="b_sc")
+        for sc in (a_sc_raw[:], wr_sc[:].rearrange("p g n -> p (g n)"), w0_sc[:], b_sc[:]):
+            nc.vector.memset(sc.bitcast(I32), 0)
+
+        zero_col = keep.tile([P, 1], F32, name="zero_col")
+        exp_col = keep.tile([P, 1], F32, name="exp_col")
+        nc.vector.memset(zero_col[:], 0.0)
+
+        x_view = x_bytes.rearrange("(p r) k -> p r k", r=TILES)
+        out_view = out.rearrange("(p r) f -> p r f", r=TILES)
+        w0_view = w0_words.rearrange("g p n t -> p g (n t)")
+
+        ident = keep.tile([P, P], F32, name="ident")
+        nc.vector.memset(ident[:], 0.0)
+        scale_cols = keep.tile([P, 8], F32, name="scale_cols")
+        xb0 = [keep.tile([P, D], U8, align_bytes=64, name=f"xb0_{r}") for r in range(2)]
+        xb = [keep.tile([P, 2, D], U8, align_bytes=64, name=f"xb{h}") for h in range(1, PAIRS)]
+
+        def x_rows(r):
+            return xb0[r][:] if r < 2 else xb[r // 2 - 1][:, r % 2, :]
+
+        def load_x_tile(r):
+            nc.sync.dma_start(out=xb0[r][:], in_=x_view[:, r, :])
+        wr_c = keep.tile([P, 2, E], I32, align_bytes=64, name="wr_c")
+        a_raw = keep.tile([P, 2, R], I32, align_bytes=64, name="a_raw")
+        b_c = keep.tile([P, F], I32, align_bytes=64, name="b_c")
+        br_bc = keep.tile([P, E], F32, name="br_bc")
+        ones = keep.tile([P, P], BF16, align_bytes=64, name="ones")
+        br_rows = keep.tile([P, E], BF16, align_bytes=64, name="br_rows")
+        nc.vector.memset(br_rows[:], 0.0)
+        nc.vector.memset(ones[:], 1.0)
+        w0_c = [keep.tile([P, 2, 512], I32, align_bytes=64, name=f"w0_c{f}") for f in range(2)]
+
+        def load_x(h):
+            nc.sync.dma_start(out=xb[h - 1][:], in_=x_view[:, 2 * h : 2 * h + 2, :])
+
+        def load_w0(f):
+            nc.sync.dma_start(out=w0_c[f][:], in_=w0_view[:, :, 2048 * f : 2048 * f + 2048].bitcast(I32))
+
+        def wr_scale(queue, q):
+            queue.dma_start(
+                out=wr_sc[32 * q : 32 * q + 4, :, :].bitcast(I32),
+                in_=wr_scales[:, 4 * q : 4 * q + 4, :].bitcast(I32).rearrange("g q n -> q g n"),
+            )
+
+        def a_scale(queue, q):
+            queue.dma_start(
+                out=a_sc_raw[32 * q : 32 * q + 4, :].bitcast(I32).rearrange("p (g n) -> p g n", g=2),
+                in_=a_scales[:, 4 * q : 4 * q + 4, :].bitcast(I32).rearrange("g q n -> q g n"),
+            )
+
+        def w0_scale(queue, q):
+            queue.dma_start(
+                out=w0_sc[32 * q : 32 * q + 8, :].bitcast(I32), in_=w0_scales[:, 4 * q : 4 * q + 4, :].bitcast(I32)
+            )
+
+        def b_scale(queue, q):
+            queue.dma_start(
+                out=b_sc[32 * q : 32 * q + 4, :].bitcast(I32), in_=b_scales[0, 4 * q : 4 * q + 4, :].bitcast(I32)
+            )
+
+        make_identity(nc, ident[:], nomemset=True)
+        nc.scalar.dma_start(out=scale_cols[:], in_=x_scale.unsqueeze(1).to_broadcast([8, 16, 8]))
+        nc.scalar.activation(out=exp_col[:], in_=zero_col[:], func=ACT.Exp)
+        load_x_tile(0)
+        load_x_tile(1)
+        wr_scale(nc.sync, 0)
+        wr_scale(nc.sync, 1)
+        a_scale(nc.sync, 0)
+        nc.sync.dma_start(out=wr_c[:], in_=wr_words.rearrange("g p n t -> p g (n t)").bitcast(I32))
+        nc.sync.dma_start(out=a_raw[:], in_=a_words.rearrange("g p n t -> p g (n t)").bitcast(I32))
+        wr_scale(nc.sync, 2)
+        wr_scale(nc.sync, 3)
+        nc.sync.dma_start(out=br_rows[0:1, :], in_=br.unsqueeze(0))
+        a_scale(nc.sync, 1)
+        a_scale(nc.sync, 2)
+        a_scale(nc.sync, 3)
+        load_x(1)
+        load_x(2)
+        load_w0(0)
+        w0_scale(nc.sync, 0)
+        w0_scale(nc.sync, 1)
+        w0_scale(nc.sync, 2)
+        w0_scale(nc.sync, 3)
+        load_w0(1)
+        nc.sync.dma_start(out=b_c[:], in_=b_words[0].rearrange("p n t -> p (n t)").bitcast(I32))
+        b_scale(nc.sync, 0)
+        b_scale(nc.sync, 1)
+        b_scale(nc.sync, 2)
+        b_scale(nc.sync, 3)
+        load_x(3)
+
+        xw = [keep.tile([P, D], BF16, align_bytes=64, name=f"xw{r}") for r in range(TILES)]
+        xg = [keep.tile([P, 2 * P * 4], BF16, align_bytes=64, name=f"xg{r}") for r in range(TILES)]
+        xq = [keep.tile([P, 2 * P], U32, align_bytes=64, name=f"xq{r}") for r in range(TILES)]
+        xs = [keep.tile([P, 2 * P], U8, align_bytes=64, name=f"xs{r}") for r in range(TILES)]
+        zb = [keep.tile([P, P, 4], BF16, align_bytes=64, name=f"zb{r}") for r in range(TILES)]
+        zq = [keep.tile([P, P], U32, align_bytes=64, name=f"zq{r}") for r in range(TILES)]
+        zs = [keep.tile([P, P], U8, align_bytes=64, name=f"zs{r}") for r in range(TILES)]
+        yo = [keep.tile([P, F], F32, align_bytes=64, name=f"yo{r}") for r in range(TILES)]
+        lb = [keep.tile([P, 2, E], F32, name=f"lb{h}") for h in range(PAIRS)]
+        ex = [keep.tile([P, 2, E], F32, name=f"ex{h}") for h in range(PAIRS)]
+        gt = [keep.tile([P, 2, E], F32, name=f"gt{h}") for h in range(PAIRS)]
+        gs = [keep.tile([P, 2, P], F32, name=f"gs{h}") for h in range(PAIRS)]
+        nm = [keep.tile([P, 2], F32, name=f"nm{h}") for h in range(PAIRS)]
+        sm = [keep.tile([P, 2], F32, name=f"sm{h}") for h in range(PAIRS)]
+        rs = [keep.tile([P, 2], F32, name=f"rs{h}") for h in range(PAIRS)]
+        a_c = keep.tile([P, 2, 4, P], I32, align_bytes=64, name="a_c")
+        a_sc = keep.tile([P, 2, 4, P], U8, align_bytes=64, name="a_sc")
+        u_ps = {}
+        y_ps = {}
+        l_ps = {}
+        g_ps = {}
+        t_ps = {}
+
+        def widen_vector(r, g):
+            for j in range(4 * g, 4 * g + 4):
+                cols = slice(P * j, P * j + P)
+                if r in CONTIG:
+                    dest = xw[r][:].rearrange("p (g u q e) -> p g q u e", g=2, u=2, e=2)[
+                        :, j // 4, 32 * (j % 4) : 32 * (j % 4) + 32
+                    ]
+                    source = x_rows(r)[:, cols].bitcast(FP8).rearrange("p (q u e) -> p q u e", u=2, e=2)
+                elif j not in S_BLOCKS[r]:
+                    dest = xw[r][:, cols]
+                    source = x_rows(r)[:, cols].bitcast(FP8)
+                else:
+                    continue
+                nc.vector.tensor_scalar(
+                    out=dest, in0=source, scalar1=scale_cols[:, j : j + 1], scalar2=None, op0=MULT
+                )
+
+        def widen_scalar(r):
+            for j in range(8):
+                if r not in CONTIG and j in S_BLOCKS[r]:
+                    cols = slice(P * j, P * j + P)
+                    nc.scalar.activation(
+                        out=xw[r][:, cols],
+                        in_=x_rows(r)[:, cols].bitcast(FP8),
+                        func=ACT.Copy,
+                        scale=scale_cols[:, j : j + 1],
+                    )
+
+        def turn(r):
+            t_ps[r] = psum.tile([P, 4, P], F32, tag="tr", bufs=2, name=f"t_ps{r}")
+            words = xw[r][:].bitcast(F32)
+            for g in range(2):
+                for u in range(2):
+                    if r in CONTIG:
+                        part = words[:, 256 * g + P * u : 256 * g + P * u + P]
+                    else:
+                        part = words[:, 256 * g + u : 256 * (g + 1) : 2]
+                    nc.tensor.transpose(t_ps[r][:, 2 * g + u, :], part, ident[:])
+
+        def interleave(r, g):
+            nc.scalar.copy(
+                out=xg[r][:, 512 * g : 512 * g + 512].bitcast(F32).rearrange("p (n u) -> p n u", u=2),
+                in_=t_ps[r][:, 2 * g : 2 * g + 2, :].rearrange("p u n -> p n u"),
+            )
+
+        def interleave_tile(r):
+            nc.scalar.copy(
+                out=xg[r][:].bitcast(F32).rearrange("p (g n u) -> p g n u", g=2, u=2),
+                in_=t_ps[r][:].rearrange("p (g u) n -> p g n u", g=2),
+            )
+
+        def spread_bias():
+            b_ps = l_ps["bias"] = psum.tile([P, E], F32, tag="y", bufs=3, name="b_ps")
+            nc.tensor.matmul(b_ps[:], lhsT=ones[:], rhs=br_rows[:], start=True, stop=True)
+
+        def copy_bias():
+            nc.scalar.copy(out=br_bc[:], in_=l_ps["bias"][:])
+
+        def quantize_x(r):
+            nc.vector.quantize_mx(out=xq[r][:].bitcast(FP8X4), scales=xs[r][:], in_=xg[r][:])
+
+        def xq_of(r, g):
+            return xq[r][:, P * g : P * g + P].bitcast(FP8X4), xs[r][:, P * g : P * g + P]
+
+        def logits(r):
+            h, i = r // 2, r % 2
+            if i == 0:
+                l_ps[h] = psum.tile([P, 2, E], F32, tag="lg", bufs=1, name=f"l_ps{h}")
+            for g in range(2):
+                codes, scales = xq_of(r, g)
+                nc.tensor.matmul_mx(
+                    out=l_ps[h][:, i, :],
+                    lhsT=codes,
+                    lhsT_scale=scales,
+                    rhs=wr_c[:, g, :].bitcast(FP8X4),
+                    rhs_scale=wr_sc[:, g, :],
+                    start=(g == 0),
+                    stop=(g == 1),
+                )
+
+        def down(r):
+            u_ps[r] = psum.tile([P, 4, P], F32, tag="u", bufs=2, name=f"u_ps{r}")
+            for t in range(4):
+                for g in range(2):
+                    codes, scales = xq_of(r, g)
+                    nc.tensor.matmul_mx(
+                        out=u_ps[r][:, t, :],
+                        lhsT=a_c[:, g, t, :].bitcast(FP8X4),
+                        lhsT_scale=a_sc[:, g, t, :],
+                        rhs=codes,
+                        rhs_scale=scales,
+                        start=(g == 0),
+                        stop=(g == 1),
+                    )
+
+        def soft_add(h):
+            nc.vector.tensor_tensor(
+                out=lb[h][:], in0=l_ps[h][:], in1=br_bc[:].unsqueeze(1).to_broadcast([P, 2, E]), op=ADD
+            )
+
+        def soft_peak(h):
+            nc.vector.tensor_reduce(out=nm[h][:], in_=lb[h][:], axis=AX, op=MAX, negate=True)
+
+        def soft_exp(h):
+            for i in range(2):
+                nc.scalar.activation(
+                    out=ex[h][:, i, :],
+                    in_=lb[h][:, i, :],
+                    func=ACT.Exp,
+                    bias=nm[h][:, i : i + 1],
+                    accum_out=sm[h][:, i : i + 1],
+                )
+
+        def soft_recip(h):
+            nc.vector.reciprocal(out=rs[h][:], in_=sm[h][:])
+
+        def soft_scale(h):
+            for i in range(2):
+                nc.vector.tensor_scalar(
+                    out=gt[h][:, i, :],
+                    in0=ex[h][:, i, :],
+                    scalar1=rs[h][:, i : i + 1],
+                    scalar2=float(E),
+                    op0=MULT,
+                    op1=MULT,
+                )
+
+        def turn_gates(h):
+            g_ps[h] = psum.tile([P, 2, P], F32, tag="lg", bufs=1, name=f"g_ps{h}")
+            for i in range(2):
+                nc.tensor.transpose(g_ps[h][:, i, :], gt[h][:, i, :], ident[:])
+
+        def copy_gates(h):
+            nc.scalar.copy(out=gs[h][:], in_=g_ps[h][:])
+
+        def gate(r):
+            nc.vector.tensor_tensor(
+                out=zb[r][:].rearrange("p (c i) t -> p c t i", i=4),
+                in0=u_ps[r][:].rearrange("p t (c i) -> p c t i", i=4),
+                in1=gs[r // 2][:, r % 2, :].rearrange("p (c i) -> p c i", i=4).unsqueeze(2).to_broadcast([P, 32, 4, 4]),
+                op=MULT,
+            )
+
+        def quantize_z(r):
+            nc.vector.quantize_mx(
+                out=zq[r][:].bitcast(FP8X4), scales=zs[r][:], in_=zb[r][:].rearrange("p n t -> p (n t)")
+            )
+
+        def base(r, c0, width, tag, bufs):
+            y_ps[r, c0] = psum.tile([P, width], F32, tag=tag, bufs=bufs, name=f"y_ps{r}_{c0}")
+            f, c = c0 // 512, c0 % 512
+            for g in range(2):
+                codes, scales = xq_of(r, g)
+                nc.tensor.matmul_mx(
+                    out=y_ps[r, c0][:],
+                    lhsT=codes,
+                    lhsT_scale=scales,
+                    rhs=w0_c[f][:, g, c : c + width].bitcast(FP8X4),
+                    rhs_scale=w0_sc[4 * g :, c0 : c0 + width],
+                    start=(g == 0),
+                    stop=False,
+                )
+
+        def lora(r, c0, width):
+            nc.tensor.matmul_mx(
+                out=y_ps[r, c0][:],
+                lhsT=zq[r][:].bitcast(FP8X4),
+                lhsT_scale=zs[r][:],
+                rhs=b_c[:, c0 : c0 + width].bitcast(FP8X4),
+                rhs_scale=b_sc[:, c0 : c0 + width],
+                start=False,
+                stop=True,
+            )
+
+        def empty(r, c0, width):
+            engine_copy = nc.vector.tensor_copy if (r, c0) in Y_V else nc.scalar.copy
+            engine_copy(out=yo[r][:, c0 : c0 + width], in_=y_ps[r, c0][:])
+
+        def store(r, c0, width):
+            nc.sync.dma_start(out=out_view[:, r, c0 : c0 + width], in_=yo[r][:, c0 : c0 + width])
+
+        def perm_words():
+            nc.vector.tensor_copy(out=a_c[:], in_=a_raw[:].rearrange("p g (m t) -> p g t m", t=4))
+
+        def perm_scales():
+            nc.vector.tensor_copy(out=a_sc[:], in_=a_sc_raw[:].rearrange("p (g m t) -> p g t m", g=2, t=4))
+
+        def bases(r, tag, bufs):
+            base(r, 0, 512, tag, bufs)
+            base(r, 512, 512, tag, bufs)
+
+        def widen(r):
+            widen_vector(r, 0)
+            widen_vector(r, 1)
+
+        def bases(r, tag, bufs):
+            base(r, 0, 512, tag, bufs)
+            base(r, 512, 512, tag, bufs)
+
+        def out_half(r, c0):
+            empty(r, c0, 512)
+
+        for r in (0, 1):
+            widen(r)
+            widen_scalar(r)
+            turn(r)
+        for r in (0, 1):
+            interleave(r, 0)
+            interleave(r, 1)
+        spread_bias()
+        perm_words()
+        quantize_x(0)
+        quantize_x(1)
+        perm_scales()
+        copy_bias()
+        logits(0)
+        logits(1)
+        soft_add(0)
+        widen_vector(2, 0)
+        soft_peak(0)
+        widen_scalar(2)
+        widen_scalar(3)
+        soft_exp(0)
+        widen_vector(2, 1)
+        widen(3)
+        soft_recip(0)
+        soft_scale(0)
+        down(0)
+        turn(2)
+        turn(3)
+        turn_gates(0)
+        interleave_tile(2)
+        interleave_tile(3)
+        copy_gates(0)
+        down(1)
+        quantize_x(2)
+        quantize_x(3)
+        gate(0)
+        gate(1)
+        for h in range(PAIRS - 1):
+            r0, r1 = 2 * h, 2 * h + 1
+            ahead = range(2 * h + 4, 2 * h + 6) if h + 2 < PAIRS else ()
+            base(r0, 0, 512, "y", 3)
+            logits(r0 + 2)
+            logits(r1 + 2)
+            soft_add(h + 1)
+            quantize_z(r0)
+            soft_peak(h + 1)
+            quantize_z(r1)
+            for r in ahead:
+                widen_scalar(r)
+            for r in ahead[:1]:
+                widen(r)
+            soft_exp(h + 1)
+            soft_recip(h + 1)
+            soft_scale(h + 1)
+            for r in ahead[1:]:
+                widen(r)
+            base(r0, 512, 512, "y", 3)
+            down(r0 + 2)
+            down(r1 + 2)
+            lora(r0, 0, 512)
+            lora(r0, 512, 512)
+            empty(r0, 0, 512)
+            base(r1, 0, 512, "y", 3)
+            turn_gates(h + 1)
+            copy_gates(h + 1)
+            empty(r0, 512, 512)
+            store(r0, 0, F)
+            for r in ahead:
+                turn(r)
+                interleave_tile(r)
+            gate(r0 + 2)
+            for r in ahead:
+                quantize_x(r)
+            gate(r1 + 2)
+            base(r1, 512, 512, "y", 3)
+            lora(r1, 0, 512)
+            lora(r1, 512, 512)
+            empty(r1, 0, 512)
+            empty(r1, 512, 512)
+            store(r1, 0, F)
+        quantize_z(6)
+        quantize_z(7)
+        bases(6, "tr", 2)
+        for c0 in (0, 512):
+            lora(6, c0, 512)
+            empty(6, c0, 512)
+            store(6, c0, 512)
+        for c0, width in ((0, 512), (512, 256), (768, 256)):
+            base(7, c0, width, "y", 3)
+            lora(7, c0, width)
+            empty(7, c0, width)
+            store(7, c0, width)

@@ -21,10 +21,10 @@ ACT = mybir.ActivationFunctionType
 
 P = 128
 TILES = 8
-PAIRS = 4
-S_BLOCKS = ((3, 6, 7), (3, 6, 7), (1, 3, 5, 7), (1, 3, 5, 7), (3, 7), (3, 7), (3, 7), (3, 7))
-CONTIG = ()
-Y_V = ((2, 512), (4, 512), (6, 512), (7, 512))
+HALF = 512
+HEAD_TILES = 2
+SCALAR_TILES = 6
+PAIRS = TILES // 2
 
 
 def tile_rankwisemoloradenserouter_d2p_kernel(
@@ -36,218 +36,177 @@ def tile_rankwisemoloradenserouter_d2p_kernel(
         psum = ctx.enter_context(tc.psum_pool(name="psum", bufs=1))
         ctx.enter_context(tc.manual_schedule())
 
-        a_sc_raw = keep.tile([P, 2 * R], U8, align_bytes=64, name="a_sc_raw")
-        wr_sc = keep.tile([P, 2, E], U8, align_bytes=64, name="wr_sc")
+        wr_sc = keep.tile([P, E], U8, align_bytes=64, name="wr_sc")
         w0_sc = keep.tile([P, F], U8, align_bytes=64, name="w0_sc")
+        a_sc = keep.tile([P, R], U8, align_bytes=64, name="a_sc")
         b_sc = keep.tile([P, F], U8, align_bytes=64, name="b_sc")
-        for sc in (a_sc_raw[:], wr_sc[:].rearrange("p g n -> p (g n)"), w0_sc[:], b_sc[:]):
-            nc.vector.memset(sc.bitcast(I32), 0)
-
-        zero_col = keep.tile([P, 1], F32, name="zero_col")
-        exp_col = keep.tile([P, 1], F32, name="exp_col")
-        nc.vector.memset(zero_col[:], 0.0)
+        zeros = keep.tile([P, P], BF16, align_bytes=64, name="zeros")
+        ident = keep.tile([P, P], F32, name="ident")
+        ones = keep.tile([P, P], BF16, align_bytes=64, name="ones")
+        br_rows = keep.tile([P, E], BF16, align_bytes=64, name="br_rows")
+        br_bc = keep.tile([P, E], F32, name="br_bc")
+        scale_cols = keep.tile([P, 8], F32, name="scale_cols")
+        nc.vector.memset(zeros[:], 0.0)
+        nc.vector.memset(wr_sc[:].bitcast(I32), 0)
+        nc.vector.memset(ident[:], 0.0)
+        nc.vector.memset(br_rows[:], 0.0)
+        for sc in (w0_sc, a_sc, b_sc):
+            nc.vector.memset(sc[:].bitcast(I32), 0)
 
         x_view = x_bytes.rearrange("(p r) k -> p r k", r=TILES)
         out_view = out.rearrange("(p r) f -> p r f", r=TILES)
         w0_view = w0_words.rearrange("g p n t -> p g (n t)")
 
-        ident = keep.tile([P, P], F32, name="ident")
-        nc.vector.memset(ident[:], 0.0)
-        scale_cols = keep.tile([P, 8], F32, name="scale_cols")
-        xb0 = [keep.tile([P, D], U8, align_bytes=64, name=f"xb0_{r}") for r in range(2)]
-        xb = [keep.tile([P, 2, D], U8, align_bytes=64, name=f"xb{h}") for h in range(1, PAIRS)]
+        b_view = b_words[0].rearrange("p n t -> p (n t)")
+        xb_head = [keep.tile([P, D], U8, align_bytes=64, name=f"xb_head{r}") for r in range(HEAD_TILES)]
+        xb = [keep.tile([P, 2, D], U8, align_bytes=64, name=f"xb{h}") for h in range(1, TILES // 2)]
+        wr_c = keep.tile([P, 2, E], I32, align_bytes=64, name="wr_c")
+        a_c = keep.tile([P, 2, R], I32, align_bytes=64, name="a_c")
+        b_c = [keep.tile([P, HALF], I32, align_bytes=64, name=f"b_c{f}") for f in range(2)]
+        w0_c = [keep.tile([P, 2, HALF], I32, align_bytes=64, name=f"w0_c{f}") for f in range(2)]
 
         def x_rows(r):
-            return xb0[r][:] if r < 2 else xb[r // 2 - 1][:, r % 2, :]
+            return xb_head[r][:] if r < HEAD_TILES else xb[r // 2 - 1][:, r % 2, :]
 
         def load_x_tile(r):
-            nc.sync.dma_start(out=xb0[r][:], in_=x_view[:, r, :])
-        wr_c = keep.tile([P, 2, E], I32, align_bytes=64, name="wr_c")
-        a_raw = keep.tile([P, 2, R], I32, align_bytes=64, name="a_raw")
-        b_c = keep.tile([P, F], I32, align_bytes=64, name="b_c")
-        br_bc = keep.tile([P, E], F32, name="br_bc")
-        ones = keep.tile([P, P], BF16, align_bytes=64, name="ones")
-        br_rows = keep.tile([P, E], BF16, align_bytes=64, name="br_rows")
-        nc.vector.memset(br_rows[:], 0.0)
-        nc.vector.memset(ones[:], 1.0)
-        w0_c = [keep.tile([P, 2, 512], I32, align_bytes=64, name=f"w0_c{f}") for f in range(2)]
+            nc.sync.dma_start(out=xb_head[r][:], in_=x_view[:, r, :])
 
-        def load_x(h):
+        def load_x_pair(h):
             nc.sync.dma_start(out=xb[h - 1][:], in_=x_view[:, 2 * h : 2 * h + 2, :])
 
         def load_w0(f):
             nc.sync.dma_start(out=w0_c[f][:], in_=w0_view[:, :, 2048 * f : 2048 * f + 2048].bitcast(I32))
 
-        def wr_scale(queue, q):
-            queue.dma_start(
-                out=wr_sc[32 * q : 32 * q + 4, :, :].bitcast(I32),
-                in_=wr_scales[:, 4 * q : 4 * q + 4, :].bitcast(I32).rearrange("g q n -> q g n"),
-            )
+        def load_words(tile, words):
+            nc.sync.dma_start(out=tile[:], in_=words.rearrange("g p n t -> p g (n t)").bitcast(I32))
 
-        def a_scale(queue, q):
-            queue.dma_start(
-                out=a_sc_raw[32 * q : 32 * q + 4, :].bitcast(I32).rearrange("p (g n) -> p g n", g=2),
-                in_=a_scales[:, 4 * q : 4 * q + 4, :].bitcast(I32).rearrange("g q n -> q g n"),
-            )
+        def load_b(f):
+            nc.sync.dma_start(out=b_c[f][:], in_=b_view[:, 2048 * f : 2048 * f + 2048].bitcast(I32))
 
-        def w0_scale(queue, q):
-            queue.dma_start(
-                out=w0_sc[32 * q : 32 * q + 8, :].bitcast(I32), in_=w0_scales[:, 4 * q : 4 * q + 4, :].bitcast(I32)
-            )
-
-        def b_scale(queue, q):
-            queue.dma_start(
-                out=b_sc[32 * q : 32 * q + 4, :].bitcast(I32), in_=b_scales[0, 4 * q : 4 * q + 4, :].bitcast(I32)
-            )
+        def load_scales(plane, scales, groups, quadrants):
+            for q in quadrants:
+                nc.sync.dma_start(
+                    out=plane[32 * q : 32 * q + 4 * groups, :].bitcast(I32),
+                    in_=scales[:, 4 * q : 4 * q + 4, :].bitcast(I32),
+                )
 
         make_identity(nc, ident[:], nomemset=True)
         nc.scalar.dma_start(out=scale_cols[:], in_=x_scale.unsqueeze(1).to_broadcast([8, 16, 8]))
-        nc.scalar.activation(out=exp_col[:], in_=zero_col[:], func=ACT.Exp)
+        nc.scalar.activation(out=ones[:], in_=zeros[:], func=ACT.Exp)
+        nc.gpsimd.dma_start(out=br_rows[0:1, :], in_=br.unsqueeze(0))
         load_x_tile(0)
         load_x_tile(1)
-        wr_scale(nc.sync, 0)
-        wr_scale(nc.sync, 1)
-        a_scale(nc.sync, 0)
-        nc.sync.dma_start(out=wr_c[:], in_=wr_words.rearrange("g p n t -> p g (n t)").bitcast(I32))
-        nc.sync.dma_start(out=a_raw[:], in_=a_words.rearrange("g p n t -> p g (n t)").bitcast(I32))
-        wr_scale(nc.sync, 2)
-        wr_scale(nc.sync, 3)
-        nc.sync.dma_start(out=br_rows[0:1, :], in_=br.unsqueeze(0))
-        a_scale(nc.sync, 1)
-        a_scale(nc.sync, 2)
-        a_scale(nc.sync, 3)
-        load_x(1)
-        load_x(2)
+        load_words(wr_c, wr_words)
+        load_scales(wr_sc, wr_scales, 2, range(3))
         load_w0(0)
-        w0_scale(nc.sync, 0)
-        w0_scale(nc.sync, 1)
-        w0_scale(nc.sync, 2)
-        w0_scale(nc.sync, 3)
+        load_scales(wr_sc, wr_scales, 2, range(3, 4))
+        load_x_pair(1)
+        load_scales(w0_sc, w0_scales, 2, range(4))
+        load_words(a_c, a_words)
+        load_scales(a_sc, a_scales, 2, range(4))
+        load_x_pair(2)
+        load_b(0)
+        load_scales(b_sc, b_scales, 1, range(4))
         load_w0(1)
-        nc.sync.dma_start(out=b_c[:], in_=b_words[0].rearrange("p n t -> p (n t)").bitcast(I32))
-        b_scale(nc.sync, 0)
-        b_scale(nc.sync, 1)
-        b_scale(nc.sync, 2)
-        b_scale(nc.sync, 3)
-        load_x(3)
+        load_b(1)
+        load_x_pair(3)
 
-        xw = [keep.tile([P, D], BF16, align_bytes=64, name=f"xw{r}") for r in range(TILES)]
-        xg = [keep.tile([P, 2 * P * 4], BF16, align_bytes=64, name=f"xg{r}") for r in range(TILES)]
-        xq = [keep.tile([P, 2 * P], U32, align_bytes=64, name=f"xq{r}") for r in range(TILES)]
-        xs = [keep.tile([P, 2 * P], U8, align_bytes=64, name=f"xs{r}") for r in range(TILES)]
-        zb = [keep.tile([P, P, 4], BF16, align_bytes=64, name=f"zb{r}") for r in range(TILES)]
-        zq = [keep.tile([P, P], U32, align_bytes=64, name=f"zq{r}") for r in range(TILES)]
-        zs = [keep.tile([P, P], U8, align_bytes=64, name=f"zs{r}") for r in range(TILES)]
-        yo = [keep.tile([P, F], F32, align_bytes=64, name=f"yo{r}") for r in range(TILES)]
-        lb = [keep.tile([P, 2, E], F32, name=f"lb{h}") for h in range(PAIRS)]
-        ex = [keep.tile([P, 2, E], F32, name=f"ex{h}") for h in range(PAIRS)]
-        gt = [keep.tile([P, 2, E], F32, name=f"gt{h}") for h in range(PAIRS)]
-        gs = [keep.tile([P, 2, P], F32, name=f"gs{h}") for h in range(PAIRS)]
-        nm = [keep.tile([P, 2], F32, name=f"nm{h}") for h in range(PAIRS)]
-        sm = [keep.tile([P, 2], F32, name=f"sm{h}") for h in range(PAIRS)]
-        rs = [keep.tile([P, 2], F32, name=f"rs{h}") for h in range(PAIRS)]
-        a_c = keep.tile([P, 2, 4, P], I32, align_bytes=64, name="a_c")
-        a_sc = keep.tile([P, 2, 4, P], U8, align_bytes=64, name="a_sc")
-        u_ps = {}
-        y_ps = {}
-        l_ps = {}
-        g_ps = {}
-        t_ps = {}
+        def tiles(shape, dtype, name, count=TILES):
+            return [keep.tile(shape, dtype, align_bytes=64, name=f"{name}{r}") for r in range(count)]
 
-        def widen_vector(r, g):
+        xw = tiles([P, D], BF16, "xw")
+        xg = tiles([P, D], BF16, "xg")
+        xq = tiles([P, 2 * P], U32, "xq")
+        xs = tiles([P, 2 * P], U8, "xs")
+        lb = tiles([P, 2, E], F32, "lb", PAIRS)
+        ex = tiles([P, 2, E], F32, "ex", PAIRS)
+        gt = tiles([P, 2, E], F32, "gt", PAIRS)
+        nm = tiles([P, 2], F32, "nm", PAIRS)
+        sm = tiles([P, 2], F32, "sm", PAIRS)
+        rs = tiles([P, 2], F32, "rs", PAIRS)
+        zw = tiles([P, R], BF16, "zw")
+        zg = tiles([P, R], BF16, "zg")
+        zq = tiles([P, P], U32, "zq")
+        zs = tiles([P, P], U8, "zs")
+        yo = tiles([P, F], F32, "yo")
+        xt_ps, zt_ps, l_ps, u_ps, y_ps = {}, {}, {}, {}, {}
+
+        def bank(index, shape, name):
+            return psum.tile(shape, F32, tag=f"bank{index}", bufs=1, name=name)
+
+        def on_scalar(r, g):
+            return r < SCALAR_TILES and g == 1
+
+        def widen(r, g):
             for j in range(4 * g, 4 * g + 4):
                 cols = slice(P * j, P * j + P)
-                if r in CONTIG:
-                    dest = xw[r][:].rearrange("p (g u q e) -> p g q u e", g=2, u=2, e=2)[
-                        :, j // 4, 32 * (j % 4) : 32 * (j % 4) + 32
-                    ]
-                    source = x_rows(r)[:, cols].bitcast(FP8).rearrange("p (q u e) -> p q u e", u=2, e=2)
-                elif j not in S_BLOCKS[r]:
-                    dest = xw[r][:, cols]
-                    source = x_rows(r)[:, cols].bitcast(FP8)
-                else:
-                    continue
-                nc.vector.tensor_scalar(
-                    out=dest, in0=source, scalar1=scale_cols[:, j : j + 1], scalar2=None, op0=MULT
-                )
-
-        def widen_scalar(r):
-            for j in range(8):
-                if r not in CONTIG and j in S_BLOCKS[r]:
-                    cols = slice(P * j, P * j + P)
+                source = x_rows(r)[:, cols].bitcast(FP8)
+                if on_scalar(r, g):
                     nc.scalar.activation(
-                        out=xw[r][:, cols],
-                        in_=x_rows(r)[:, cols].bitcast(FP8),
-                        func=ACT.Copy,
-                        scale=scale_cols[:, j : j + 1],
+                        out=xw[r][:, cols], in_=source, func=ACT.Copy, scale=scale_cols[:, j : j + 1]
+                    )
+                else:
+                    planes = xw[r][:].rearrange("p (g u q e) -> p g q u e", g=2, u=2, e=2)
+                    nc.vector.tensor_scalar(
+                        out=planes[:, g, 32 * (j % 4) : 32 * (j % 4) + 32],
+                        in0=source.rearrange("p (q u e) -> p q u e", u=2, e=2),
+                        scalar1=scale_cols[:, j : j + 1],
+                        scalar2=None,
+                        op0=MULT,
                     )
 
-        def turn(r):
-            t_ps[r] = psum.tile([P, 4, P], F32, tag="tr", bufs=2, name=f"t_ps{r}")
+        def turn_x(r, b):
+            xt_ps[r] = bank(b, [P, 4, P], f"xt_ps{r}")
             words = xw[r][:].bitcast(F32)
             for g in range(2):
                 for u in range(2):
-                    if r in CONTIG:
-                        part = words[:, 256 * g + P * u : 256 * g + P * u + P]
-                    else:
+                    if on_scalar(r, g):
                         part = words[:, 256 * g + u : 256 * (g + 1) : 2]
-                    nc.tensor.transpose(t_ps[r][:, 2 * g + u, :], part, ident[:])
+                    else:
+                        part = words[:, 256 * g + P * u : 256 * g + P * u + P]
+                    nc.tensor.transpose(xt_ps[r][:, 2 * g + u, :], part, ident[:])
 
-        def interleave(r, g):
-            nc.scalar.copy(
-                out=xg[r][:, 512 * g : 512 * g + 512].bitcast(F32).rearrange("p (n u) -> p n u", u=2),
-                in_=t_ps[r][:, 2 * g : 2 * g + 2, :].rearrange("p u n -> p n u"),
-            )
-
-        def interleave_tile(r):
+        def copy_x(r):
             nc.scalar.copy(
                 out=xg[r][:].bitcast(F32).rearrange("p (g n u) -> p g n u", g=2, u=2),
-                in_=t_ps[r][:].rearrange("p (g u) n -> p g n u", g=2),
+                in_=xt_ps[r][:].rearrange("p (g u) n -> p g n u", g=2),
             )
-
-        def spread_bias():
-            b_ps = l_ps["bias"] = psum.tile([P, E], F32, tag="y", bufs=3, name="b_ps")
-            nc.tensor.matmul(b_ps[:], lhsT=ones[:], rhs=br_rows[:], start=True, stop=True)
-
-        def copy_bias():
-            nc.scalar.copy(out=br_bc[:], in_=l_ps["bias"][:])
 
         def quantize_x(r):
             nc.vector.quantize_mx(out=xq[r][:].bitcast(FP8X4), scales=xs[r][:], in_=xg[r][:])
 
-        def xq_of(r, g):
-            return xq[r][:, P * g : P * g + P].bitcast(FP8X4), xs[r][:, P * g : P * g + P]
+        def spread_bias(b):
+            l_ps["bias"] = bank(b, [P, E], "b_ps")
+            nc.tensor.matmul(l_ps["bias"][:], lhsT=ones[:], rhs=br_rows[:], start=True, stop=True)
 
-        def logits(r):
-            h, i = r // 2, r % 2
-            if i == 0:
-                l_ps[h] = psum.tile([P, 2, E], F32, tag="lg", bufs=1, name=f"l_ps{h}")
+        def copy_bias():
+            nc.scalar.copy(out=br_bc[:], in_=l_ps["bias"][:])
+
+        def x_product(dest, r, codes_of, plane, cols, close):
             for g in range(2):
-                codes, scales = xq_of(r, g)
                 nc.tensor.matmul_mx(
-                    out=l_ps[h][:, i, :],
-                    lhsT=codes,
-                    lhsT_scale=scales,
-                    rhs=wr_c[:, g, :].bitcast(FP8X4),
-                    rhs_scale=wr_sc[:, g, :],
+                    out=dest,
+                    lhsT=xq[r][:, P * g : P * g + P].bitcast(FP8X4),
+                    lhsT_scale=xs[r][:, P * g : P * g + P],
+                    rhs=codes_of(g).bitcast(FP8X4),
+                    rhs_scale=plane[4 * g :, cols],
                     start=(g == 0),
-                    stop=(g == 1),
+                    stop=(close and g == 1),
                 )
 
-        def down(r):
-            u_ps[r] = psum.tile([P, 4, P], F32, tag="u", bufs=2, name=f"u_ps{r}")
-            for t in range(4):
-                for g in range(2):
-                    codes, scales = xq_of(r, g)
-                    nc.tensor.matmul_mx(
-                        out=u_ps[r][:, t, :],
-                        lhsT=a_c[:, g, t, :].bitcast(FP8X4),
-                        lhsT_scale=a_sc[:, g, t, :],
-                        rhs=codes,
-                        rhs_scale=scales,
-                        start=(g == 0),
-                        stop=(g == 1),
-                    )
+        def logits(r, b):
+            if r % 2 == 0:
+                l_ps[r // 2] = bank(b, [P, 2, E], f"l_ps{r // 2}")
+            x_product(l_ps[r // 2][:, r % 2, :], r, lambda g: wr_c[:, g, :], wr_sc, slice(0, E), True)
+
+        def down(r, b):
+            u_ps[r] = bank(b, [P, R], f"u_ps{r}")
+            x_product(u_ps[r][:], r, lambda g: a_c[:, g, :], a_sc, slice(0, R), True)
+
+        def base(r, c0, width, b):
+            y_ps[r, c0] = bank(b, [P, width], f"y_ps{r}_{c0}")
+            f, c = divmod(c0, HALF)
+            x_product(y_ps[r, c0][:], r, lambda g: w0_c[f][:, g, c : c + width], w0_sc, slice(c0, c0 + width), False)
 
         def soft_add(h):
             nc.vector.tensor_tensor(
@@ -281,170 +240,203 @@ def tile_rankwisemoloradenserouter_d2p_kernel(
                     op1=MULT,
                 )
 
-        def turn_gates(h):
-            g_ps[h] = psum.tile([P, 2, P], F32, tag="lg", bufs=1, name=f"g_ps{h}")
-            for i in range(2):
-                nc.tensor.transpose(g_ps[h][:, i, :], gt[h][:, i, :], ident[:])
-
-        def copy_gates(h):
-            nc.scalar.copy(out=gs[h][:], in_=g_ps[h][:])
-
         def gate(r):
             nc.vector.tensor_tensor(
-                out=zb[r][:].rearrange("p (c i) t -> p c t i", i=4),
-                in0=u_ps[r][:].rearrange("p t (c i) -> p c t i", i=4),
-                in1=gs[r // 2][:, r % 2, :].rearrange("p (c i) -> p c i", i=4).unsqueeze(2).to_broadcast([P, 32, 4, 4]),
+                out=zw[r][:].rearrange("p (u e i) -> p u e i", u=2, i=2),
+                in0=u_ps[r][:].rearrange("p (e u i) -> p u e i", u=2, i=2),
+                in1=gt[r // 2][:, r % 2, :].unsqueeze(1).unsqueeze(3).to_broadcast([P, 2, E, 2]),
                 op=MULT,
             )
 
-        def quantize_z(r):
-            nc.vector.quantize_mx(
-                out=zq[r][:].bitcast(FP8X4), scales=zs[r][:], in_=zb[r][:].rearrange("p n t -> p (n t)")
+        def turn_z(h, b):
+            zt_ps[h] = bank(b, [P, 2, 2, P], f"zt_ps{h}")
+            for i in range(2):
+                words = zw[2 * h + i][:].bitcast(F32)
+                for u in range(2):
+                    nc.tensor.transpose(zt_ps[h][:, i, u, :], words[:, P * u : P * u + P], ident[:])
+
+        def copy_z(r):
+            nc.scalar.copy(
+                out=zg[r][:].bitcast(F32).rearrange("p (n u) -> p n u", u=2),
+                in_=zt_ps[r // 2][:, r % 2].rearrange("p u n -> p n u"),
             )
 
-        def base(r, c0, width, tag, bufs):
-            y_ps[r, c0] = psum.tile([P, width], F32, tag=tag, bufs=bufs, name=f"y_ps{r}_{c0}")
-            f, c = c0 // 512, c0 % 512
-            for g in range(2):
-                codes, scales = xq_of(r, g)
-                nc.tensor.matmul_mx(
-                    out=y_ps[r, c0][:],
-                    lhsT=codes,
-                    lhsT_scale=scales,
-                    rhs=w0_c[f][:, g, c : c + width].bitcast(FP8X4),
-                    rhs_scale=w0_sc[4 * g :, c0 : c0 + width],
-                    start=(g == 0),
-                    stop=False,
-                )
+        def quantize_z(r):
+            nc.vector.quantize_mx(out=zq[r][:].bitcast(FP8X4), scales=zs[r][:], in_=zg[r][:])
 
         def lora(r, c0, width):
+            f, c = divmod(c0, HALF)
             nc.tensor.matmul_mx(
                 out=y_ps[r, c0][:],
                 lhsT=zq[r][:].bitcast(FP8X4),
                 lhsT_scale=zs[r][:],
-                rhs=b_c[:, c0 : c0 + width].bitcast(FP8X4),
+                rhs=b_c[f][:, c : c + width].bitcast(FP8X4),
                 rhs_scale=b_sc[:, c0 : c0 + width],
                 start=False,
                 stop=True,
             )
 
-        def empty(r, c0, width):
-            engine_copy = nc.vector.tensor_copy if (r, c0) in Y_V else nc.scalar.copy
-            engine_copy(out=yo[r][:, c0 : c0 + width], in_=y_ps[r, c0][:])
+        def finish(r, c0, width, copy):
+            cols = slice(c0, c0 + width)
+            copy(out=yo[r][:, cols], in_=y_ps[r, c0][:])
+            nc.sync.dma_start(out=out_view[:, r, cols], in_=yo[r][:, cols])
 
-        def store(r, c0, width):
-            nc.sync.dma_start(out=out_view[:, r, c0 : c0 + width], in_=yo[r][:, c0 : c0 + width])
+        on_s, on_v = nc.scalar.copy, nc.vector.tensor_copy
 
-        def perm_words():
-            nc.vector.tensor_copy(out=a_c[:], in_=a_raw[:].rearrange("p g (m t) -> p g t m", t=4))
-
-        def perm_scales():
-            nc.vector.tensor_copy(out=a_sc[:], in_=a_sc_raw[:].rearrange("p (g m t) -> p g t m", g=2, t=4))
-
-        def bases(r, tag, bufs):
-            base(r, 0, 512, tag, bufs)
-            base(r, 512, 512, tag, bufs)
-
-        def widen(r):
-            widen_vector(r, 0)
-            widen_vector(r, 1)
-
-        def bases(r, tag, bufs):
-            base(r, 0, 512, tag, bufs)
-            base(r, 512, 512, tag, bufs)
-
-        def out_half(r, c0):
-            empty(r, c0, 512)
-
-        for r in (0, 1):
-            widen(r)
-            widen_scalar(r)
-            turn(r)
-        for r in (0, 1):
-            interleave(r, 0)
-            interleave(r, 1)
-        spread_bias()
-        perm_words()
+        widen(0, 0)
+        widen(0, 1)
+        widen(1, 0)
+        widen(1, 1)
+        turn_x(0, 0)
+        turn_x(1, 1)
+        copy_x(0)
+        spread_bias(2)
         quantize_x(0)
-        quantize_x(1)
-        perm_scales()
+        copy_x(1)
         copy_bias()
-        logits(0)
-        logits(1)
+        widen(2, 0)
+        quantize_x(1)
+        widen(2, 1)
+        widen(3, 0)
+        widen(3, 1)
+        logits(0, 3)
+        base(0, 0, HALF, 4)
+        logits(1, 3)
+        base(1, 0, HALF, 5)
         soft_add(0)
-        widen_vector(2, 0)
+        turn_x(2, 0)
+        turn_x(3, 1)
         soft_peak(0)
-        widen_scalar(2)
-        widen_scalar(3)
         soft_exp(0)
-        widen_vector(2, 1)
-        widen(3)
+        copy_x(2)
+        copy_x(3)
+        widen(4, 0)
         soft_recip(0)
+        widen(5, 0)
+        down(0, 6)
+        down(1, 7)
         soft_scale(0)
-        down(0)
-        turn(2)
-        turn(3)
-        turn_gates(0)
-        interleave_tile(2)
-        interleave_tile(3)
-        copy_gates(0)
-        down(1)
         quantize_x(2)
-        quantize_x(3)
         gate(0)
+        quantize_x(3)
         gate(1)
-        for h in range(PAIRS - 1):
-            r0, r1 = 2 * h, 2 * h + 1
-            ahead = range(2 * h + 4, 2 * h + 6) if h + 2 < PAIRS else ()
-            base(r0, 0, 512, "y", 3)
-            logits(r0 + 2)
-            logits(r1 + 2)
-            soft_add(h + 1)
-            quantize_z(r0)
-            soft_peak(h + 1)
-            quantize_z(r1)
-            for r in ahead:
-                widen_scalar(r)
-            for r in ahead[:1]:
-                widen(r)
-            soft_exp(h + 1)
-            soft_recip(h + 1)
-            soft_scale(h + 1)
-            for r in ahead[1:]:
-                widen(r)
-            base(r0, 512, 512, "y", 3)
-            down(r0 + 2)
-            down(r1 + 2)
-            lora(r0, 0, 512)
-            lora(r0, 512, 512)
-            empty(r0, 0, 512)
-            base(r1, 0, 512, "y", 3)
-            turn_gates(h + 1)
-            copy_gates(h + 1)
-            empty(r0, 512, 512)
-            store(r0, 0, F)
-            for r in ahead:
-                turn(r)
-                interleave_tile(r)
-            gate(r0 + 2)
-            for r in ahead:
-                quantize_x(r)
-            gate(r1 + 2)
-            base(r1, 512, 512, "y", 3)
-            lora(r1, 0, 512)
-            lora(r1, 512, 512)
-            empty(r1, 0, 512)
-            empty(r1, 512, 512)
-            store(r1, 0, F)
+        widen(4, 1)
+        widen(5, 1)
+        base(2, 0, HALF, 3)
+        logits(2, 2)
+        logits(3, 2)
+        base(3, 0, HALF, 0)
+        soft_add(1)
+        turn_z(0, 1)
+        turn_x(4, 6)
+        turn_x(5, 7)
+        widen(6, 0)
+        soft_peak(1)
+        soft_exp(1)
+        copy_z(0)
+        copy_z(1)
+        widen(6, 1)
+        soft_recip(1)
+        quantize_z(0)
+        soft_scale(1)
+        quantize_z(1)
+        copy_x(4)
+        copy_x(5)
+        down(2, 2)
+        down(3, 1)
+        quantize_x(4)
+        gate(2)
+        quantize_x(5)
+        gate(3)
+        lora(0, 0, HALF)
+        lora(1, 0, HALF)
+        finish(0, 0, HALF, on_s)
+        finish(1, 0, HALF, on_s)
+        base(0, HALF, HALF, 6)
+        lora(0, HALF, HALF)
+        logits(4, 7)
+        logits(5, 7)
+        base(1, HALF, HALF, 4)
+        lora(1, HALF, HALF)
+        widen(7, 0)
+        soft_add(2)
+        widen(7, 1)
+        soft_peak(2)
+        finish(0, HALF, HALF, on_s)
+        soft_exp(2)
+        finish(1, HALF, HALF, on_s)
+        turn_z(1, 5)
+        turn_x(6, 2)
+        turn_x(7, 1)
+        soft_recip(2)
+        copy_z(2)
+        copy_z(3)
+        quantize_z(2)
+        soft_scale(2)
+        quantize_z(3)
+        copy_x(6)
+        copy_x(7)
+        down(4, 7)
+        down(5, 6)
+        gate(4)
+        quantize_x(6)
+        gate(5)
+        quantize_x(7)
+        lora(2, 0, HALF)
+        lora(3, 0, HALF)
+        finish(2, 0, HALF, on_s)
+        finish(3, 0, HALF, on_s)
+        base(2, HALF, HALF, 4)
+        lora(2, HALF, HALF)
+        base(3, HALF, HALF, 2)
+        lora(3, HALF, HALF)
+        logits(6, 5)
+        logits(7, 5)
+        finish(2, HALF, HALF, on_v)
+        soft_add(3)
+        soft_peak(3)
+        finish(3, HALF, HALF, on_s)
+        soft_exp(3)
+        soft_recip(3)
+        base(4, 0, HALF, 1)
+        base(5, 0, HALF, 3)
+        turn_z(2, 0)
+        soft_scale(3)
+        copy_z(4)
+        copy_z(5)
+        quantize_z(4)
+        down(6, 7)
+        down(7, 6)
+        quantize_z(5)
+        gate(6)
+        gate(7)
+        lora(4, 0, HALF)
+        lora(5, 0, HALF)
+        finish(4, 0, HALF, on_s)
+        finish(5, 0, HALF, on_s)
+        base(4, HALF, HALF, 4)
+        lora(4, HALF, HALF)
+        base(5, HALF, HALF, 5)
+        lora(5, HALF, HALF)
+        finish(4, HALF, HALF, on_v)
+        turn_z(3, 2)
+        copy_z(6)
+        copy_z(7)
+        finish(5, HALF, HALF, on_v)
         quantize_z(6)
         quantize_z(7)
-        bases(6, "tr", 2)
-        for c0 in (0, 512):
-            lora(6, c0, 512)
-            empty(6, c0, 512)
-            store(6, c0, 512)
-        for c0, width in ((0, 512), (512, 256), (768, 256)):
-            base(7, c0, width, "y", 3)
-            lora(7, c0, width)
-            empty(7, c0, width)
-            store(7, c0, width)
+        base(6, 0, HALF, 0)
+        base(6, HALF, HALF, 1)
+        lora(6, 0, HALF)
+        lora(6, HALF, HALF)
+        finish(6, 0, HALF, on_s)
+        finish(6, HALF, HALF, on_v)
+        base(7, 0, HALF, 3)
+        lora(7, 0, HALF)
+        finish(7, 0, HALF, on_s)
+        base(7, HALF, 256, 7)
+        lora(7, HALF, 256)
+        finish(7, HALF, 256, on_v)
+        base(7, 768, 256, 4)
+        lora(7, 768, 256)
+        finish(7, 768, 256, on_s)

@@ -22,8 +22,7 @@ ACT = mybir.ActivationFunctionType
 P = 128
 TILES = 8
 HALF = 512
-HEAD_TILES = 2
-SCALAR_TILES = 6
+SCALAR_TILES = (0, 1, 4, 5)
 PAIRS = TILES // 2
 
 
@@ -58,21 +57,17 @@ def tile_rankwisemoloradenserouter_d2p_kernel(
         w0_view = w0_words.rearrange("g p n t -> p g (n t)")
 
         b_view = b_words[0].rearrange("p n t -> p (n t)")
-        xb_head = [keep.tile([P, D], U8, align_bytes=64, name=f"xb_head{r}") for r in range(HEAD_TILES)]
-        xb = [keep.tile([P, 2, D], U8, align_bytes=64, name=f"xb{h}") for h in range(1, TILES // 2)]
+        xb = [keep.tile([P, 2, D], U8, align_bytes=64, name=f"xb{h}") for h in range(PAIRS)]
         wr_c = keep.tile([P, 2, E], I32, align_bytes=64, name="wr_c")
         a_c = keep.tile([P, 2, R], I32, align_bytes=64, name="a_c")
         b_c = [keep.tile([P, HALF], I32, align_bytes=64, name=f"b_c{f}") for f in range(2)]
         w0_c = [keep.tile([P, 2, HALF], I32, align_bytes=64, name=f"w0_c{f}") for f in range(2)]
 
         def x_rows(r):
-            return xb_head[r][:] if r < HEAD_TILES else xb[r // 2 - 1][:, r % 2, :]
-
-        def load_x_tile(r):
-            nc.sync.dma_start(out=xb_head[r][:], in_=x_view[:, r, :])
+            return xb[r // 2][:, r % 2, :]
 
         def load_x_pair(h):
-            nc.sync.dma_start(out=xb[h - 1][:], in_=x_view[:, 2 * h : 2 * h + 2, :])
+            nc.sync.dma_start(out=xb[h][:], in_=x_view[:, 2 * h : 2 * h + 2, :])
 
         def load_w0(f):
             nc.sync.dma_start(out=w0_c[f][:], in_=w0_view[:, :, 2048 * f : 2048 * f + 2048].bitcast(I32))
@@ -93,23 +88,21 @@ def tile_rankwisemoloradenserouter_d2p_kernel(
         make_identity(nc, ident[:], nomemset=True)
         nc.scalar.dma_start(out=scale_cols[:], in_=x_scale.unsqueeze(1).to_broadcast([8, 16, 8]))
         nc.scalar.activation(out=ones[:], in_=zeros[:], func=ACT.Exp)
-        nc.gpsimd.dma_start(out=br_rows[0:1, :], in_=br.unsqueeze(0))
-        load_x_tile(0)
-        load_x_tile(1)
-        load_words(wr_c, wr_words)
-        load_scales(wr_sc, wr_scales, 2, range(3))
-        load_w0(0)
-        load_scales(wr_sc, wr_scales, 2, range(3, 4))
+        load_x_pair(0)
         load_x_pair(1)
+        load_words(wr_c, wr_words)
+        load_scales(wr_sc, wr_scales, 2, range(4))
+        nc.sync.dma_start(out=br_rows[0:1, :], in_=br.unsqueeze(0))
+        load_w0(0)
         load_scales(w0_sc, w0_scales, 2, range(4))
         load_words(a_c, a_words)
-        load_scales(a_sc, a_scales, 2, range(4))
         load_x_pair(2)
+        load_scales(a_sc, a_scales, 2, range(4))
+        load_x_pair(3)
         load_b(0)
         load_scales(b_sc, b_scales, 1, range(4))
         load_w0(1)
         load_b(1)
-        load_x_pair(3)
 
         def tiles(shape, dtype, name, count=TILES):
             return [keep.tile(shape, dtype, align_bytes=64, name=f"{name}{r}") for r in range(count)]
@@ -135,7 +128,7 @@ def tile_rankwisemoloradenserouter_d2p_kernel(
             return psum.tile(shape, F32, tag=f"bank{index}", bufs=1, name=name)
 
         def on_scalar(r, g):
-            return r < SCALAR_TILES and g == 1
+            return r in SCALAR_TILES and g == 1
 
         def widen(r, g):
             for j in range(4 * g, 4 * g + 4):
@@ -146,13 +139,8 @@ def tile_rankwisemoloradenserouter_d2p_kernel(
                         out=xw[r][:, cols], in_=source, func=ACT.Copy, scale=scale_cols[:, j : j + 1]
                     )
                 else:
-                    planes = xw[r][:].rearrange("p (g u q e) -> p g q u e", g=2, u=2, e=2)
                     nc.vector.tensor_scalar(
-                        out=planes[:, g, 32 * (j % 4) : 32 * (j % 4) + 32],
-                        in0=source.rearrange("p (q u e) -> p q u e", u=2, e=2),
-                        scalar1=scale_cols[:, j : j + 1],
-                        scalar2=None,
-                        op0=MULT,
+                        out=xw[r][:, cols], in0=source, scalar1=scale_cols[:, j : j + 1], scalar2=None, op0=MULT
                     )
 
         def turn_x(r, b):
@@ -160,10 +148,7 @@ def tile_rankwisemoloradenserouter_d2p_kernel(
             words = xw[r][:].bitcast(F32)
             for g in range(2):
                 for u in range(2):
-                    if on_scalar(r, g):
-                        part = words[:, 256 * g + u : 256 * (g + 1) : 2]
-                    else:
-                        part = words[:, 256 * g + P * u : 256 * g + P * u + P]
+                    part = words[:, 256 * g + u : 256 * (g + 1) : 2]
                     nc.tensor.transpose(xt_ps[r][:, 2 * g + u, :], part, ident[:])
 
         def copy_x(r):
@@ -287,76 +272,76 @@ def tile_rankwisemoloradenserouter_d2p_kernel(
         widen(0, 1)
         widen(1, 0)
         widen(1, 1)
+        widen(2, 0)
+        widen(2, 1)
         turn_x(0, 0)
         turn_x(1, 1)
+        turn_x(2, 2)
         copy_x(0)
-        spread_bias(2)
-        quantize_x(0)
         copy_x(1)
-        copy_bias()
-        widen(2, 0)
-        quantize_x(1)
-        widen(2, 1)
         widen(3, 0)
         widen(3, 1)
-        logits(0, 3)
-        base(0, 0, HALF, 4)
-        logits(1, 3)
-        base(1, 0, HALF, 5)
+        turn_x(3, 3)
+        quantize_x(0)
+        quantize_x(1)
+        copy_x(2)
+        spread_bias(4)
+        copy_bias()
+        copy_x(3)
+        logits(0, 5)
+        logits(1, 5)
+        base(0, 0, HALF, 6)
+        base(1, 0, HALF, 7)
+        quantize_x(2)
         soft_add(0)
-        turn_x(2, 0)
-        turn_x(3, 1)
+        quantize_x(3)
         soft_peak(0)
         soft_exp(0)
-        copy_x(2)
-        copy_x(3)
-        widen(4, 0)
+        logits(2, 0)
+        logits(3, 0)
+        base(2, 0, HALF, 1)
+        down(0, 2)
+        down(1, 3)
+        base(3, 0, HALF, 4)
+        soft_add(1)
         soft_recip(0)
-        widen(5, 0)
-        down(0, 6)
-        down(1, 7)
+        widen(4, 0)
         soft_scale(0)
-        quantize_x(2)
-        gate(0)
-        quantize_x(3)
-        gate(1)
         widen(4, 1)
         widen(5, 1)
-        base(2, 0, HALF, 3)
-        logits(2, 2)
-        logits(3, 2)
-        base(3, 0, HALF, 0)
-        soft_add(1)
-        turn_z(0, 1)
-        turn_x(4, 6)
-        turn_x(5, 7)
-        widen(6, 0)
+        widen(5, 0)
+        gate(0)
+        gate(1)
         soft_peak(1)
         soft_exp(1)
+        turn_x(4, 5)
+        turn_x(5, 0)
+        turn_z(0, 2)
+        copy_x(4)
         copy_z(0)
         copy_z(1)
-        widen(6, 1)
-        soft_recip(1)
-        quantize_z(0)
-        soft_scale(1)
-        quantize_z(1)
-        copy_x(4)
         copy_x(5)
-        down(2, 2)
-        down(3, 1)
+        widen(6, 0)
+        soft_recip(1)
+        widen(6, 1)
+        soft_scale(1)
         quantize_x(4)
+        quantize_z(0)
+        quantize_z(1)
+        down(2, 3)
+        base(0, HALF, HALF, 5)
+        down(3, 2)
         gate(2)
         quantize_x(5)
         gate(3)
         lora(0, 0, HALF)
         lora(1, 0, HALF)
+        lora(0, HALF, HALF)
         finish(0, 0, HALF, on_s)
         finish(1, 0, HALF, on_s)
-        base(0, HALF, HALF, 6)
-        lora(0, HALF, HALF)
-        logits(4, 7)
-        logits(5, 7)
-        base(1, HALF, HALF, 4)
+        logits(4, 0)
+        logits(5, 0)
+        base(1, HALF, HALF, 6)
         lora(1, HALF, HALF)
         widen(7, 0)
         soft_add(2)
@@ -364,20 +349,20 @@ def tile_rankwisemoloradenserouter_d2p_kernel(
         soft_peak(2)
         finish(0, HALF, HALF, on_s)
         soft_exp(2)
-        finish(1, HALF, HALF, on_s)
-        turn_z(1, 5)
-        turn_x(6, 2)
-        turn_x(7, 1)
-        soft_recip(2)
+        turn_z(1, 7)
+        turn_x(6, 3)
+        turn_x(7, 2)
         copy_z(2)
         copy_z(3)
+        finish(1, HALF, HALF, on_v)
+        soft_recip(2)
         quantize_z(2)
         soft_scale(2)
         quantize_z(3)
         copy_x(6)
         copy_x(7)
-        down(4, 7)
-        down(5, 6)
+        down(4, 0)
+        down(5, 5)
         gate(4)
         quantize_x(6)
         gate(5)
@@ -386,27 +371,27 @@ def tile_rankwisemoloradenserouter_d2p_kernel(
         lora(3, 0, HALF)
         finish(2, 0, HALF, on_s)
         finish(3, 0, HALF, on_s)
-        base(2, HALF, HALF, 4)
+        base(2, HALF, HALF, 6)
         lora(2, HALF, HALF)
-        base(3, HALF, HALF, 2)
+        base(3, HALF, HALF, 7)
         lora(3, HALF, HALF)
-        logits(6, 5)
-        logits(7, 5)
+        logits(6, 3)
+        logits(7, 3)
         finish(2, HALF, HALF, on_v)
         soft_add(3)
-        soft_peak(3)
         finish(3, HALF, HALF, on_s)
+        soft_peak(3)
         soft_exp(3)
         soft_recip(3)
-        base(4, 0, HALF, 1)
-        base(5, 0, HALF, 3)
-        turn_z(2, 0)
+        base(4, 0, HALF, 2)
+        base(5, 0, HALF, 1)
+        turn_z(2, 4)
         soft_scale(3)
         copy_z(4)
         copy_z(5)
         quantize_z(4)
-        down(6, 7)
-        down(7, 6)
+        down(6, 0)
+        down(7, 5)
         quantize_z(5)
         gate(6)
         gate(7)
@@ -414,29 +399,29 @@ def tile_rankwisemoloradenserouter_d2p_kernel(
         lora(5, 0, HALF)
         finish(4, 0, HALF, on_s)
         finish(5, 0, HALF, on_s)
-        base(4, HALF, HALF, 4)
+        base(4, HALF, HALF, 6)
         lora(4, HALF, HALF)
-        base(5, HALF, HALF, 5)
+        base(5, HALF, HALF, 7)
         lora(5, HALF, HALF)
         finish(4, HALF, HALF, on_v)
-        turn_z(3, 2)
+        turn_z(3, 3)
         copy_z(6)
         copy_z(7)
         finish(5, HALF, HALF, on_v)
         quantize_z(6)
         quantize_z(7)
-        base(6, 0, HALF, 0)
-        base(6, HALF, HALF, 1)
+        base(6, 0, HALF, 4)
+        base(6, HALF, HALF, 2)
         lora(6, 0, HALF)
         lora(6, HALF, HALF)
         finish(6, 0, HALF, on_s)
         finish(6, HALF, HALF, on_v)
-        base(7, 0, HALF, 3)
+        base(7, 0, HALF, 1)
         lora(7, 0, HALF)
         finish(7, 0, HALF, on_s)
-        base(7, HALF, 256, 7)
+        base(7, HALF, 256, 0)
         lora(7, HALF, 256)
         finish(7, HALF, 256, on_v)
-        base(7, 768, 256, 4)
+        base(7, 768, 256, 5)
         lora(7, 768, 256)
         finish(7, 768, 256, on_s)

@@ -22,7 +22,7 @@ ACT = mybir.ActivationFunctionType
 P = 128
 TILES = 8
 HALF = 512
-SCALAR_TILES = (0, 1, 4, 5)
+PLAIN = ((0, 1), (1, 1), (4, 1), (5, 1))
 PAIRS = TILES // 2
 
 
@@ -49,8 +49,9 @@ def tile_rankwisemoloradenserouter_d2p_kernel(
         nc.vector.memset(wr_sc[:].bitcast(I32), 0)
         nc.vector.memset(ident[:], 0.0)
         nc.vector.memset(br_rows[:], 0.0)
-        for sc in (w0_sc, a_sc, b_sc):
-            nc.vector.memset(sc[:].bitcast(I32), 0)
+        nc.vector.memset(w0_sc[:].bitcast(I32), 0)
+        nc.vector.memset(a_sc[:].bitcast(I32), 0)
+        nc.vector.memset(b_sc[:].bitcast(I32), 0)
 
         x_view = x_bytes.rearrange("(p r) k -> p r k", r=TILES)
         out_view = out.rearrange("(p r) f -> p r f", r=TILES)
@@ -78,10 +79,10 @@ def tile_rankwisemoloradenserouter_d2p_kernel(
         def load_b(f):
             nc.sync.dma_start(out=b_c[f][:], in_=b_view[:, 2048 * f : 2048 * f + 2048].bitcast(I32))
 
-        def load_scales(plane, scales, groups, quadrants):
+        def load_scales(queue, plane, scales, quadrants):
             for q in quadrants:
-                nc.sync.dma_start(
-                    out=plane[32 * q : 32 * q + 4 * groups, :].bitcast(I32),
+                queue.dma_start(
+                    out=plane[32 * q : 32 * q + 4 * scales.shape[0], :].bitcast(I32),
                     in_=scales[:, 4 * q : 4 * q + 4, :].bitcast(I32),
                 )
 
@@ -91,16 +92,16 @@ def tile_rankwisemoloradenserouter_d2p_kernel(
         load_x_pair(0)
         load_x_pair(1)
         load_words(wr_c, wr_words)
-        load_scales(wr_sc, wr_scales, 2, range(4))
+        load_scales(nc.sync, wr_sc, wr_scales, range(0, 4))
         nc.sync.dma_start(out=br_rows[0:1, :], in_=br.unsqueeze(0))
         load_w0(0)
-        load_scales(w0_sc, w0_scales, 2, range(4))
+        load_scales(nc.sync, w0_sc, w0_scales, range(0, 4))
         load_words(a_c, a_words)
         load_x_pair(2)
-        load_scales(a_sc, a_scales, 2, range(4))
+        load_scales(nc.sync, a_sc, a_scales, range(0, 4))
         load_x_pair(3)
         load_b(0)
-        load_scales(b_sc, b_scales, 1, range(4))
+        load_scales(nc.sync, b_sc, b_scales, range(0, 4))
         load_w0(1)
         load_b(1)
 
@@ -127,28 +128,35 @@ def tile_rankwisemoloradenserouter_d2p_kernel(
         def bank(index, shape, name):
             return psum.tile(shape, F32, tag=f"bank{index}", bufs=1, name=name)
 
-        def on_scalar(r, g):
-            return r in SCALAR_TILES and g == 1
-
-        def widen(r, g):
-            for j in range(4 * g, 4 * g + 4):
-                cols = slice(P * j, P * j + P)
-                source = x_rows(r)[:, cols].bitcast(FP8)
-                if on_scalar(r, g):
-                    nc.scalar.activation(
-                        out=xw[r][:, cols], in_=source, func=ACT.Copy, scale=scale_cols[:, j : j + 1]
-                    )
+        def widen_vector(r, blocks):
+            for j in blocks:
+                source = x_rows(r)[:, P * j : P * j + P].bitcast(FP8)
+                if (r, j // 4) in PLAIN:
+                    dest = xw[r][:, P * j : P * j + P]
                 else:
-                    nc.vector.tensor_scalar(
-                        out=xw[r][:, cols], in0=source, scalar1=scale_cols[:, j : j + 1], scalar2=None, op0=MULT
-                    )
+                    planes = xw[r][:].rearrange("p (g u q e) -> p g q u e", g=2, u=2, e=2)
+                    dest = planes[:, j // 4, 32 * (j % 4) : 32 * (j % 4) + 32]
+                    source = source.rearrange("p (q u e) -> p q u e", u=2, e=2)
+                nc.vector.tensor_scalar(
+                    out=dest, in0=source, scalar1=scale_cols[:, j : j + 1], scalar2=None, op0=MULT
+                )
+
+        def widen_scalar(r, blocks):
+            for j in blocks:
+                cols = slice(P * j, P * j + P)
+                nc.scalar.activation(
+                    out=xw[r][:, cols], in_=x_rows(r)[:, cols].bitcast(FP8), func=ACT.Copy, scale=scale_cols[:, j : j + 1]
+                )
 
         def turn_x(r, b):
             xt_ps[r] = bank(b, [P, 4, P], f"xt_ps{r}")
             words = xw[r][:].bitcast(F32)
             for g in range(2):
                 for u in range(2):
-                    part = words[:, 256 * g + u : 256 * (g + 1) : 2]
+                    if (r, g) in PLAIN:
+                        part = words[:, 256 * g + u : 256 * (g + 1) : 2]
+                    else:
+                        part = words[:, 256 * g + P * u : 256 * g + P * u + P]
                     nc.tensor.transpose(xt_ps[r][:, 2 * g + u, :], part, ident[:])
 
         def copy_x(r):
@@ -268,19 +276,19 @@ def tile_rankwisemoloradenserouter_d2p_kernel(
 
         on_s, on_v = nc.scalar.copy, nc.vector.tensor_copy
 
-        widen(0, 0)
-        widen(0, 1)
-        widen(1, 0)
-        widen(1, 1)
-        widen(2, 0)
-        widen(2, 1)
+        widen_vector(0, range(4))
+        widen_scalar(0, range(4, 8))
+        widen_vector(1, range(4))
+        widen_scalar(1, range(4, 8))
+        widen_vector(2, range(4))
+        widen_vector(2, range(4, 8))
         turn_x(0, 0)
         turn_x(1, 1)
         turn_x(2, 2)
         copy_x(0)
         copy_x(1)
-        widen(3, 0)
-        widen(3, 1)
+        widen_vector(3, range(4))
+        widen_vector(3, range(4, 8))
         turn_x(3, 3)
         quantize_x(0)
         quantize_x(1)
@@ -305,11 +313,11 @@ def tile_rankwisemoloradenserouter_d2p_kernel(
         base(3, 0, HALF, 4)
         soft_add(1)
         soft_recip(0)
-        widen(4, 0)
+        widen_vector(4, range(4))
         soft_scale(0)
-        widen(4, 1)
-        widen(5, 1)
-        widen(5, 0)
+        widen_scalar(4, range(4, 8))
+        widen_scalar(5, range(4, 8))
+        widen_vector(5, range(4))
         gate(0)
         gate(1)
         soft_peak(1)
@@ -321,9 +329,9 @@ def tile_rankwisemoloradenserouter_d2p_kernel(
         copy_z(0)
         copy_z(1)
         copy_x(5)
-        widen(6, 0)
+        widen_vector(6, range(4))
         soft_recip(1)
-        widen(6, 1)
+        widen_vector(6, range(4, 8))
         soft_scale(1)
         quantize_x(4)
         quantize_z(0)
@@ -343,9 +351,9 @@ def tile_rankwisemoloradenserouter_d2p_kernel(
         logits(5, 0)
         base(1, HALF, HALF, 6)
         lora(1, HALF, HALF)
-        widen(7, 0)
+        widen_vector(7, range(4))
         soft_add(2)
-        widen(7, 1)
+        widen_vector(7, range(4, 8))
         soft_peak(2)
         finish(0, HALF, HALF, on_s)
         soft_exp(2)

@@ -22,7 +22,7 @@ ACT = mybir.ActivationFunctionType
 P = 128
 TILES = 8
 HALF = 512
-PLAIN = ((0, 1), (1, 1), (4, 1), (5, 1))
+PLAIN = ((0, 1), (1, 1), (4, 1), (5, 1), (6, 1))
 PAIRS = TILES // 2
 
 
@@ -289,12 +289,12 @@ def tile_rankwisemoloradenserouter_d2p_kernel(
         copy_x(1)
         widen_vector(3, range(4))
         widen_vector(3, range(4, 8))
+        spread_bias(4)
         turn_x(3, 3)
         quantize_x(0)
         quantize_x(1)
-        copy_x(2)
-        spread_bias(4)
         copy_bias()
+        copy_x(2)
         copy_x(3)
         logits(0, 5)
         logits(1, 5)
@@ -311,9 +311,9 @@ def tile_rankwisemoloradenserouter_d2p_kernel(
         down(0, 2)
         down(1, 3)
         base(3, 0, HALF, 4)
-        soft_add(1)
-        soft_recip(0)
         widen_vector(4, range(4))
+        soft_recip(0)
+        soft_add(1)
         soft_scale(0)
         widen_scalar(4, range(4, 8))
         widen_scalar(5, range(4, 8))
@@ -321,31 +321,31 @@ def tile_rankwisemoloradenserouter_d2p_kernel(
         gate(0)
         gate(1)
         soft_peak(1)
-        soft_exp(1)
+        widen_scalar(6, range(4, 8))
         turn_x(4, 5)
         turn_x(5, 0)
         turn_z(0, 2)
         copy_x(4)
+        soft_exp(1)
         copy_z(0)
         copy_z(1)
         copy_x(5)
         widen_vector(6, range(4))
-        soft_recip(1)
-        widen_vector(6, range(4, 8))
-        soft_scale(1)
         quantize_x(4)
+        soft_recip(1)
         quantize_z(0)
+        soft_scale(1)
         quantize_z(1)
         down(2, 3)
         base(0, HALF, HALF, 5)
+        lora(0, 0, HALF)
         down(3, 2)
         gate(2)
         quantize_x(5)
         gate(3)
-        lora(0, 0, HALF)
+        finish(0, 0, HALF, on_s)
         lora(1, 0, HALF)
         lora(0, HALF, HALF)
-        finish(0, 0, HALF, on_s)
         finish(1, 0, HALF, on_s)
         logits(4, 0)
         logits(5, 0)
@@ -356,13 +356,13 @@ def tile_rankwisemoloradenserouter_d2p_kernel(
         widen_vector(7, range(4, 8))
         soft_peak(2)
         finish(0, HALF, HALF, on_s)
+        finish(1, HALF, HALF, on_s)
         soft_exp(2)
         turn_z(1, 7)
         turn_x(6, 3)
         turn_x(7, 2)
         copy_z(2)
         copy_z(3)
-        finish(1, HALF, HALF, on_v)
         soft_recip(2)
         quantize_z(2)
         soft_scale(2)
@@ -385,7 +385,7 @@ def tile_rankwisemoloradenserouter_d2p_kernel(
         lora(3, HALF, HALF)
         logits(6, 3)
         logits(7, 3)
-        finish(2, HALF, HALF, on_v)
+        finish(2, HALF, HALF, on_s)
         soft_add(3)
         finish(3, HALF, HALF, on_s)
         soft_peak(3)
@@ -409,27 +409,27 @@ def tile_rankwisemoloradenserouter_d2p_kernel(
         finish(5, 0, HALF, on_s)
         base(4, HALF, HALF, 6)
         lora(4, HALF, HALF)
-        base(5, HALF, HALF, 7)
-        lora(5, HALF, HALF)
         finish(4, HALF, HALF, on_v)
         turn_z(3, 3)
         copy_z(6)
         copy_z(7)
-        finish(5, HALF, HALF, on_v)
         quantize_z(6)
         quantize_z(7)
+        base(5, HALF, HALF, 7)
+        lora(5, HALF, HALF)
+        finish(5, HALF, HALF, on_s)
         base(6, 0, HALF, 4)
-        base(6, HALF, HALF, 2)
         lora(6, 0, HALF)
+        finish(6, 0, HALF, on_v)
+        base(6, HALF, HALF, 2)
         lora(6, HALF, HALF)
-        finish(6, 0, HALF, on_s)
-        finish(6, HALF, HALF, on_v)
+        finish(6, HALF, HALF, on_s)
         base(7, 0, HALF, 1)
         lora(7, 0, HALF)
-        finish(7, 0, HALF, on_s)
+        finish(7, 0, HALF, on_v)
         base(7, HALF, 256, 0)
         lora(7, HALF, 256)
-        finish(7, HALF, 256, on_v)
+        finish(7, HALF, 256, on_s)
         base(7, 768, 256, 5)
         lora(7, 768, 256)
-        finish(7, 768, 256, on_s)
+        finish(7, 768, 256, on_v)

@@ -35,14 +35,14 @@ def tile_rankwisemoloradenserouter_d2p_kernel(
         psum = ctx.enter_context(tc.psum_pool(name="psum", bufs=1))
         ctx.enter_context(tc.manual_schedule())
 
-        wr_sc = keep.tile([P, E], U8, align_bytes=64, name="wr_sc")
-        w0_sc = keep.tile([P, F], U8, align_bytes=64, name="w0_sc")
-        a_sc = keep.tile([P, R], U8, align_bytes=64, name="a_sc")
-        b_sc = keep.tile([P, F], U8, align_bytes=64, name="b_sc")
-        zeros = keep.tile([P, P], BF16, align_bytes=64, name="zeros")
+        wr_sc = keep.tile([P, E], U8, align_bytes=256, name="wr_sc")
+        w0_sc = keep.tile([P, F], U8, align_bytes=256, name="w0_sc")
+        a_sc = keep.tile([P, R], U8, align_bytes=256, name="a_sc")
+        b_sc = keep.tile([P, F], U8, align_bytes=256, name="b_sc")
+        zeros = keep.tile([P, P], BF16, align_bytes=256, name="zeros")
         ident = keep.tile([P, P], F32, name="ident")
-        ones = keep.tile([P, P], BF16, align_bytes=64, name="ones")
-        br_rows = keep.tile([P, E], BF16, align_bytes=64, name="br_rows")
+        ones = keep.tile([P, P], BF16, align_bytes=256, name="ones")
+        br_rows = keep.tile([P, E], BF16, align_bytes=256, name="br_rows")
         br_bc = keep.tile([P, E], F32, name="br_bc")
         scale_cols = keep.tile([P, 8], F32, name="scale_cols")
         nc.vector.memset(zeros[:], 0.0)
@@ -58,11 +58,11 @@ def tile_rankwisemoloradenserouter_d2p_kernel(
         w0_view = w0_words.rearrange("g p n t -> p g (n t)")
 
         b_view = b_words[0].rearrange("p n t -> p (n t)")
-        xb = [keep.tile([P, 2, D], U8, align_bytes=64, name=f"xb{h}") for h in range(PAIRS)]
-        wr_c = keep.tile([P, 2, E], I32, align_bytes=64, name="wr_c")
-        a_c = keep.tile([P, 2, R], I32, align_bytes=64, name="a_c")
-        b_c = [keep.tile([P, HALF], I32, align_bytes=64, name=f"b_c{f}") for f in range(2)]
-        w0_c = [keep.tile([P, 2, HALF], I32, align_bytes=64, name=f"w0_c{f}") for f in range(2)]
+        xb = [keep.tile([P, 2, D], U8, align_bytes=256, name=f"xb{h}") for h in range(PAIRS)]
+        wr_c = keep.tile([P, 2, E], I32, align_bytes=256, name="wr_c")
+        a_c = keep.tile([P, 2, R], I32, align_bytes=256, name="a_c")
+        b_c = [keep.tile([P, HALF], I32, align_bytes=256, name=f"b_c{f}") for f in range(2)]
+        w0_c = [keep.tile([P, 2, HALF], I32, align_bytes=256, name=f"w0_c{f}") for f in range(2)]
 
         def x_rows(r):
             return xb[r // 2][:, r % 2, :]
@@ -106,7 +106,7 @@ def tile_rankwisemoloradenserouter_d2p_kernel(
         load_b(1)
 
         def tiles(shape, dtype, name, count=TILES):
-            return [keep.tile(shape, dtype, align_bytes=64, name=f"{name}{r}") for r in range(count)]
+            return [keep.tile(shape, dtype, align_bytes=256, name=f"{name}{r}") for r in range(count)]
 
         xw = tiles([P, D], BF16, "xw")
         xg = tiles([P, D], BF16, "xg")
@@ -373,23 +373,23 @@ def tile_rankwisemoloradenserouter_d2p_kernel(
         down(5, 5)
         gate(4)
         quantize_x(6)
-        gate(5)
         quantize_x(7)
+        gate(5)
         lora(2, 0, HALF)
         lora(3, 0, HALF)
         finish(2, 0, HALF, on_s)
         finish(3, 0, HALF, on_s)
         base(2, HALF, HALF, 6)
         lora(2, HALF, HALF)
-        base(3, HALF, HALF, 7)
-        lora(3, HALF, HALF)
         logits(6, 3)
         logits(7, 3)
-        finish(2, HALF, HALF, on_s)
         soft_add(3)
-        finish(3, HALF, HALF, on_s)
+        base(3, HALF, HALF, 7)
+        lora(3, HALF, HALF)
         soft_peak(3)
+        finish(2, HALF, HALF, on_s)
         soft_exp(3)
+        finish(3, HALF, HALF, on_s)
         soft_recip(3)
         base(4, 0, HALF, 2)
         base(5, 0, HALF, 1)
@@ -409,27 +409,27 @@ def tile_rankwisemoloradenserouter_d2p_kernel(
         finish(5, 0, HALF, on_s)
         base(4, HALF, HALF, 6)
         lora(4, HALF, HALF)
+        base(5, HALF, HALF, 7)
+        lora(5, HALF, HALF)
         finish(4, HALF, HALF, on_v)
         turn_z(3, 3)
         copy_z(6)
         copy_z(7)
+        finish(5, HALF, HALF, on_v)
         quantize_z(6)
         quantize_z(7)
-        base(5, HALF, HALF, 7)
-        lora(5, HALF, HALF)
-        finish(5, HALF, HALF, on_s)
         base(6, 0, HALF, 4)
-        lora(6, 0, HALF)
-        finish(6, 0, HALF, on_v)
         base(6, HALF, HALF, 2)
+        lora(6, 0, HALF)
         lora(6, HALF, HALF)
-        finish(6, HALF, HALF, on_s)
+        finish(6, 0, HALF, on_s)
+        finish(6, HALF, HALF, on_v)
         base(7, 0, HALF, 1)
         lora(7, 0, HALF)
-        finish(7, 0, HALF, on_v)
+        finish(7, 0, HALF, on_s)
         base(7, HALF, 256, 0)
         lora(7, HALF, 256)
-        finish(7, HALF, 256, on_s)
+        finish(7, HALF, 256, on_v)
         base(7, 768, 256, 5)
         lora(7, 768, 256)
-        finish(7, 768, 256, on_v)
+        finish(7, 768, 256, on_s)

@@ -22,7 +22,7 @@ ACT = mybir.ActivationFunctionType
 P = 128
 TILES = 8
 HALF = 512
-PLAIN = ((0, 1), (1, 1), (4, 1), (5, 1), (6, 1))
+PLAIN = ((1, 1), (3, 1), (4, 1), (5, 1))
 PAIRS = TILES // 2
 
 
@@ -41,16 +41,18 @@ def tile_rankwisemoloradenserouter_d2p_kernel(
         b_sc = keep.tile([P, F], U8, align_bytes=256, name="b_sc")
         zeros = keep.tile([P, P], BF16, align_bytes=256, name="zeros")
         ident = keep.tile([P, P], F32, name="ident")
+        idle = keep.tile([P, HALF], BF16, align_bytes=256, name="idle")
         ones = keep.tile([P, P], BF16, align_bytes=256, name="ones")
         br_rows = keep.tile([P, E], BF16, align_bytes=256, name="br_rows")
         br_bc = keep.tile([P, E], F32, name="br_bc")
         scale_cols = keep.tile([P, 8], F32, name="scale_cols")
+        nc.vector.memset(a_sc[:].bitcast(I32), 0)
+        nc.vector.memset(idle[:], 0.0)
         nc.vector.memset(zeros[:], 0.0)
-        nc.vector.memset(wr_sc[:].bitcast(I32), 0)
         nc.vector.memset(ident[:], 0.0)
         nc.vector.memset(br_rows[:], 0.0)
+        nc.vector.memset(wr_sc[:].bitcast(I32), 0)
         nc.vector.memset(w0_sc[:].bitcast(I32), 0)
-        nc.vector.memset(a_sc[:].bitcast(I32), 0)
         nc.vector.memset(b_sc[:].bitcast(I32), 0)
 
         x_view = x_bytes.rearrange("(p r) k -> p r k", r=TILES)
@@ -58,17 +60,20 @@ def tile_rankwisemoloradenserouter_d2p_kernel(
         w0_view = w0_words.rearrange("g p n t -> p g (n t)")
 
         b_view = b_words[0].rearrange("p n t -> p (n t)")
-        xb = [keep.tile([P, 2, D], U8, align_bytes=256, name=f"xb{h}") for h in range(PAIRS)]
+        x_groups = ((0, 1), (1, 2), (2, 4), (4, 6), (6, 8))
+        xb = [keep.tile([P, r1 - r0, D], U8, align_bytes=256, name=f"xb{r0}") for r0, r1 in x_groups]
         wr_c = keep.tile([P, 2, E], I32, align_bytes=256, name="wr_c")
         a_c = keep.tile([P, 2, R], I32, align_bytes=256, name="a_c")
         b_c = [keep.tile([P, HALF], I32, align_bytes=256, name=f"b_c{f}") for f in range(2)]
         w0_c = [keep.tile([P, 2, HALF], I32, align_bytes=256, name=f"w0_c{f}") for f in range(2)]
 
         def x_rows(r):
-            return xb[r // 2][:, r % 2, :]
+            i = [r0 <= r < r1 for r0, r1 in x_groups].index(True)
+            return xb[i][:, r - x_groups[i][0], :]
 
-        def load_x_pair(h):
-            nc.sync.dma_start(out=xb[h][:], in_=x_view[:, 2 * h : 2 * h + 2, :])
+        def load_x(i):
+            r0, r1 = x_groups[i]
+            nc.sync.dma_start(out=xb[i][:], in_=x_view[:, r0:r1, :])
 
         def load_w0(f):
             nc.sync.dma_start(out=w0_c[f][:], in_=w0_view[:, :, 2048 * f : 2048 * f + 2048].bitcast(I32))
@@ -89,27 +94,29 @@ def tile_rankwisemoloradenserouter_d2p_kernel(
         make_identity(nc, ident[:], nomemset=True)
         nc.scalar.dma_start(out=scale_cols[:], in_=x_scale.unsqueeze(1).to_broadcast([8, 16, 8]))
         nc.scalar.activation(out=ones[:], in_=zeros[:], func=ACT.Exp)
-        load_x_pair(0)
-        load_x_pair(1)
+        load_x(0)
+        load_x(1)
+        load_x(2)
+        load_scales(nc.sync, a_sc, a_scales, range(0, 4))
+        load_words(a_c, a_words)
         load_words(wr_c, wr_words)
-        load_scales(nc.sync, wr_sc, wr_scales, range(0, 4))
         nc.sync.dma_start(out=br_rows[0:1, :], in_=br.unsqueeze(0))
+        load_scales(nc.sync, wr_sc, wr_scales, range(0, 4))
+        load_x(3)
         load_w0(0)
         load_scales(nc.sync, w0_sc, w0_scales, range(0, 4))
-        load_words(a_c, a_words)
-        load_x_pair(2)
-        load_scales(nc.sync, a_sc, a_scales, range(0, 4))
-        load_x_pair(3)
+        load_w0(1)
         load_b(0)
         load_scales(nc.sync, b_sc, b_scales, range(0, 4))
-        load_w0(1)
+        load_x(4)
         load_b(1)
 
         def tiles(shape, dtype, name, count=TILES):
             return [keep.tile(shape, dtype, align_bytes=256, name=f"{name}{r}") for r in range(count)]
 
-        xw = tiles([P, D], BF16, "xw")
+        xw = [tiles([P, HALF], BF16, f"xw{r}_", 2) for r in range(TILES)]
         xg = tiles([P, D], BF16, "xg")
+        xg_half = [tiles([P, HALF], BF16, f"xg_half{r}_", 2) for r in range(2)]
         xq = tiles([P, 2 * P], U32, "xq")
         xs = tiles([P, 2 * P], U8, "xs")
         lb = tiles([P, 2, E], F32, "lb", PAIRS)
@@ -128,45 +135,65 @@ def tile_rankwisemoloradenserouter_d2p_kernel(
         def bank(index, shape, name):
             return psum.tile(shape, F32, tag=f"bank{index}", bufs=1, name=name)
 
-        def widen_vector(r, blocks):
-            for j in blocks:
-                source = x_rows(r)[:, P * j : P * j + P].bitcast(FP8)
-                if (r, j // 4) in PLAIN:
-                    dest = xw[r][:, P * j : P * j + P]
-                else:
-                    planes = xw[r][:].rearrange("p (g u q e) -> p g q u e", g=2, u=2, e=2)
-                    dest = planes[:, j // 4, 32 * (j % 4) : 32 * (j % 4) + 32]
-                    source = source.rearrange("p (q u e) -> p q u e", u=2, e=2)
+        def widen_vector(r, g):
+            planes = xw[r][g][:].rearrange("p (u q e) -> p q u e", u=2, e=2)
+            for j in range(4):
+                source = x_rows(r)[:, HALF * g + P * j : HALF * g + P * j + P].bitcast(FP8)
                 nc.vector.tensor_scalar(
-                    out=dest, in0=source, scalar1=scale_cols[:, j : j + 1], scalar2=None, op0=MULT
+                    out=planes[:, 32 * j : 32 * j + 32],
+                    in0=source.rearrange("p (q u e) -> p q u e", u=2, e=2),
+                    scalar1=scale_cols[:, 4 * g + j : 4 * g + j + 1],
+                    scalar2=None,
+                    op0=MULT,
                 )
 
-        def widen_scalar(r, blocks):
+        def widen_scalar(r, g, blocks=range(4)):
             for j in blocks:
-                cols = slice(P * j, P * j + P)
                 nc.scalar.activation(
-                    out=xw[r][:, cols], in_=x_rows(r)[:, cols].bitcast(FP8), func=ACT.Copy, scale=scale_cols[:, j : j + 1]
+                    out=xw[r][g][:, P * j : P * j + P],
+                    in_=x_rows(r)[:, HALF * g + P * j : HALF * g + P * j + P].bitcast(FP8),
+                    func=ACT.Copy,
+                    scale=scale_cols[:, 4 * g + j : 4 * g + j + 1],
                 )
+
+        def turn_half(r, g, dest):
+            words = xw[r][g][:].bitcast(F32)
+            for u in range(2):
+                part = words[:, u : 2 * P : 2] if (r, g) in PLAIN else words[:, P * u : P * u + P]
+                nc.tensor.transpose(dest[:, u, :], part, ident[:])
 
         def turn_x(r, b):
-            xt_ps[r] = bank(b, [P, 4, P], f"xt_ps{r}")
-            words = xw[r][:].bitcast(F32)
+            xt_ps[r] = bank(b, [P, 2, 2, P], f"xt_ps{r}")
             for g in range(2):
-                for u in range(2):
-                    if (r, g) in PLAIN:
-                        part = words[:, 256 * g + u : 256 * (g + 1) : 2]
-                    else:
-                        part = words[:, 256 * g + P * u : 256 * g + P * u + P]
-                    nc.tensor.transpose(xt_ps[r][:, 2 * g + u, :], part, ident[:])
+                turn_half(r, g, xt_ps[r][:, g])
+
+        def turn_first(r, g, b):
+            xt_ps[r, g] = bank(b, [P, 2, P], f"xt_half{r}_{g}")
+            turn_half(r, g, xt_ps[r, g])
+
+        def copy_first(r, g, copy):
+            copy(
+                out=xg_half[r][g][:].bitcast(F32).rearrange("p (n u) -> p n u", u=2),
+                in_=xt_ps[r, g][:].rearrange("p u n -> p n u"),
+            )
+
+        def quantize_first(r, g):
+            cols = slice(P * g, P * g + P)
+            nc.vector.quantize_mx(out=xq[r][:, cols].bitcast(FP8X4), scales=xs[r][:, cols], in_=xg_half[r][g][:])
 
         def copy_x(r):
             nc.scalar.copy(
                 out=xg[r][:].bitcast(F32).rearrange("p (g n u) -> p g n u", g=2, u=2),
-                in_=xt_ps[r][:].rearrange("p (g u) n -> p g n u", g=2),
+                in_=xt_ps[r][:].rearrange("p g u n -> p g n u"),
             )
 
         def quantize_x(r):
             nc.vector.quantize_mx(out=xq[r][:].bitcast(FP8X4), scales=xs[r][:], in_=xg[r][:])
+
+        def warm(count, b):
+            scrap = bank(b, [P, HALF], "scrap")
+            for i in range(count):
+                nc.tensor.matmul(scrap[:], lhsT=idle[:, :P], rhs=idle[:], start=True, stop=True)
 
         def spread_bias(b):
             l_ps["bias"] = bank(b, [P, E], "b_ps")
@@ -223,23 +250,19 @@ def tile_rankwisemoloradenserouter_d2p_kernel(
             nc.vector.reciprocal(out=rs[h][:], in_=sm[h][:])
 
         def soft_scale(h):
-            for i in range(2):
-                nc.vector.tensor_scalar(
-                    out=gt[h][:, i, :],
-                    in0=ex[h][:, i, :],
-                    scalar1=rs[h][:, i : i + 1],
-                    scalar2=float(E),
+            nc.vector.tensor_scalar(out=gt[h][:], in0=ex[h][:], scalar1=float(E), scalar2=None, op0=MULT)
+
+        def gate(r, halves=range(2)):
+            h, i = divmod(r, 2)
+            for u in halves:
+                nc.vector.scalar_tensor_tensor(
+                    out=zw[r][:, 2 * E * u : 2 * E * u + 2 * E].rearrange("p (e c) -> p e c", c=2),
+                    in0=u_ps[r][:].rearrange("p (e u c) -> p u e c", u=2, c=2)[:, u],
+                    scalar=rs[h][:, i : i + 1],
+                    in1=gt[h][:, i, :].unsqueeze(2).to_broadcast([P, E, 2]),
                     op0=MULT,
                     op1=MULT,
                 )
-
-        def gate(r):
-            nc.vector.tensor_tensor(
-                out=zw[r][:].rearrange("p (u e i) -> p u e i", u=2, i=2),
-                in0=u_ps[r][:].rearrange("p (e u i) -> p u e i", u=2, i=2),
-                in1=gt[r // 2][:, r % 2, :].unsqueeze(1).unsqueeze(3).to_broadcast([P, 2, E, 2]),
-                op=MULT,
-            )
 
         def turn_z(h, b):
             zt_ps[h] = bank(b, [P, 2, 2, P], f"zt_ps{h}")
@@ -269,6 +292,10 @@ def tile_rankwisemoloradenserouter_d2p_kernel(
                 stop=True,
             )
 
+        def whole(r, c0, width, b):
+            base(r, c0, width, b)
+            lora(r, c0, width)
+
         def finish(r, c0, width, copy):
             cols = slice(c0, c0 + width)
             copy(out=yo[r][:, cols], in_=y_ps[r, c0][:])
@@ -276,160 +303,161 @@ def tile_rankwisemoloradenserouter_d2p_kernel(
 
         on_s, on_v = nc.scalar.copy, nc.vector.tensor_copy
 
-        widen_vector(0, range(4))
-        widen_scalar(0, range(4, 8))
-        widen_vector(1, range(4))
-        widen_scalar(1, range(4, 8))
-        widen_vector(2, range(4))
-        widen_vector(2, range(4, 8))
-        turn_x(0, 0)
-        turn_x(1, 1)
-        turn_x(2, 2)
-        copy_x(0)
-        copy_x(1)
-        widen_vector(3, range(4))
-        widen_vector(3, range(4, 8))
+        warm(4, 7)
+        widen_vector(0, 0)
+        widen_vector(0, 1)
+        widen_scalar(1, 1)
+        widen_vector(1, 0)
+        turn_first(0, 0, 0)
+        warm(1, 7)
+        turn_first(0, 1, 1)
+        warm(1, 7)
+        turn_first(1, 0, 2)
+        turn_first(1, 1, 6)
+        warm(1, 7)
+        widen_scalar(3, 1)
+        copy_first(0, 0, on_s)
+        copy_first(0, 1, on_s)
+        copy_first(1, 0, on_s)
+        widen_vector(2, 0)
+        widen_vector(2, 1)
+        widen_vector(3, 0)
+        quantize_first(0, 0)
+        quantize_first(0, 1)
+        copy_first(1, 1, on_v)
+        quantize_first(1, 0)
+        quantize_first(1, 1)
+        turn_x(2, 3)
+        turn_x(3, 0)
+        down(0, 1)
         spread_bias(4)
-        turn_x(3, 3)
-        quantize_x(0)
-        quantize_x(1)
-        copy_bias()
-        copy_x(2)
-        copy_x(3)
         logits(0, 5)
         logits(1, 5)
-        base(0, 0, HALF, 6)
-        base(1, 0, HALF, 7)
+        copy_x(2)
+        copy_x(3)
+        copy_bias()
+        down(1, 2)
         quantize_x(2)
         soft_add(0)
         quantize_x(3)
         soft_peak(0)
         soft_exp(0)
-        logits(2, 0)
-        logits(3, 0)
-        base(2, 0, HALF, 1)
-        down(0, 2)
-        down(1, 3)
-        base(3, 0, HALF, 4)
-        widen_vector(4, range(4))
-        soft_recip(0)
+        down(2, 3)
+        logits(2, 4)
+        logits(3, 4)
+        down(3, 0)
+        base(0, 0, HALF, 6)
+        base(1, 0, HALF, 7)
+        widen_scalar(4, 1)
+        widen_vector(4, 0)
+        widen_vector(5, 0)
         soft_add(1)
+        soft_recip(0)
         soft_scale(0)
-        widen_scalar(4, range(4, 8))
-        widen_scalar(5, range(4, 8))
-        widen_vector(5, range(4))
-        gate(0)
-        gate(1)
         soft_peak(1)
-        widen_scalar(6, range(4, 8))
-        turn_x(4, 5)
-        turn_x(5, 0)
-        turn_z(0, 2)
-        copy_x(4)
         soft_exp(1)
+        widen_scalar(5, 1)
+        turn_x(4, 4)
+        base(2, 0, HALF, 5)
+        gate(0)
+        gate(1, range(0, 1))
+        soft_recip(1)
+        soft_scale(1)
+        gate(1, range(1, 2))
+        copy_x(4)
+        turn_x(5, 1)
+        turn_z(0, 2)
+        gate(2)
+        gate(3)
+        copy_x(5)
         copy_z(0)
         copy_z(1)
-        copy_x(5)
-        widen_vector(6, range(4))
         quantize_x(4)
-        soft_recip(1)
+        base(0, HALF, HALF, 3)
+        base(1, HALF, HALF, 0)
+        logits(4, 4)
+        down(4, 1)
+        widen_vector(6, 0)
         quantize_z(0)
-        soft_scale(1)
-        quantize_z(1)
-        down(2, 3)
-        base(0, HALF, HALF, 5)
-        lora(0, 0, HALF)
-        down(3, 2)
-        gate(2)
         quantize_x(5)
-        gate(3)
-        finish(0, 0, HALF, on_s)
-        lora(1, 0, HALF)
+        quantize_z(1)
+        lora(0, 0, HALF)
         lora(0, HALF, HALF)
-        finish(1, 0, HALF, on_s)
-        logits(4, 0)
-        logits(5, 0)
-        base(1, HALF, HALF, 6)
+        logits(5, 4)
+        lora(1, 0, HALF)
         lora(1, HALF, HALF)
-        widen_vector(7, range(4))
-        soft_add(2)
-        widen_vector(7, range(4, 8))
-        soft_peak(2)
+        widen_vector(6, 1)
+        widen_vector(7, 0)
+        widen_vector(7, 1)
+        finish(0, 0, HALF, on_s)
         finish(0, HALF, HALF, on_s)
-        finish(1, HALF, HALF, on_s)
-        soft_exp(2)
-        turn_z(1, 7)
-        turn_x(6, 3)
-        turn_x(7, 2)
+        soft_add(2)
+        turn_z(1, 2)
+        turn_x(6, 6)
+        turn_x(7, 3)
+        finish(1, 0, HALF, on_v)
+        soft_peak(2)
         copy_z(2)
         copy_z(3)
-        soft_recip(2)
+        soft_exp(2)
+        finish(1, HALF, HALF, on_v)
+        down(5, 7)
+        base(2, HALF, HALF, 0)
         quantize_z(2)
+        soft_recip(2)
         soft_scale(2)
         quantize_z(3)
         copy_x(6)
         copy_x(7)
-        down(4, 0)
-        down(5, 5)
+        lora(2, 0, HALF)
+        lora(2, HALF, HALF)
         gate(4)
         quantize_x(6)
-        quantize_x(7)
         gate(5)
-        lora(2, 0, HALF)
-        lora(3, 0, HALF)
+        quantize_x(7)
         finish(2, 0, HALF, on_s)
-        finish(3, 0, HALF, on_s)
-        base(2, HALF, HALF, 6)
-        lora(2, HALF, HALF)
-        logits(6, 3)
-        logits(7, 3)
-        soft_add(3)
-        base(3, HALF, HALF, 7)
-        lora(3, HALF, HALF)
-        soft_peak(3)
+        whole(3, 0, HALF, 2)
+        logits(6, 4)
         finish(2, HALF, HALF, on_s)
-        soft_exp(3)
-        finish(3, HALF, HALF, on_s)
-        soft_recip(3)
-        base(4, 0, HALF, 2)
-        base(5, 0, HALF, 1)
-        turn_z(2, 4)
-        soft_scale(3)
+        whole(3, HALF, HALF, 6)
+        logits(7, 4)
+        soft_add(3)
+        turn_z(2, 1)
+        finish(3, 0, HALF, on_s)
+        soft_peak(3)
         copy_z(4)
         copy_z(5)
+        soft_exp(3)
+        down(6, 3)
+        down(7, 7)
         quantize_z(4)
-        down(6, 0)
-        down(7, 5)
+        finish(3, HALF, HALF, on_v)
         quantize_z(5)
+        soft_recip(3)
+        soft_scale(3)
+        whole(4, 0, HALF, 5)
+        whole(4, HALF, HALF, 0)
         gate(6)
         gate(7)
-        lora(4, 0, HALF)
-        lora(5, 0, HALF)
         finish(4, 0, HALF, on_s)
-        finish(5, 0, HALF, on_s)
-        base(4, HALF, HALF, 6)
-        lora(4, HALF, HALF)
-        base(5, HALF, HALF, 7)
-        lora(5, HALF, HALF)
-        finish(4, HALF, HALF, on_v)
+        base(5, 0, HALF, 2)
         turn_z(3, 3)
+        finish(4, HALF, HALF, on_v)
         copy_z(6)
         copy_z(7)
-        finish(5, HALF, HALF, on_v)
+        lora(5, 0, HALF)
+        whole(5, HALF, HALF, 4)
         quantize_z(6)
         quantize_z(7)
-        base(6, 0, HALF, 4)
-        base(6, HALF, HALF, 2)
-        lora(6, 0, HALF)
-        lora(6, HALF, HALF)
+        finish(5, 0, HALF, on_s)
+        finish(5, HALF, HALF, on_v)
+        whole(6, 0, HALF, 6)
         finish(6, 0, HALF, on_s)
+        whole(6, HALF, HALF, 1)
         finish(6, HALF, HALF, on_v)
-        base(7, 0, HALF, 1)
-        lora(7, 0, HALF)
+        whole(7, 0, HALF, 5)
         finish(7, 0, HALF, on_s)
-        base(7, HALF, 256, 0)
-        lora(7, HALF, 256)
+        whole(7, HALF, 256, 0)
         finish(7, HALF, 256, on_v)
-        base(7, 768, 256, 5)
-        lora(7, 768, 256)
+        whole(7, 768, 256, 7)
         finish(7, 768, 256, on_s)

@@ -22,7 +22,8 @@ ACT = mybir.ActivationFunctionType
 P = 128
 TILES = 8
 HALF = 512
-PLAIN = ((1, 1), (3, 1), (4, 1), (5, 1))
+PLAIN = ((1, 1), (3, 1))
+SORTED = ((4, 1), (5, 1), (7, 1))
 PAIRS = TILES // 2
 
 
@@ -115,6 +116,7 @@ def tile_rankwisemoloradenserouter_d2p_kernel(
             return [keep.tile(shape, dtype, align_bytes=256, name=f"{name}{r}") for r in range(count)]
 
         xw = [tiles([P, HALF], BF16, f"xw{r}_", 2) for r in range(TILES)]
+        xp = {key: keep.tile([P, HALF], BF16, align_bytes=256, name=f"xp{key[0]}_{key[1]}") for key in SORTED}
         xg = tiles([P, D], BF16, "xg")
         xg_half = [tiles([P, HALF], BF16, f"xg_half{r}_", 2) for r in range(2)]
         xq = tiles([P, 2 * P], U32, "xq")
@@ -150,11 +152,17 @@ def tile_rankwisemoloradenserouter_d2p_kernel(
         def widen_scalar(r, g, blocks=range(4)):
             for j in blocks:
                 nc.scalar.activation(
-                    out=xw[r][g][:, P * j : P * j + P],
+                    out=(xp[r, g] if (r, g) in SORTED else xw[r][g])[:, P * j : P * j + P],
                     in_=x_rows(r)[:, HALF * g + P * j : HALF * g + P * j + P].bitcast(FP8),
                     func=ACT.Copy,
                     scale=scale_cols[:, 4 * g + j : 4 * g + j + 1],
                 )
+
+        def sort_words(r, g, copy):
+            copy(
+                out=xw[r][g][:].bitcast(F32).rearrange("p (u q) -> p u q", u=2),
+                in_=xp[r, g][:].bitcast(F32).rearrange("p (q u) -> p u q", u=2),
+            )
 
         def turn_half(r, g, dest):
             words = xw[r][g][:].bitcast(F32)
@@ -181,8 +189,8 @@ def tile_rankwisemoloradenserouter_d2p_kernel(
             cols = slice(P * g, P * g + P)
             nc.vector.quantize_mx(out=xq[r][:, cols].bitcast(FP8X4), scales=xs[r][:, cols], in_=xg_half[r][g][:])
 
-        def copy_x(r):
-            nc.scalar.copy(
+        def copy_x(r, copy=nc.scalar.copy):
+            copy(
                 out=xg[r][:].bitcast(F32).rearrange("p (g n u) -> p g n u", g=2, u=2),
                 in_=xt_ps[r][:].rearrange("p g u n -> p g n u"),
             )
@@ -319,12 +327,12 @@ def tile_rankwisemoloradenserouter_d2p_kernel(
         copy_first(0, 0, on_s)
         copy_first(0, 1, on_s)
         copy_first(1, 0, on_s)
+        copy_first(1, 1, on_s)
         widen_vector(2, 0)
         widen_vector(2, 1)
         widen_vector(3, 0)
         quantize_first(0, 0)
         quantize_first(0, 1)
-        copy_first(1, 1, on_v)
         quantize_first(1, 0)
         quantize_first(1, 1)
         turn_x(2, 3)
@@ -338,25 +346,27 @@ def tile_rankwisemoloradenserouter_d2p_kernel(
         copy_bias()
         down(1, 2)
         quantize_x(2)
+        widen_vector(4, 0)
         soft_add(0)
+        widen_scalar(4, 1)
+        sort_words(4, 1, on_s)
         quantize_x(3)
         soft_peak(0)
         soft_exp(0)
+        widen_scalar(5, 1)
         down(2, 3)
         logits(2, 4)
         logits(3, 4)
         down(3, 0)
         base(0, 0, HALF, 6)
         base(1, 0, HALF, 7)
-        widen_scalar(4, 1)
-        widen_vector(4, 0)
         widen_vector(5, 0)
         soft_add(1)
         soft_recip(0)
         soft_scale(0)
         soft_peak(1)
         soft_exp(1)
-        widen_scalar(5, 1)
+        sort_words(5, 1, on_s)
         turn_x(4, 4)
         base(2, 0, HALF, 5)
         gate(0)
@@ -372,6 +382,8 @@ def tile_rankwisemoloradenserouter_d2p_kernel(
         copy_x(5)
         copy_z(0)
         copy_z(1)
+        widen_scalar(7, 1)
+        sort_words(7, 1, on_s)
         quantize_x(4)
         base(0, HALF, HALF, 3)
         base(1, HALF, HALF, 0)
@@ -388,53 +400,53 @@ def tile_rankwisemoloradenserouter_d2p_kernel(
         lora(1, HALF, HALF)
         widen_vector(6, 1)
         widen_vector(7, 0)
-        widen_vector(7, 1)
         finish(0, 0, HALF, on_s)
-        finish(0, HALF, HALF, on_s)
+        finish(0, HALF, HALF, on_v)
+        finish(1, 0, HALF, on_s)
         soft_add(2)
         turn_z(1, 2)
         turn_x(6, 6)
         turn_x(7, 3)
-        finish(1, 0, HALF, on_v)
+        finish(1, HALF, HALF, on_v)
         soft_peak(2)
         copy_z(2)
         copy_z(3)
         soft_exp(2)
-        finish(1, HALF, HALF, on_v)
         down(5, 7)
         base(2, HALF, HALF, 0)
         quantize_z(2)
+        copy_x(6, on_v)
+        quantize_z(3)
         soft_recip(2)
         soft_scale(2)
-        quantize_z(3)
-        copy_x(6)
         copy_x(7)
         lora(2, 0, HALF)
         lora(2, HALF, HALF)
-        gate(4)
         quantize_x(6)
-        gate(5)
+        gate(4)
         quantize_x(7)
+        gate(5)
         finish(2, 0, HALF, on_s)
         whole(3, 0, HALF, 2)
         logits(6, 4)
         finish(2, HALF, HALF, on_s)
-        whole(3, HALF, HALF, 6)
+        base(3, HALF, HALF, 6)
         logits(7, 4)
+        lora(3, HALF, HALF)
         soft_add(3)
         turn_z(2, 1)
         finish(3, 0, HALF, on_s)
         soft_peak(3)
         copy_z(4)
-        copy_z(5)
         soft_exp(3)
+        copy_z(5)
         down(6, 3)
         down(7, 7)
-        quantize_z(4)
         finish(3, HALF, HALF, on_v)
-        quantize_z(5)
+        quantize_z(4)
         soft_recip(3)
         soft_scale(3)
+        quantize_z(5)
         whole(4, 0, HALF, 5)
         whole(4, HALF, HALF, 0)
         gate(6)

@@ -47,11 +47,10 @@ def tile_rankwisemoloradenserouter_d2p_kernel(
         br_rows = keep.tile([P, E], BF16, align_bytes=256, name="br_rows")
         br_bc = keep.tile([P, E], F32, name="br_bc")
         scale_cols = keep.tile([P, 8], F32, name="scale_cols")
-        nc.vector.memset(a_sc[:].bitcast(I32), 0)
         nc.vector.memset(idle[:], 0.0)
-        nc.vector.memset(zeros[:], 0.0)
-        nc.vector.memset(ident[:], 0.0)
         nc.vector.memset(br_rows[:], 0.0)
+        nc.vector.memset(a_sc[:].bitcast(I32), 0)
+        nc.vector.memset(zeros[:], 0.0)
         nc.vector.memset(wr_sc[:].bitcast(I32), 0)
         nc.vector.memset(w0_sc[:].bitcast(I32), 0)
         nc.vector.memset(b_sc[:].bitcast(I32), 0)
@@ -92,16 +91,16 @@ def tile_rankwisemoloradenserouter_d2p_kernel(
                     in_=scales[:, 4 * q : 4 * q + 4, :].bitcast(I32),
                 )
 
-        make_identity(nc, ident[:], nomemset=True)
+        make_identity(nc, ident[:])
         nc.scalar.dma_start(out=scale_cols[:], in_=x_scale.unsqueeze(1).to_broadcast([8, 16, 8]))
         nc.scalar.activation(out=ones[:], in_=zeros[:], func=ACT.Exp)
         load_x(0)
         load_x(1)
         load_x(2)
+        nc.sync.dma_start(out=br_rows[0:1, :], in_=br.unsqueeze(0))
         load_scales(nc.sync, a_sc, a_scales, range(0, 4))
         load_words(a_c, a_words)
         load_words(wr_c, wr_words)
-        nc.sync.dma_start(out=br_rows[0:1, :], in_=br.unsqueeze(0))
         load_scales(nc.sync, wr_sc, wr_scales, range(0, 4))
         load_x(3)
         load_w0(0)
@@ -170,9 +169,9 @@ def tile_rankwisemoloradenserouter_d2p_kernel(
                 part = words[:, u : 2 * P : 2] if (r, g) in PLAIN else words[:, P * u : P * u + P]
                 nc.tensor.transpose(dest[:, u, :], part, ident[:])
 
-        def turn_x(r, b):
+        def turn_x(r, b, order=(0, 1)):
             xt_ps[r] = bank(b, [P, 2, 2, P], f"xt_ps{r}")
-            for g in range(2):
+            for g in order:
                 turn_half(r, g, xt_ps[r][:, g])
 
         def turn_first(r, g, b):
@@ -335,15 +334,15 @@ def tile_rankwisemoloradenserouter_d2p_kernel(
         quantize_first(0, 1)
         quantize_first(1, 0)
         quantize_first(1, 1)
-        turn_x(2, 3)
-        turn_x(3, 0)
-        down(0, 1)
         spread_bias(4)
+        turn_x(2, 3)
+        turn_x(3, 0, (1, 0))
+        down(0, 1)
         logits(0, 5)
         logits(1, 5)
+        copy_bias()
         copy_x(2)
         copy_x(3)
-        copy_bias()
         down(1, 2)
         quantize_x(2)
         widen_vector(4, 0)
@@ -367,32 +366,32 @@ def tile_rankwisemoloradenserouter_d2p_kernel(
         soft_peak(1)
         soft_exp(1)
         sort_words(5, 1, on_s)
-        turn_x(4, 4)
         base(2, 0, HALF, 5)
         gate(0)
         gate(1, range(0, 1))
         soft_recip(1)
         soft_scale(1)
         gate(1, range(1, 2))
-        copy_x(4)
+        turn_x(4, 4)
         turn_x(5, 1)
         turn_z(0, 2)
         gate(2)
         gate(3)
-        copy_x(5)
+        copy_x(4)
         copy_z(0)
         copy_z(1)
+        copy_x(5)
         widen_scalar(7, 1)
         sort_words(7, 1, on_s)
         quantize_x(4)
         base(0, HALF, HALF, 3)
         base(1, HALF, HALF, 0)
         logits(4, 4)
-        down(4, 1)
-        widen_vector(6, 0)
+        down(4, 2)
         quantize_z(0)
-        quantize_x(5)
+        widen_vector(6, 0)
         quantize_z(1)
+        quantize_x(5)
         lora(0, 0, HALF)
         lora(0, HALF, HALF)
         logits(5, 4)
@@ -404,7 +403,7 @@ def tile_rankwisemoloradenserouter_d2p_kernel(
         finish(0, HALF, HALF, on_v)
         finish(1, 0, HALF, on_s)
         soft_add(2)
-        turn_z(1, 2)
+        turn_z(1, 1)
         turn_x(6, 6)
         turn_x(7, 3)
         finish(1, HALF, HALF, on_v)
@@ -427,14 +426,14 @@ def tile_rankwisemoloradenserouter_d2p_kernel(
         quantize_x(7)
         gate(5)
         finish(2, 0, HALF, on_s)
-        whole(3, 0, HALF, 2)
+        whole(3, 0, HALF, 1)
         logits(6, 4)
         finish(2, HALF, HALF, on_s)
         base(3, HALF, HALF, 6)
         logits(7, 4)
         lora(3, HALF, HALF)
         soft_add(3)
-        turn_z(2, 1)
+        turn_z(2, 2)
         finish(3, 0, HALF, on_s)
         soft_peak(3)
         copy_z(4)
@@ -452,7 +451,7 @@ def tile_rankwisemoloradenserouter_d2p_kernel(
         gate(6)
         gate(7)
         finish(4, 0, HALF, on_s)
-        base(5, 0, HALF, 2)
+        base(5, 0, HALF, 1)
         turn_z(3, 3)
         finish(4, HALF, HALF, on_v)
         copy_z(6)
@@ -463,13 +462,17 @@ def tile_rankwisemoloradenserouter_d2p_kernel(
         quantize_z(7)
         finish(5, 0, HALF, on_s)
         finish(5, HALF, HALF, on_v)
-        whole(6, 0, HALF, 6)
-        finish(6, 0, HALF, on_s)
-        whole(6, HALF, HALF, 1)
-        finish(6, HALF, HALF, on_v)
-        whole(7, 0, HALF, 5)
-        finish(7, 0, HALF, on_s)
-        whole(7, HALF, 256, 0)
-        finish(7, HALF, 256, on_v)
-        whole(7, 768, 256, 7)
+        whole(6, 0, 512, 6)
+        finish(6, 0, 512, on_s)
+        whole(6, 512, 256, 2)
+        finish(6, 512, 256, on_v)
+        whole(6, 768, 256, 5)
+        finish(6, 768, 256, on_s)
+        whole(7, 0, 256, 0)
+        finish(7, 0, 256, on_v)
+        whole(7, 256, 256, 7)
+        finish(7, 256, 256, on_s)
+        whole(7, 512, 256, 3)
+        finish(7, 512, 256, on_v)
+        whole(7, 768, 256, 1)
         finish(7, 768, 256, on_s)

@@ -23,7 +23,7 @@ P = 128
 TILES = 8
 HALF = 512
 PLAIN = ((1, 1), (3, 1))
-SORTED = ((4, 1), (5, 1), (7, 1))
+SORTED = ((4, 1), (5, 0), (5, 1), (7, 1))
 PAIRS = TILES // 2
 
 
@@ -321,7 +321,6 @@ def tile_rankwisemoloradenserouter_d2p_kernel(
         warm(1, 7)
         turn_first(1, 0, 2)
         turn_first(1, 1, 6)
-        warm(1, 7)
         widen_scalar(3, 1)
         copy_first(0, 0, on_s)
         copy_first(0, 1, on_s)
@@ -342,29 +341,30 @@ def tile_rankwisemoloradenserouter_d2p_kernel(
         logits(1, 5)
         copy_bias()
         copy_x(2)
-        copy_x(3)
+        copy_x(3, on_v)
         down(1, 2)
         quantize_x(2)
-        widen_vector(4, 0)
         soft_add(0)
         widen_scalar(4, 1)
-        sort_words(4, 1, on_s)
+        widen_scalar(5, 0)
         quantize_x(3)
         soft_peak(0)
+        widen_vector(4, 0)
         soft_exp(0)
-        widen_scalar(5, 1)
+        sort_words(4, 1, on_s)
+        sort_words(5, 0, on_s)
         down(2, 3)
         logits(2, 4)
         logits(3, 4)
         down(3, 0)
         base(0, 0, HALF, 6)
         base(1, 0, HALF, 7)
-        widen_vector(5, 0)
         soft_add(1)
         soft_recip(0)
         soft_scale(0)
         soft_peak(1)
         soft_exp(1)
+        widen_scalar(5, 1)
         sort_words(5, 1, on_s)
         base(2, 0, HALF, 5)
         gate(0)
@@ -373,8 +373,9 @@ def tile_rankwisemoloradenserouter_d2p_kernel(
         soft_scale(1)
         gate(1, range(1, 2))
         turn_x(4, 4)
-        turn_x(5, 1)
+        turn_x(5, 1, (0,))
         turn_z(0, 2)
+        turn_half(5, 1, xt_ps[5][:, 1])
         gate(2)
         gate(3)
         copy_x(4)

@@ -20,11 +20,17 @@ AX = mybir.AxisListType.X
 ACT = mybir.ActivationFunctionType
 
 P = 128
-TILES = 8
-HALF = 512
-PLAIN = ((1, 1), (3, 1))
-SORTED = ((4, 1), (5, 0), (5, 1), (7, 1))
+TILES = T // P
 PAIRS = TILES // 2
+PASS = 512
+BANK = 512
+QUARTER = 256
+BLOCKS = PASS // P
+
+X_LOADS = ((0, 1), (1, 2), (2, 4), (4, 6), (6, 8))
+UNSORTED = ((1, 1), (3, 1))
+SORTED_BY_COPY = ((4, 1), (5, 0), (5, 1), (7, 1))
+BY_HALVES = (0, 1)
 
 
 def tile_rankwisemoloradenserouter_d2p_kernel(
@@ -36,237 +42,248 @@ def tile_rankwisemoloradenserouter_d2p_kernel(
         psum = ctx.enter_context(tc.psum_pool(name="psum", bufs=1))
         ctx.enter_context(tc.manual_schedule())
 
-        wr_sc = keep.tile([P, E], U8, align_bytes=256, name="wr_sc")
-        w0_sc = keep.tile([P, F], U8, align_bytes=256, name="w0_sc")
-        a_sc = keep.tile([P, R], U8, align_bytes=256, name="a_sc")
-        b_sc = keep.tile([P, F], U8, align_bytes=256, name="b_sc")
-        zeros = keep.tile([P, P], BF16, align_bytes=256, name="zeros")
-        ident = keep.tile([P, P], F32, name="ident")
-        idle = keep.tile([P, HALF], BF16, align_bytes=256, name="idle")
-        ones = keep.tile([P, P], BF16, align_bytes=256, name="ones")
-        br_rows = keep.tile([P, E], BF16, align_bytes=256, name="br_rows")
-        br_bc = keep.tile([P, E], F32, name="br_bc")
-        scale_cols = keep.tile([P, 8], F32, name="scale_cols")
-        nc.vector.memset(idle[:], 0.0)
-        nc.vector.memset(br_rows[:], 0.0)
-        nc.vector.memset(a_sc[:].bitcast(I32), 0)
-        nc.vector.memset(zeros[:], 0.0)
-        nc.vector.memset(wr_sc[:].bitcast(I32), 0)
-        nc.vector.memset(w0_sc[:].bitcast(I32), 0)
-        nc.vector.memset(b_sc[:].bitcast(I32), 0)
+        def sbuf(shape, dtype, name):
+            return keep.tile(shape, dtype, align_bytes=256, name=name)
 
-        x_view = x_bytes.rearrange("(p r) k -> p r k", r=TILES)
-        out_view = out.rearrange("(p r) f -> p r f", r=TILES)
-        w0_view = w0_words.rearrange("g p n t -> p g (n t)")
-
-        b_view = b_words[0].rearrange("p n t -> p (n t)")
-        x_groups = ((0, 1), (1, 2), (2, 4), (4, 6), (6, 8))
-        xb = [keep.tile([P, r1 - r0, D], U8, align_bytes=256, name=f"xb{r0}") for r0, r1 in x_groups]
-        wr_c = keep.tile([P, 2, E], I32, align_bytes=256, name="wr_c")
-        a_c = keep.tile([P, 2, R], I32, align_bytes=256, name="a_c")
-        b_c = [keep.tile([P, HALF], I32, align_bytes=256, name=f"b_c{f}") for f in range(2)]
-        w0_c = [keep.tile([P, 2, HALF], I32, align_bytes=256, name=f"w0_c{f}") for f in range(2)]
-
-        def x_rows(r):
-            i = [r0 <= r < r1 for r0, r1 in x_groups].index(True)
-            return xb[i][:, r - x_groups[i][0], :]
-
-        def load_x(i):
-            r0, r1 = x_groups[i]
-            nc.sync.dma_start(out=xb[i][:], in_=x_view[:, r0:r1, :])
-
-        def load_w0(f):
-            nc.sync.dma_start(out=w0_c[f][:], in_=w0_view[:, :, 2048 * f : 2048 * f + 2048].bitcast(I32))
-
-        def load_words(tile, words):
-            nc.sync.dma_start(out=tile[:], in_=words.rearrange("g p n t -> p g (n t)").bitcast(I32))
-
-        def load_b(f):
-            nc.sync.dma_start(out=b_c[f][:], in_=b_view[:, 2048 * f : 2048 * f + 2048].bitcast(I32))
-
-        def load_scales(queue, plane, scales, quadrants):
-            for q in quadrants:
-                queue.dma_start(
-                    out=plane[32 * q : 32 * q + 4 * scales.shape[0], :].bitcast(I32),
-                    in_=scales[:, 4 * q : 4 * q + 4, :].bitcast(I32),
-                )
-
-        make_identity(nc, ident[:])
-        nc.scalar.dma_start(out=scale_cols[:], in_=x_scale.unsqueeze(1).to_broadcast([8, 16, 8]))
-        nc.scalar.activation(out=ones[:], in_=zeros[:], func=ACT.Exp)
-        load_x(0)
-        load_x(1)
-        load_x(2)
-        nc.sync.dma_start(out=br_rows[0:1, :], in_=br.unsqueeze(0))
-        load_scales(nc.sync, a_sc, a_scales, range(0, 4))
-        load_words(a_c, a_words)
-        load_words(wr_c, wr_words)
-        load_scales(nc.sync, wr_sc, wr_scales, range(0, 4))
-        load_x(3)
-        load_w0(0)
-        load_scales(nc.sync, w0_sc, w0_scales, range(0, 4))
-        load_w0(1)
-        load_b(0)
-        load_scales(nc.sync, b_sc, b_scales, range(0, 4))
-        load_x(4)
-        load_b(1)
-
-        def tiles(shape, dtype, name, count=TILES):
-            return [keep.tile(shape, dtype, align_bytes=256, name=f"{name}{r}") for r in range(count)]
-
-        xw = [tiles([P, HALF], BF16, f"xw{r}_", 2) for r in range(TILES)]
-        xp = {key: keep.tile([P, HALF], BF16, align_bytes=256, name=f"xp{key[0]}_{key[1]}") for key in SORTED}
-        xg = tiles([P, D], BF16, "xg")
-        xg_half = [tiles([P, HALF], BF16, f"xg_half{r}_", 2) for r in range(2)]
-        xq = tiles([P, 2 * P], U32, "xq")
-        xs = tiles([P, 2 * P], U8, "xs")
-        lb = tiles([P, 2, E], F32, "lb", PAIRS)
-        ex = tiles([P, 2, E], F32, "ex", PAIRS)
-        gt = tiles([P, 2, E], F32, "gt", PAIRS)
-        nm = tiles([P, 2], F32, "nm", PAIRS)
-        sm = tiles([P, 2], F32, "sm", PAIRS)
-        rs = tiles([P, 2], F32, "rs", PAIRS)
-        zw = tiles([P, R], BF16, "zw")
-        zg = tiles([P, R], BF16, "zg")
-        zq = tiles([P, P], U32, "zq")
-        zs = tiles([P, P], U8, "zs")
-        yo = tiles([P, F], F32, "yo")
-        xt_ps, zt_ps, l_ps, u_ps, y_ps = {}, {}, {}, {}, {}
+        def sbuf_each(keys, shape, dtype, name):
+            return {key: sbuf(shape, dtype, f"{name}_{i}") for i, key in enumerate(keys)}
 
         def bank(index, shape, name):
             return psum.tile(shape, F32, tag=f"bank{index}", bufs=1, name=name)
 
+        zeros = sbuf([P, BANK], BF16, "zeros")
+        ones = sbuf([P, P], BF16, "ones")
+        ident = sbuf([P, P], F32, "ident")
+        br_rows = sbuf([P, E], BF16, "br_rows")
+        br_spread = sbuf([P, E], F32, "br_spread")
+        x_scale_cols = sbuf([P, D // P], F32, "x_scale_cols")
+        wr_sc = sbuf([P, E], U8, "wr_sc")
+        a_sc = sbuf([P, R], U8, "a_sc")
+        w0_sc = sbuf([P, F], U8, "w0_sc")
+        b_sc = sbuf([P, F], U8, "b_sc")
+        x_raw = {(r0, r1): sbuf([P, r1 - r0, D], U8, f"x_raw{r0}") for r0, r1 in X_LOADS}
+        wr_codes = sbuf([P, 2, E], I32, "wr_codes")
+        a_codes = sbuf([P, 2, R], I32, "a_codes")
+        w0_codes = sbuf_each(range(2), [P, 2, BANK], I32, "w0_codes")
+        b_codes = sbuf_each(range(2), [P, 1, BANK], I32, "b_codes")
+
+        nc.vector.memset(zeros[:], 0.0)
+        nc.vector.memset(br_rows[:], 0.0)
+        for plane in (a_sc, wr_sc, w0_sc, b_sc):
+            nc.vector.memset(plane[:].bitcast(I32), 0)
+
+        x_view = x_bytes.rearrange("(p r) k -> p r k", r=TILES)
+        out_view = out.rearrange("(p r) f -> p r f", r=TILES)
+
+        def load_x(i):
+            r0, r1 = X_LOADS[i]
+            nc.sync.dma_start(out=x_raw[r0, r1][:], in_=x_view[:, r0:r1, :])
+
+        def load_codes(tile, words, c0, width):
+            rows = words.rearrange("g p n t -> p g (n t)")
+            nc.sync.dma_start(out=tile, in_=rows[:, :, 4 * c0 : 4 * (c0 + width)].bitcast(I32))
+
+        def load_scales(plane, scales):
+            for quadrant in range(4):
+                nc.sync.dma_start(
+                    out=plane[32 * quadrant : 32 * quadrant + 4 * scales.shape[0], :].bitcast(I32),
+                    in_=scales[:, 4 * quadrant : 4 * quadrant + 4, :].bitcast(I32),
+                )
+
+        make_identity(nc, ident[:])
+        nc.scalar.dma_start(out=x_scale_cols[:], in_=x_scale.unsqueeze(1).to_broadcast([T // P, P // TILES, D // P]))
+        nc.scalar.activation(out=ones[:], in_=zeros[:, :P], func=ACT.Exp)
+        load_x(0)
+        load_x(1)
+        load_x(2)
+        nc.sync.dma_start(out=br_rows[0:1, :], in_=br.unsqueeze(0))
+        load_scales(a_sc, a_scales)
+        load_codes(a_codes[:], a_words, 0, R)
+        load_codes(wr_codes[:], wr_words, 0, E)
+        load_scales(wr_sc, wr_scales)
+        load_x(3)
+        load_codes(w0_codes[0][:], w0_words, 0, BANK)
+        load_scales(w0_sc, w0_scales)
+        load_codes(w0_codes[1][:], w0_words, BANK, BANK)
+        load_codes(b_codes[0][:], b_words, 0, BANK)
+        load_scales(b_sc, b_scales)
+        load_x(4)
+        load_codes(b_codes[1][:], b_words, BANK, BANK)
+
+        halves = [(r, g) for r in range(TILES) for g in range(2)]
+        x_wide = sbuf_each(halves, [P, PASS], BF16, "x_wide")
+        x_plain = sbuf_each(SORTED_BY_COPY, [P, PASS], BF16, "x_plain")
+        x_in = sbuf_each(range(len(BY_HALVES), TILES), [P, D], BF16, "x_in")
+        x_in_half = sbuf_each(halves[: 2 * len(BY_HALVES)], [P, PASS], BF16, "x_in_half")
+        x_codes = sbuf_each(range(TILES), [P, 2 * P], U32, "x_codes")
+        x_sc = sbuf_each(range(TILES), [P, 2 * P], U8, "x_sc")
+        logit = sbuf_each(range(PAIRS), [P, 2, E], F32, "logit")
+        weight = sbuf_each(range(PAIRS), [P, 2, E], F32, "weight")
+        weight_e = sbuf_each(range(PAIRS), [P, 2, E], F32, "weight_e")
+        neg_max = sbuf_each(range(PAIRS), [P, 2], F32, "neg_max")
+        total = sbuf_each(range(PAIRS), [P, 2], F32, "total")
+        inv_total = sbuf_each(range(PAIRS), [P, 2], F32, "inv_total")
+        z_wide = sbuf_each(range(TILES), [P, R], BF16, "z_wide")
+        z_in = sbuf_each(range(TILES), [P, R], BF16, "z_in")
+        z_codes = sbuf_each(range(TILES), [P, P], U32, "z_codes")
+        z_sc = sbuf_each(range(TILES), [P, P], U8, "z_sc")
+        y_out = sbuf_each(range(TILES), [P, F], F32, "y_out")
+        xt_ps, zt_ps, l_ps, u_ps, y_ps, br_ps = {}, {}, {}, {}, {}, {}
+        on_scalar, on_vector = nc.scalar.copy, nc.vector.tensor_copy
+
+        def x_block(r, g, j):
+            r0, r1 = [run for run in X_LOADS if run[0] <= r < run[1]][0]
+            c0 = PASS * g + P * j
+            return x_raw[r0, r1][:, r - r0, c0 : c0 + P].bitcast(FP8), x_scale_cols[:, c0 // P : c0 // P + 1]
+
         def widen_vector(r, g):
-            planes = xw[r][g][:].rearrange("p (u q e) -> p q u e", u=2, e=2)
-            for j in range(4):
-                source = x_rows(r)[:, HALF * g + P * j : HALF * g + P * j + P].bitcast(FP8)
+            runs = x_wide[r, g][:].rearrange("p (s q e) -> p q s e", s=2, e=2)
+            for j in range(BLOCKS):
+                codes, scale = x_block(r, g, j)
                 nc.vector.tensor_scalar(
-                    out=planes[:, 32 * j : 32 * j + 32],
-                    in0=source.rearrange("p (q u e) -> p q u e", u=2, e=2),
-                    scalar1=scale_cols[:, 4 * g + j : 4 * g + j + 1],
+                    out=runs[:, 32 * j : 32 * j + 32],
+                    in0=codes.rearrange("p (q s e) -> p q s e", s=2, e=2),
+                    scalar1=scale,
                     scalar2=None,
                     op0=MULT,
                 )
 
-        def widen_scalar(r, g, blocks=range(4)):
+        def widen_scalar(r, g, blocks=range(BLOCKS)):
+            dest = x_plain[r, g] if (r, g) in SORTED_BY_COPY else x_wide[r, g]
             for j in blocks:
-                nc.scalar.activation(
-                    out=(xp[r, g] if (r, g) in SORTED else xw[r][g])[:, P * j : P * j + P],
-                    in_=x_rows(r)[:, HALF * g + P * j : HALF * g + P * j + P].bitcast(FP8),
-                    func=ACT.Copy,
-                    scale=scale_cols[:, 4 * g + j : 4 * g + j + 1],
-                )
+                codes, scale = x_block(r, g, j)
+                nc.scalar.activation(out=dest[:, P * j : P * j + P], in_=codes, func=ACT.Copy, scale=scale)
 
-        def sort_words(r, g, copy):
-            copy(
-                out=xw[r][g][:].bitcast(F32).rearrange("p (u q) -> p u q", u=2),
-                in_=xp[r, g][:].bitcast(F32).rearrange("p (q u) -> p u q", u=2),
+        def sort_half(r, g):
+            nc.scalar.copy(
+                out=x_wide[r, g][:].bitcast(F32).rearrange("p (s q) -> p s q", s=2),
+                in_=x_plain[r, g][:].bitcast(F32).rearrange("p (q s) -> p s q", s=2),
             )
 
-        def turn_half(r, g, dest):
-            words = xw[r][g][:].bitcast(F32)
-            for u in range(2):
-                part = words[:, u : 2 * P : 2] if (r, g) in PLAIN else words[:, P * u : P * u + P]
-                nc.tensor.transpose(dest[:, u, :], part, ident[:])
+        def transpose_half(r, g, dest):
+            words = x_wide[r, g][:].bitcast(F32)
+            for s in range(2):
+                run = words[:, s::2] if (r, g) in UNSORTED else words[:, P * s : P * s + P]
+                nc.tensor.transpose(dest[:, s, :], run, ident[:])
 
-        def turn_x(r, b, order=(0, 1)):
-            xt_ps[r] = bank(b, [P, 2, 2, P], f"xt_ps{r}")
-            for g in order:
-                turn_half(r, g, xt_ps[r][:, g])
+        def turn_x_half(r, g, b):
+            xt_ps[r, g] = bank(b, [P, 2, P], f"xt_ps{r}_{g}")
+            transpose_half(r, g, xt_ps[r, g])
 
-        def turn_first(r, g, b):
-            xt_ps[r, g] = bank(b, [P, 2, P], f"xt_half{r}_{g}")
-            turn_half(r, g, xt_ps[r, g])
-
-        def copy_first(r, g, copy):
-            copy(
-                out=xg_half[r][g][:].bitcast(F32).rearrange("p (n u) -> p n u", u=2),
-                in_=xt_ps[r, g][:].rearrange("p u n -> p n u"),
+        def copy_x_half(r, g):
+            nc.scalar.copy(
+                out=x_in_half[r, g][:].bitcast(F32).rearrange("p (n s) -> p n s", s=2),
+                in_=xt_ps[r, g][:].rearrange("p s n -> p n s"),
             )
 
-        def quantize_first(r, g):
+        def quantize_x_half(r, g):
             cols = slice(P * g, P * g + P)
-            nc.vector.quantize_mx(out=xq[r][:, cols].bitcast(FP8X4), scales=xs[r][:, cols], in_=xg_half[r][g][:])
+            nc.vector.quantize_mx(out=x_codes[r][:, cols].bitcast(FP8X4), scales=x_sc[r][:, cols], in_=x_in_half[r, g][:])
 
-        def copy_x(r, copy=nc.scalar.copy):
+        def turn_x(r, b, passes=(0, 1)):
+            xt_ps[r] = bank(b, [P, 2, 2, P], f"xt_ps{r}")
+            for g in passes:
+                transpose_half(r, g, xt_ps[r][:, g])
+
+        def copy_x(r, copy):
             copy(
-                out=xg[r][:].bitcast(F32).rearrange("p (g n u) -> p g n u", g=2, u=2),
-                in_=xt_ps[r][:].rearrange("p g u n -> p g n u"),
+                out=x_in[r][:].bitcast(F32).rearrange("p (g n s) -> p g n s", g=2, s=2),
+                in_=xt_ps[r][:].rearrange("p g s n -> p g n s"),
             )
 
         def quantize_x(r):
-            nc.vector.quantize_mx(out=xq[r][:].bitcast(FP8X4), scales=xs[r][:], in_=xg[r][:])
+            nc.vector.quantize_mx(out=x_codes[r][:].bitcast(FP8X4), scales=x_sc[r][:], in_=x_in[r][:])
 
-        def warm(count, b):
-            scrap = bank(b, [P, HALF], "scrap")
+        def warm_up(count, b):
+            scrap = bank(b, [P, BANK], "scrap")
             for i in range(count):
-                nc.tensor.matmul(scrap[:], lhsT=idle[:, :P], rhs=idle[:], start=True, stop=True)
+                nc.tensor.matmul(scrap[:], lhsT=zeros[:, :P], rhs=zeros[:], start=True, stop=True)
 
         def spread_bias(b):
-            l_ps["bias"] = bank(b, [P, E], "b_ps")
-            nc.tensor.matmul(l_ps["bias"][:], lhsT=ones[:], rhs=br_rows[:], start=True, stop=True)
+            br_ps[0] = bank(b, [P, E], "br_ps")
+            nc.tensor.matmul(br_ps[0][:], lhsT=ones[:], rhs=br_rows[:], start=True, stop=True)
 
         def copy_bias():
-            nc.scalar.copy(out=br_bc[:], in_=l_ps["bias"][:])
+            nc.scalar.copy(out=br_spread[:], in_=br_ps[0][:])
 
-        def x_product(dest, r, codes_of, plane, cols, close):
+        def x_product(dest, r, codes, c, plane, c0, width, close):
             for g in range(2):
                 nc.tensor.matmul_mx(
                     out=dest,
-                    lhsT=xq[r][:, P * g : P * g + P].bitcast(FP8X4),
-                    lhsT_scale=xs[r][:, P * g : P * g + P],
-                    rhs=codes_of(g).bitcast(FP8X4),
-                    rhs_scale=plane[4 * g :, cols],
+                    lhsT=x_codes[r][:, P * g : P * g + P].bitcast(FP8X4),
+                    lhsT_scale=x_sc[r][:, P * g : P * g + P],
+                    rhs=codes[:, g, c : c + width].bitcast(FP8X4),
+                    rhs_scale=plane[4 * g :, c0 : c0 + width],
                     start=(g == 0),
                     stop=(close and g == 1),
                 )
 
-        def logits(r, b):
-            if r % 2 == 0:
-                l_ps[r // 2] = bank(b, [P, 2, E], f"l_ps{r // 2}")
-            x_product(l_ps[r // 2][:, r % 2, :], r, lambda g: wr_c[:, g, :], wr_sc, slice(0, E), True)
+        def router(r, b):
+            h, i = divmod(r, 2)
+            if i == 0:
+                l_ps[h] = bank(b, [P, 2, E], f"l_ps{h}")
+            x_product(l_ps[h][:, i, :], r, wr_codes, 0, wr_sc, 0, E, True)
 
         def down(r, b):
             u_ps[r] = bank(b, [P, R], f"u_ps{r}")
-            x_product(u_ps[r][:], r, lambda g: a_c[:, g, :], a_sc, slice(0, R), True)
+            x_product(u_ps[r][:], r, a_codes, 0, a_sc, 0, R, True)
 
         def base(r, c0, width, b):
             y_ps[r, c0] = bank(b, [P, width], f"y_ps{r}_{c0}")
-            f, c = divmod(c0, HALF)
-            x_product(y_ps[r, c0][:], r, lambda g: w0_c[f][:, g, c : c + width], w0_sc, slice(c0, c0 + width), False)
+            f, c = divmod(c0, BANK)
+            x_product(y_ps[r, c0][:], r, w0_codes[f], c, w0_sc, c0, width, False)
 
-        def soft_add(h):
-            nc.vector.tensor_tensor(
-                out=lb[h][:], in0=l_ps[h][:], in1=br_bc[:].unsqueeze(1).to_broadcast([P, 2, E]), op=ADD
+        def lora(r, c0, width):
+            f, c = divmod(c0, BANK)
+            nc.tensor.matmul_mx(
+                out=y_ps[r, c0][:],
+                lhsT=z_codes[r][:].bitcast(FP8X4),
+                lhsT_scale=z_sc[r][:],
+                rhs=b_codes[f][:, 0, c : c + width].bitcast(FP8X4),
+                rhs_scale=b_sc[:, c0 : c0 + width],
+                start=False,
+                stop=True,
             )
 
-        def soft_peak(h):
-            nc.vector.tensor_reduce(out=nm[h][:], in_=lb[h][:], axis=AX, op=MAX, negate=True)
+        def base_and_lora(r, c0, width, b):
+            base(r, c0, width, b)
+            lora(r, c0, width)
 
-        def soft_exp(h):
+        def store(r, c0, width, copy):
+            cols = slice(c0, c0 + width)
+            copy(out=y_out[r][:, cols], in_=y_ps[r, c0][:])
+            nc.sync.dma_start(out=out_view[:, r, cols], in_=y_out[r][:, cols])
+
+        def add_bias(h):
+            nc.vector.tensor_tensor(
+                out=logit[h][:], in0=l_ps[h][:], in1=br_spread[:].unsqueeze(1).to_broadcast([P, 2, E]), op=ADD
+            )
+
+        def row_max(h):
+            nc.vector.tensor_reduce(out=neg_max[h][:], in_=logit[h][:], axis=AX, op=MAX, negate=True)
+
+        def exp_and_sum(h):
             for i in range(2):
                 nc.scalar.activation(
-                    out=ex[h][:, i, :],
-                    in_=lb[h][:, i, :],
+                    out=weight[h][:, i, :],
+                    in_=logit[h][:, i, :],
                     func=ACT.Exp,
-                    bias=nm[h][:, i : i + 1],
-                    accum_out=sm[h][:, i : i + 1],
+                    bias=neg_max[h][:, i : i + 1],
+                    accum_out=total[h][:, i : i + 1],
                 )
 
-        def soft_recip(h):
-            nc.vector.reciprocal(out=rs[h][:], in_=sm[h][:])
+        def normalisers(h):
+            nc.vector.reciprocal(out=inv_total[h][:], in_=total[h][:])
+            nc.vector.tensor_scalar(out=weight_e[h][:], in0=weight[h][:], scalar1=float(E), scalar2=None, op0=MULT)
 
-        def soft_scale(h):
-            nc.vector.tensor_scalar(out=gt[h][:], in0=ex[h][:], scalar1=float(E), scalar2=None, op0=MULT)
-
-        def gate(r, halves=range(2)):
+        def gate(r, runs=(0, 1)):
             h, i = divmod(r, 2)
-            for u in halves:
+            for s in runs:
                 nc.vector.scalar_tensor_tensor(
-                    out=zw[r][:, 2 * E * u : 2 * E * u + 2 * E].rearrange("p (e c) -> p e c", c=2),
-                    in0=u_ps[r][:].rearrange("p (e u c) -> p u e c", u=2, c=2)[:, u],
-                    scalar=rs[h][:, i : i + 1],
-                    in1=gt[h][:, i, :].unsqueeze(2).to_broadcast([P, E, 2]),
+                    out=z_wide[r][:, 2 * E * s : 2 * E * s + 2 * E].rearrange("p (e c) -> p e c", c=2),
+                    in0=u_ps[r][:].rearrange("p (e s c) -> p s e c", s=2, c=2)[:, s],
+                    scalar=inv_total[h][:, i : i + 1],
+                    in1=weight_e[h][:, i, :].unsqueeze(2).to_broadcast([P, E, 2]),
                     op0=MULT,
                     op1=MULT,
                 )
@@ -274,206 +291,173 @@ def tile_rankwisemoloradenserouter_d2p_kernel(
         def turn_z(h, b):
             zt_ps[h] = bank(b, [P, 2, 2, P], f"zt_ps{h}")
             for i in range(2):
-                words = zw[2 * h + i][:].bitcast(F32)
-                for u in range(2):
-                    nc.tensor.transpose(zt_ps[h][:, i, u, :], words[:, P * u : P * u + P], ident[:])
+                words = z_wide[2 * h + i][:].bitcast(F32)
+                for s in range(2):
+                    nc.tensor.transpose(zt_ps[h][:, i, s, :], words[:, P * s : P * s + P], ident[:])
 
         def copy_z(r):
             nc.scalar.copy(
-                out=zg[r][:].bitcast(F32).rearrange("p (n u) -> p n u", u=2),
-                in_=zt_ps[r // 2][:, r % 2].rearrange("p u n -> p n u"),
+                out=z_in[r][:].bitcast(F32).rearrange("p (n s) -> p n s", s=2),
+                in_=zt_ps[r // 2][:, r % 2].rearrange("p s n -> p n s"),
             )
 
         def quantize_z(r):
-            nc.vector.quantize_mx(out=zq[r][:].bitcast(FP8X4), scales=zs[r][:], in_=zg[r][:])
+            nc.vector.quantize_mx(out=z_codes[r][:].bitcast(FP8X4), scales=z_sc[r][:], in_=z_in[r][:])
 
-        def lora(r, c0, width):
-            f, c = divmod(c0, HALF)
-            nc.tensor.matmul_mx(
-                out=y_ps[r, c0][:],
-                lhsT=zq[r][:].bitcast(FP8X4),
-                lhsT_scale=zs[r][:],
-                rhs=b_c[f][:, c : c + width].bitcast(FP8X4),
-                rhs_scale=b_sc[:, c0 : c0 + width],
-                start=False,
-                stop=True,
-            )
 
-        def whole(r, c0, width, b):
-            base(r, c0, width, b)
-            lora(r, c0, width)
-
-        def finish(r, c0, width, copy):
-            cols = slice(c0, c0 + width)
-            copy(out=yo[r][:, cols], in_=y_ps[r, c0][:])
-            nc.sync.dma_start(out=out_view[:, r, cols], in_=yo[r][:, cols])
-
-        on_s, on_v = nc.scalar.copy, nc.vector.tensor_copy
-
-        warm(4, 7)
+        warm_up(4, 7)
         widen_vector(0, 0)
         widen_vector(0, 1)
         widen_scalar(1, 1)
         widen_vector(1, 0)
-        turn_first(0, 0, 0)
-        warm(1, 7)
-        turn_first(0, 1, 1)
-        warm(1, 7)
-        turn_first(1, 0, 2)
-        turn_first(1, 1, 6)
+        for g in range(2):
+            turn_x_half(0, g, g)
+            warm_up(1, 7)
+        turn_x_half(1, 0, 2)
+        turn_x_half(1, 1, 6)
         widen_scalar(3, 1)
-        copy_first(0, 0, on_s)
-        copy_first(0, 1, on_s)
-        copy_first(1, 0, on_s)
-        copy_first(1, 1, on_s)
+        for r, g in x_in_half:
+            copy_x_half(r, g)
         widen_vector(2, 0)
         widen_vector(2, 1)
         widen_vector(3, 0)
-        quantize_first(0, 0)
-        quantize_first(0, 1)
-        quantize_first(1, 0)
-        quantize_first(1, 1)
+        for r, g in x_in_half:
+            quantize_x_half(r, g)
         spread_bias(4)
         turn_x(2, 3)
         turn_x(3, 0, (1, 0))
+
         down(0, 1)
-        logits(0, 5)
-        logits(1, 5)
+        router(0, 5)
+        router(1, 5)
         copy_bias()
-        copy_x(2)
-        copy_x(3, on_v)
+        copy_x(2, on_scalar)
+        copy_x(3, on_vector)
         down(1, 2)
         quantize_x(2)
-        soft_add(0)
+        add_bias(0)
         widen_scalar(4, 1)
-        widen_scalar(5, 0)
+        widen_scalar(5, 0, range(0, BLOCKS // 2))
         quantize_x(3)
-        soft_peak(0)
+        row_max(0)
         widen_vector(4, 0)
-        soft_exp(0)
-        sort_words(4, 1, on_s)
-        sort_words(5, 0, on_s)
+        exp_and_sum(0)
+        widen_scalar(5, 0, range(BLOCKS // 2, BLOCKS))
+        sort_half(4, 1)
+        sort_half(5, 0)
         down(2, 3)
-        logits(2, 4)
-        logits(3, 4)
+        router(2, 4)
+        router(3, 4)
         down(3, 0)
-        base(0, 0, HALF, 6)
-        base(1, 0, HALF, 7)
-        soft_add(1)
-        soft_recip(0)
-        soft_scale(0)
-        soft_peak(1)
-        soft_exp(1)
+        base(0, 0, BANK, 6)
+        base(1, 0, BANK, 7)
+        add_bias(1)
+        normalisers(0)
+        row_max(1)
+        exp_and_sum(1)
         widen_scalar(5, 1)
-        sort_words(5, 1, on_s)
-        base(2, 0, HALF, 5)
+        sort_half(5, 1)
+        base(2, 0, BANK, 5)
         gate(0)
-        gate(1, range(0, 1))
-        soft_recip(1)
-        soft_scale(1)
-        gate(1, range(1, 2))
+        gate(1, (0,))
+        normalisers(1)
+        gate(1, (1,))
+
         turn_x(4, 4)
         turn_x(5, 1, (0,))
         turn_z(0, 2)
-        turn_half(5, 1, xt_ps[5][:, 1])
+        transpose_half(5, 1, xt_ps[5][:, 1])
         gate(2)
         gate(3)
-        copy_x(4)
+        copy_x(4, on_scalar)
         copy_z(0)
         copy_z(1)
-        copy_x(5)
+        copy_x(5, on_scalar)
         widen_scalar(7, 1)
-        sort_words(7, 1, on_s)
+        sort_half(7, 1)
         quantize_x(4)
-        base(0, HALF, HALF, 3)
-        base(1, HALF, HALF, 0)
-        logits(4, 4)
+        base(0, BANK, BANK, 3)
+        base(1, BANK, BANK, 0)
+        router(4, 4)
         down(4, 2)
         quantize_z(0)
         widen_vector(6, 0)
         quantize_z(1)
         quantize_x(5)
-        lora(0, 0, HALF)
-        lora(0, HALF, HALF)
-        logits(5, 4)
-        lora(1, 0, HALF)
-        lora(1, HALF, HALF)
+        lora(0, 0, BANK)
+        lora(0, BANK, BANK)
+        router(5, 4)
+        lora(1, 0, BANK)
+        lora(1, BANK, BANK)
         widen_vector(6, 1)
         widen_vector(7, 0)
-        finish(0, 0, HALF, on_s)
-        finish(0, HALF, HALF, on_v)
-        finish(1, 0, HALF, on_s)
-        soft_add(2)
+        store(0, 0, BANK, on_scalar)
+        store(0, BANK, BANK, on_vector)
+        store(1, 0, BANK, on_scalar)
+        add_bias(2)
+
         turn_z(1, 1)
         turn_x(6, 6)
         turn_x(7, 3)
-        finish(1, HALF, HALF, on_v)
-        soft_peak(2)
+        store(1, BANK, BANK, on_vector)
+        row_max(2)
         copy_z(2)
         copy_z(3)
-        soft_exp(2)
+        exp_and_sum(2)
         down(5, 7)
-        base(2, HALF, HALF, 0)
+        base(2, BANK, BANK, 0)
         quantize_z(2)
-        copy_x(6, on_v)
+        copy_x(6, on_vector)
         quantize_z(3)
-        soft_recip(2)
-        soft_scale(2)
-        copy_x(7)
-        lora(2, 0, HALF)
-        lora(2, HALF, HALF)
+        normalisers(2)
+        copy_x(7, on_scalar)
+        lora(2, 0, BANK)
+        lora(2, BANK, BANK)
         quantize_x(6)
         gate(4)
         quantize_x(7)
         gate(5)
-        finish(2, 0, HALF, on_s)
-        whole(3, 0, HALF, 1)
-        logits(6, 4)
-        finish(2, HALF, HALF, on_s)
-        base(3, HALF, HALF, 6)
-        logits(7, 4)
-        lora(3, HALF, HALF)
-        soft_add(3)
+        store(2, 0, BANK, on_scalar)
+        base_and_lora(3, 0, BANK, 1)
+        router(6, 4)
+        store(2, BANK, BANK, on_scalar)
+        base(3, BANK, BANK, 6)
+        router(7, 4)
+        lora(3, BANK, BANK)
+        add_bias(3)
+
         turn_z(2, 2)
-        finish(3, 0, HALF, on_s)
-        soft_peak(3)
+        store(3, 0, BANK, on_scalar)
+        row_max(3)
         copy_z(4)
-        soft_exp(3)
+        exp_and_sum(3)
         copy_z(5)
         down(6, 3)
         down(7, 7)
-        finish(3, HALF, HALF, on_v)
+        store(3, BANK, BANK, on_vector)
         quantize_z(4)
-        soft_recip(3)
-        soft_scale(3)
+        normalisers(3)
         quantize_z(5)
-        whole(4, 0, HALF, 5)
-        whole(4, HALF, HALF, 0)
+        base_and_lora(4, 0, BANK, 5)
+        base_and_lora(4, BANK, BANK, 0)
         gate(6)
         gate(7)
-        finish(4, 0, HALF, on_s)
-        base(5, 0, HALF, 1)
+        store(4, 0, BANK, on_scalar)
+        base(5, 0, BANK, 1)
+
         turn_z(3, 3)
-        finish(4, HALF, HALF, on_v)
+        store(4, BANK, BANK, on_vector)
         copy_z(6)
         copy_z(7)
-        lora(5, 0, HALF)
-        whole(5, HALF, HALF, 4)
+        lora(5, 0, BANK)
+        base_and_lora(5, BANK, BANK, 4)
         quantize_z(6)
         quantize_z(7)
-        finish(5, 0, HALF, on_s)
-        finish(5, HALF, HALF, on_v)
-        whole(6, 0, 512, 6)
-        finish(6, 0, 512, on_s)
-        whole(6, 512, 256, 2)
-        finish(6, 512, 256, on_v)
-        whole(6, 768, 256, 5)
-        finish(6, 768, 256, on_s)
-        whole(7, 0, 256, 0)
-        finish(7, 0, 256, on_v)
-        whole(7, 256, 256, 7)
-        finish(7, 256, 256, on_s)
-        whole(7, 512, 256, 3)
-        finish(7, 512, 256, on_v)
-        whole(7, 768, 256, 1)
-        finish(7, 768, 256, on_s)
+        store(5, 0, BANK, on_scalar)
+        store(5, BANK, BANK, on_vector)
+        base_and_lora(6, 0, BANK, 6)
+        store(6, 0, BANK, on_scalar)
+        quarters = [(6, c0) for c0 in range(BANK, F, QUARTER)] + [(7, c0) for c0 in range(0, F, QUARTER)]
+        for i, ((r, c0), b) in enumerate(zip(quarters, (2, 5, 0, 7, 3, 1))):
+            base_and_lora(r, c0, QUARTER, b)
+            store(r, c0, QUARTER, on_scalar if i % 2 else on_vector)

@@ -65,7 +65,7 @@ def tile_rankwisemoloradenserouter_d2p_kernel(
         wr_codes = sbuf([P, 2, E], I32, "wr_codes")
         a_codes = sbuf([P, 2, R], I32, "a_codes")
         w0_codes = sbuf_each(range(2), [P, 2, BANK], I32, "w0_codes")
-        b_codes = sbuf_each(range(2), [P, 1, BANK], I32, "b_codes")
+        b_codes = sbuf([P, 1, F], I32, "b_codes")
 
         nc.vector.memset(zeros[:], 0.0)
         nc.vector.memset(br_rows[:], 0.0)
@@ -102,13 +102,13 @@ def tile_rankwisemoloradenserouter_d2p_kernel(
         load_codes(wr_codes[:], wr_words, 0, E)
         load_scales(wr_sc, wr_scales)
         load_x(3)
-        load_codes(w0_codes[0][:], w0_words, 0, BANK)
+        load_codes(w0_codes[0][:, :, :QUARTER], w0_words, 0, QUARTER)
         load_scales(w0_sc, w0_scales)
+        load_codes(w0_codes[0][:, :, QUARTER:], w0_words, QUARTER, QUARTER)
         load_codes(w0_codes[1][:], w0_words, BANK, BANK)
-        load_codes(b_codes[0][:], b_words, 0, BANK)
-        load_scales(b_sc, b_scales)
         load_x(4)
-        load_codes(b_codes[1][:], b_words, BANK, BANK)
+        load_scales(b_sc, b_scales)
+        load_codes(b_codes[:], b_words, 0, F)
 
         halves = [(r, g) for r in range(TILES) for g in range(2)]
         x_wide = sbuf_each(halves, [P, PASS], BF16, "x_wide")
@@ -206,15 +206,15 @@ def tile_rankwisemoloradenserouter_d2p_kernel(
         def copy_bias():
             nc.scalar.copy(out=br_spread[:], in_=br_ps[0][:])
 
-        def x_product(dest, r, codes, c, plane, c0, width, close):
-            for g in range(2):
+        def x_product(dest, r, codes, c, plane, c0, width, close, opens=True, passes=(0, 1)):
+            for g in passes:
                 nc.tensor.matmul_mx(
                     out=dest,
                     lhsT=x_codes[r][:, P * g : P * g + P].bitcast(FP8X4),
                     lhsT_scale=x_sc[r][:, P * g : P * g + P],
                     rhs=codes[:, g, c : c + width].bitcast(FP8X4),
                     rhs_scale=plane[4 * g :, c0 : c0 + width],
-                    start=(g == 0),
+                    start=(opens and g == 0),
                     stop=(close and g == 1),
                 )
 
@@ -228,18 +228,24 @@ def tile_rankwisemoloradenserouter_d2p_kernel(
             u_ps[r] = bank(b, [P, R], f"u_ps{r}")
             x_product(u_ps[r][:], r, a_codes, 0, a_sc, 0, R, True)
 
-        def base(r, c0, width, b):
-            y_ps[r, c0] = bank(b, [P, width], f"y_ps{r}_{c0}")
+        def base(r, c0, width, b, passes=(0, 1)):
+            if 0 in passes:
+                y_ps[r, c0] = bank(b, [P, width], f"y_ps{r}_{c0}")
             f, c = divmod(c0, BANK)
-            x_product(y_ps[r, c0][:], r, w0_codes[f], c, w0_sc, c0, width, False)
+            x_product(y_ps[r, c0][:], r, w0_codes[f], c, w0_sc, c0, width, False, True, passes)
+
+        def base_quarter(r, q, b):
+            if q == 0:
+                y_ps[r, 0] = bank(b, [P, BANK], f"y_ps{r}_0")
+            c0 = QUARTER * q
+            x_product(y_ps[r, 0][:, c0 : c0 + QUARTER], r, w0_codes[0], c0, w0_sc, c0, QUARTER, False, q == 0)
 
         def lora(r, c0, width):
-            f, c = divmod(c0, BANK)
             nc.tensor.matmul_mx(
                 out=y_ps[r, c0][:],
                 lhsT=z_codes[r][:].bitcast(FP8X4),
                 lhsT_scale=z_sc[r][:],
-                rhs=b_codes[f][:, 0, c : c + width].bitcast(FP8X4),
+                rhs=b_codes[:, 0, c0 : c0 + width].bitcast(FP8X4),
                 rhs_scale=b_sc[:, c0 : c0 + width],
                 start=False,
                 stop=True,
@@ -272,9 +278,11 @@ def tile_rankwisemoloradenserouter_d2p_kernel(
                     accum_out=total[h][:, i : i + 1],
                 )
 
-        def normalisers(h):
-            nc.vector.reciprocal(out=inv_total[h][:], in_=total[h][:])
-            nc.vector.tensor_scalar(out=weight_e[h][:], in0=weight[h][:], scalar1=float(E), scalar2=None, op0=MULT)
+        def normalisers(h, tiles=slice(0, 2)):
+            nc.vector.reciprocal(out=inv_total[h][:, tiles], in_=total[h][:, tiles])
+            nc.vector.tensor_scalar(
+                out=weight_e[h][:, tiles], in0=weight[h][:, tiles], scalar1=float(E), scalar2=None, op0=MULT
+            )
 
         def gate(r, runs=(0, 1)):
             h, i = divmod(r, 2)
@@ -288,17 +296,18 @@ def tile_rankwisemoloradenserouter_d2p_kernel(
                     op1=MULT,
                 )
 
-        def turn_z(h, b):
-            zt_ps[h] = bank(b, [P, 2, 2, P], f"zt_ps{h}")
-            for i in range(2):
-                words = z_wide[2 * h + i][:].bitcast(F32)
+        def turn_z(tiles, b):
+            dest = bank(b, [P, len(tiles), 2, P], f"zt_ps{tiles[0]}")
+            for i, r in enumerate(tiles):
+                zt_ps[r] = dest[:, i]
+                words = z_wide[r][:].bitcast(F32)
                 for s in range(2):
-                    nc.tensor.transpose(zt_ps[h][:, i, s, :], words[:, P * s : P * s + P], ident[:])
+                    nc.tensor.transpose(zt_ps[r][:, s, :], words[:, P * s : P * s + P], ident[:])
 
         def copy_z(r):
             nc.scalar.copy(
                 out=z_in[r][:].bitcast(F32).rearrange("p (n s) -> p n s", s=2),
-                in_=zt_ps[r // 2][:, r % 2].rearrange("p s n -> p n s"),
+                in_=zt_ps[r].rearrange("p s n -> p n s"),
             )
 
         def quantize_z(r):
@@ -337,27 +346,29 @@ def tile_rankwisemoloradenserouter_d2p_kernel(
         quantize_x(2)
         add_bias(0)
         widen_scalar(4, 1)
-        widen_scalar(5, 0, range(0, BLOCKS // 2))
+        widen_scalar(5, 0)
         quantize_x(3)
         row_max(0)
         widen_vector(4, 0)
         exp_and_sum(0)
-        widen_scalar(5, 0, range(BLOCKS // 2, BLOCKS))
         sort_half(4, 1)
         sort_half(5, 0)
+        widen_scalar(5, 1, range(0, BLOCKS - 1))
         down(2, 3)
         router(2, 4)
         router(3, 4)
         down(3, 0)
-        base(0, 0, BANK, 6)
-        base(1, 0, BANK, 7)
+        base_quarter(0, 0, 6)
+        base_quarter(1, 0, 7)
         add_bias(1)
         normalisers(0)
         row_max(1)
         exp_and_sum(1)
-        widen_scalar(5, 1)
+        widen_scalar(5, 1, range(BLOCKS - 1, BLOCKS))
         sort_half(5, 1)
-        base(2, 0, BANK, 5)
+        base_quarter(2, 0, 5)
+        for r in range(3):
+            base_quarter(r, 1, None)
         gate(0)
         gate(1, (0,))
         normalisers(1)
@@ -365,7 +376,7 @@ def tile_rankwisemoloradenserouter_d2p_kernel(
 
         turn_x(4, 4)
         turn_x(5, 1, (0,))
-        turn_z(0, 2)
+        turn_z((0, 1), 2)
         transpose_half(5, 1, xt_ps[5][:, 1])
         gate(2)
         gate(3)
@@ -396,68 +407,72 @@ def tile_rankwisemoloradenserouter_d2p_kernel(
         store(1, 0, BANK, on_scalar)
         add_bias(2)
 
-        turn_z(1, 1)
-        turn_x(6, 6)
-        turn_x(7, 3)
-        store(1, BANK, BANK, on_vector)
+        turn_x(6, 1)
+        turn_x(7, 6)
+        turn_z((2, 3), 3)
         row_max(2)
+        copy_x(6, on_scalar)
+        copy_x(7, on_vector)
+        down(5, 7)
+        exp_and_sum(2)
         copy_z(2)
         copy_z(3)
-        exp_and_sum(2)
-        down(5, 7)
-        base(2, BANK, BANK, 0)
-        quantize_z(2)
-        copy_x(6, on_vector)
-        quantize_z(3)
+        quantize_x(6)
+        quantize_x(7)
+        base(3, 0, BANK, 1)
+        router(6, 4)
+        base(2, BANK, BANK, 6, (0,))
+        router(7, 4)
         normalisers(2)
-        copy_x(7, on_scalar)
+        quantize_z(2)
+        gate(4, (0,))
+        store(1, BANK, BANK, on_scalar)
+        base(2, BANK, BANK, 6, (1,))
+        add_bias(3)
+        gate(4, (1,))
+        row_max(3)
         lora(2, 0, BANK)
         lora(2, BANK, BANK)
-        quantize_x(6)
-        gate(4)
-        quantize_x(7)
+        down(6, 3)
+        exp_and_sum(3)
+        quantize_z(3)
         gate(5)
         store(2, 0, BANK, on_scalar)
-        base_and_lora(3, 0, BANK, 1)
-        router(6, 4)
+        down(7, 0)
+        normalisers(3, slice(0, 1))
+        normalisers(3, slice(1, 2))
+        lora(3, 0, BANK)
         store(2, BANK, BANK, on_scalar)
-        base(3, BANK, BANK, 6)
-        router(7, 4)
-        lora(3, BANK, BANK)
-        add_bias(3)
-
-        turn_z(2, 2)
-        store(3, 0, BANK, on_scalar)
-        row_max(3)
-        copy_z(4)
-        exp_and_sum(3)
-        copy_z(5)
-        down(6, 3)
-        down(7, 7)
-        store(3, BANK, BANK, on_vector)
-        quantize_z(4)
-        normalisers(3)
-        quantize_z(5)
-        base_and_lora(4, 0, BANK, 5)
-        base_and_lora(4, BANK, BANK, 0)
+        base_and_lora(3, BANK, BANK, 4)
         gate(6)
         gate(7)
-        store(4, 0, BANK, on_scalar)
-        base(5, 0, BANK, 1)
+        store(3, 0, BANK, on_scalar)
+        base(4, 0, BANK, 5)
 
-        turn_z(3, 3)
-        store(4, BANK, BANK, on_vector)
+        turn_z((4,), 7)
+        turn_z((5,), 2)
+        turn_z((6, 7), 3)
+        store(3, BANK, BANK, on_vector)
+        copy_z(4)
+        copy_z(5)
+        base(4, BANK, BANK, 6)
+        base(5, 0, BANK, 1, (0,))
+        quantize_z(4)
         copy_z(6)
+        quantize_z(5)
         copy_z(7)
+        lora(4, 0, BANK)
+        lora(4, BANK, BANK)
+        base(5, 0, BANK, 1, (1,))
         lora(5, 0, BANK)
-        base_and_lora(5, BANK, BANK, 4)
         quantize_z(6)
         quantize_z(7)
+        store(4, 0, BANK, on_scalar)
+        store(4, BANK, BANK, on_vector)
         store(5, 0, BANK, on_scalar)
+        base_and_lora(5, BANK, BANK, 0)
         store(5, BANK, BANK, on_vector)
-        base_and_lora(6, 0, BANK, 6)
-        store(6, 0, BANK, on_scalar)
-        quarters = [(6, c0) for c0 in range(BANK, F, QUARTER)] + [(7, c0) for c0 in range(0, F, QUARTER)]
-        for i, ((r, c0), b) in enumerate(zip(quarters, (2, 5, 0, 7, 3, 1))):
+        pieces = [(r, c0) for r in (6, 7) for c0 in range(0, F, QUARTER)]
+        for i, ((r, c0), b) in enumerate(zip(pieces, (4, 7, 2, 3, 5, 6, 1, 0))):
             base_and_lora(r, c0, QUARTER, b)
-            store(r, c0, QUARTER, on_scalar if i % 2 else on_vector)
+            store(r, c0, QUARTER, on_vector if i % 2 else on_scalar)

@@ -65,7 +65,7 @@ def tile_rankwisemoloradenserouter_d2p_kernel(
         wr_codes = sbuf([P, 2, E], I32, "wr_codes")
         a_codes = sbuf([P, 2, R], I32, "a_codes")
         w0_codes = sbuf_each(range(2), [P, 2, BANK], I32, "w0_codes")
-        b_codes = sbuf([P, 1, F], I32, "b_codes")
+        b_codes = sbuf_each(range(2), [P, 1, BANK], I32, "b_codes")
 
         nc.vector.memset(zeros[:], 0.0)
         nc.vector.memset(br_rows[:], 0.0)
@@ -102,13 +102,13 @@ def tile_rankwisemoloradenserouter_d2p_kernel(
         load_codes(wr_codes[:], wr_words, 0, E)
         load_scales(wr_sc, wr_scales)
         load_x(3)
-        load_codes(w0_codes[0][:, :, :QUARTER], w0_words, 0, QUARTER)
+        load_codes(w0_codes[0][:], w0_words, 0, BANK)
         load_scales(w0_sc, w0_scales)
-        load_codes(w0_codes[0][:, :, QUARTER:], w0_words, QUARTER, QUARTER)
         load_codes(w0_codes[1][:], w0_words, BANK, BANK)
-        load_x(4)
+        load_codes(b_codes[0][:], b_words, 0, BANK)
         load_scales(b_sc, b_scales)
-        load_codes(b_codes[:], b_words, 0, F)
+        load_x(4)
+        load_codes(b_codes[1][:], b_words, BANK, BANK)
 
         halves = [(r, g) for r in range(TILES) for g in range(2)]
         x_wide = sbuf_each(halves, [P, PASS], BF16, "x_wide")
@@ -206,7 +206,7 @@ def tile_rankwisemoloradenserouter_d2p_kernel(
         def copy_bias():
             nc.scalar.copy(out=br_spread[:], in_=br_ps[0][:])
 
-        def x_product(dest, r, codes, c, plane, c0, width, close, opens=True, passes=(0, 1)):
+        def x_product(dest, r, codes, c, plane, c0, width, close, passes=(0, 1)):
             for g in passes:
                 nc.tensor.matmul_mx(
                     out=dest,
@@ -214,7 +214,7 @@ def tile_rankwisemoloradenserouter_d2p_kernel(
                     lhsT_scale=x_sc[r][:, P * g : P * g + P],
                     rhs=codes[:, g, c : c + width].bitcast(FP8X4),
                     rhs_scale=plane[4 * g :, c0 : c0 + width],
-                    start=(opens and g == 0),
+                    start=(g == 0),
                     stop=(close and g == 1),
                 )
 
@@ -232,20 +232,15 @@ def tile_rankwisemoloradenserouter_d2p_kernel(
             if 0 in passes:
                 y_ps[r, c0] = bank(b, [P, width], f"y_ps{r}_{c0}")
             f, c = divmod(c0, BANK)
-            x_product(y_ps[r, c0][:], r, w0_codes[f], c, w0_sc, c0, width, False, True, passes)
-
-        def base_quarter(r, q, b):
-            if q == 0:
-                y_ps[r, 0] = bank(b, [P, BANK], f"y_ps{r}_0")
-            c0 = QUARTER * q
-            x_product(y_ps[r, 0][:, c0 : c0 + QUARTER], r, w0_codes[0], c0, w0_sc, c0, QUARTER, False, q == 0)
+            x_product(y_ps[r, c0][:], r, w0_codes[f], c, w0_sc, c0, width, False, passes)
 
         def lora(r, c0, width):
+            f, c = divmod(c0, BANK)
             nc.tensor.matmul_mx(
                 out=y_ps[r, c0][:],
                 lhsT=z_codes[r][:].bitcast(FP8X4),
                 lhsT_scale=z_sc[r][:],
-                rhs=b_codes[:, 0, c0 : c0 + width].bitcast(FP8X4),
+                rhs=b_codes[f][:, 0, c : c + width].bitcast(FP8X4),
                 rhs_scale=b_sc[:, c0 : c0 + width],
                 start=False,
                 stop=True,
@@ -346,29 +341,27 @@ def tile_rankwisemoloradenserouter_d2p_kernel(
         quantize_x(2)
         add_bias(0)
         widen_scalar(4, 1)
-        widen_scalar(5, 0)
+        widen_scalar(5, 0, range(0, BLOCKS // 2))
         quantize_x(3)
         row_max(0)
         widen_vector(4, 0)
         exp_and_sum(0)
+        widen_scalar(5, 0, range(BLOCKS // 2, BLOCKS))
         sort_half(4, 1)
         sort_half(5, 0)
-        widen_scalar(5, 1, range(0, BLOCKS - 1))
         down(2, 3)
         router(2, 4)
         router(3, 4)
         down(3, 0)
-        base_quarter(0, 0, 6)
-        base_quarter(1, 0, 7)
+        base(0, 0, BANK, 6)
+        base(1, 0, BANK, 7)
         add_bias(1)
         normalisers(0)
         row_max(1)
         exp_and_sum(1)
-        widen_scalar(5, 1, range(BLOCKS - 1, BLOCKS))
+        widen_scalar(5, 1)
         sort_half(5, 1)
-        base_quarter(2, 0, 5)
-        for r in range(3):
-            base_quarter(r, 1, None)
+        base(2, 0, BANK, 5)
         gate(0)
         gate(1, (0,))
         normalisers(1)
@@ -472,7 +465,9 @@ def tile_rankwisemoloradenserouter_d2p_kernel(
         store(5, 0, BANK, on_scalar)
         base_and_lora(5, BANK, BANK, 0)
         store(5, BANK, BANK, on_vector)
-        pieces = [(r, c0) for r in (6, 7) for c0 in range(0, F, QUARTER)]
-        for i, ((r, c0), b) in enumerate(zip(pieces, (4, 7, 2, 3, 5, 6, 1, 0))):
+        base_and_lora(6, 0, BANK, 4)
+        store(6, 0, BANK, on_scalar)
+        pieces = [(6, c0) for c0 in range(BANK, F, QUARTER)] + [(7, c0) for c0 in range(0, F, QUARTER)]
+        for i, ((r, c0), b) in enumerate(zip(pieces, (7, 2, 3, 5, 6, 1))):
             base_and_lora(r, c0, QUARTER, b)
-            store(r, c0, QUARTER, on_vector if i % 2 else on_scalar)
+            store(r, c0, QUARTER, on_scalar if i % 2 else on_vector)

@@ -62,9 +62,13 @@ def tile_rankwisemoloradenserouter_d2p_kernel(
         w0_sc = sbuf([P, F], U8, "w0_sc")
         b_sc = sbuf([P, F], U8, "b_sc")
         x_raw = {(r0, r1): sbuf([P, r1 - r0, D], U8, f"x_raw{r0}") for r0, r1 in X_LOADS}
-        wr_codes = sbuf([P, 2, E], I32, "wr_codes")
-        a_codes = sbuf([P, 2, R], I32, "a_codes")
-        w0_codes = sbuf_each(range(2), [P, 2, BANK], I32, "w0_codes")
+        wr_both = sbuf([P, 2, E], I32, "wr_both")
+        a_both = sbuf([P, 2, R], I32, "a_both")
+        w0_first = sbuf_each(range(2), [P, 1, BANK], I32, "w0_first")
+        w0_second = sbuf([P, 2, BANK], I32, "w0_second")
+        wr_codes = [wr_both[:, g] for g in range(2)]
+        a_codes = [a_both[:, g] for g in range(2)]
+        w0_codes = [[w0_first[g][:, 0] for g in range(2)], [w0_second[:, g] for g in range(2)]]
         b_codes = sbuf_each(range(2), [P, 1, BANK], I32, "b_codes")
 
         nc.vector.memset(zeros[:], 0.0)
@@ -98,13 +102,14 @@ def tile_rankwisemoloradenserouter_d2p_kernel(
         load_x(2)
         nc.sync.dma_start(out=br_rows[0:1, :], in_=br.unsqueeze(0))
         load_scales(a_sc, a_scales)
-        load_codes(a_codes[:], a_words, 0, R)
-        load_codes(wr_codes[:], wr_words, 0, E)
+        load_codes(a_both[:], a_words, 0, R)
+        load_codes(wr_both[:], wr_words, 0, E)
         load_scales(wr_sc, wr_scales)
         load_x(3)
-        load_codes(w0_codes[0][:], w0_words, 0, BANK)
+        load_codes(w0_first[0][:], w0_words[0:1], 0, BANK)
         load_scales(w0_sc, w0_scales)
-        load_codes(w0_codes[1][:], w0_words, BANK, BANK)
+        load_codes(w0_first[1][:], w0_words[1:2], 0, BANK)
+        load_codes(w0_second[:], w0_words, BANK, BANK)
         load_codes(b_codes[0][:], b_words, 0, BANK)
         load_scales(b_sc, b_scales)
         load_x(4)
@@ -212,7 +217,7 @@ def tile_rankwisemoloradenserouter_d2p_kernel(
                     out=dest,
                     lhsT=x_codes[r][:, P * g : P * g + P].bitcast(FP8X4),
                     lhsT_scale=x_sc[r][:, P * g : P * g + P],
-                    rhs=codes[:, g, c : c + width].bitcast(FP8X4),
+                    rhs=codes[g][:, c : c + width].bitcast(FP8X4),
                     rhs_scale=plane[4 * g :, c0 : c0 + width],
                     start=(g == 0),
                     stop=(close and g == 1),
@@ -349,19 +354,22 @@ def tile_rankwisemoloradenserouter_d2p_kernel(
         widen_scalar(5, 0, range(BLOCKS // 2, BLOCKS))
         sort_half(4, 1)
         sort_half(5, 0)
+        widen_scalar(5, 1, range(0, 1))
         down(2, 3)
         router(2, 4)
         router(3, 4)
         down(3, 0)
-        base(0, 0, BANK, 6)
-        base(1, 0, BANK, 7)
+        base(0, 0, BANK, 6, (0,))
+        base(1, 0, BANK, 7, (0,))
         add_bias(1)
         normalisers(0)
         row_max(1)
         exp_and_sum(1)
-        widen_scalar(5, 1)
+        widen_scalar(5, 1, range(1, BLOCKS))
         sort_half(5, 1)
-        base(2, 0, BANK, 5)
+        base(2, 0, BANK, 5, (0,))
+        for r in range(3):
+            base(r, 0, BANK, None, (1,))
         gate(0)
         gate(1, (0,))
         normalisers(1)

@@ -255,10 +255,15 @@ def tile_rankwisemoloradenserouter_d2p_kernel(
             base(r, c0, width, b)
             lora(r, c0, width)
 
+        def copy_y(r, c0, width, copy):
+            copy(out=y_out[r][:, c0 : c0 + width], in_=y_ps[r, c0][:])
+
+        def store_y(r, c0, width):
+            nc.sync.dma_start(out=out_view[:, r, c0 : c0 + width], in_=y_out[r][:, c0 : c0 + width])
+
         def store(r, c0, width, copy):
-            cols = slice(c0, c0 + width)
-            copy(out=y_out[r][:, cols], in_=y_ps[r, c0][:])
-            nc.sync.dma_start(out=out_view[:, r, cols], in_=y_out[r][:, cols])
+            copy_y(r, c0, width, copy)
+            store_y(r, c0, width)
 
         def add_bias(h):
             nc.vector.tensor_tensor(
@@ -438,12 +443,13 @@ def tile_rankwisemoloradenserouter_d2p_kernel(
         exp_and_sum(3)
         quantize_z(3)
         gate(5)
-        store(2, 0, BANK, on_scalar)
+        copy_y(2, 0, BANK, on_scalar)
         down(7, 0)
         normalisers(3, slice(0, 1))
         normalisers(3, slice(1, 2))
         lora(3, 0, BANK)
-        store(2, BANK, BANK, on_scalar)
+        copy_y(2, BANK, BANK, on_scalar)
+        store_y(2, 0, F)
         base_and_lora(3, BANK, BANK, 4)
         gate(6)
         gate(7)

@@ -25,12 +25,11 @@ PAIRS = TILES // 2
 PASS = 512
 BANK = 512
 QUARTER = 256
-BLOCKS = PASS // P
+QUAD = 32
+
+FIRST, SECOND = slice(0, 1), slice(1, 2)
 
 X_LOADS = ((0, 1), (1, 2), (2, 4), (4, 6), (6, 8))
-UNSORTED = ((1, 1), (3, 1))
-SORTED_BY_COPY = ((4, 1), (5, 0), (5, 1), (7, 1))
-BY_HALVES = (0, 1)
 
 
 def tile_rankwisemoloradenserouter_d2p_kernel(
@@ -56,28 +55,28 @@ def tile_rankwisemoloradenserouter_d2p_kernel(
         ident = sbuf([P, P], F32, "ident")
         br_rows = sbuf([P, E], BF16, "br_rows")
         br_spread = sbuf([P, E], F32, "br_spread")
-        x_scale_cols = sbuf([P, D // P], F32, "x_scale_cols")
+        quadrant_of = sbuf([P, 4], F32, "quadrant_of")
+        scale_four = sbuf([P, 4], F32, "scale_four")
+        scale_kept = sbuf([P, QUAD, 4], F32, "scale_kept")
+        scale_rows = sbuf([P, QUAD], F32, "scale_rows")
+        scale_cols = sbuf([P, QUAD], F32, "scale_cols")
         wr_sc = sbuf([P, E], U8, "wr_sc")
+        a_sc_in = sbuf([P, R], U8, "a_sc_in")
         a_sc = sbuf([P, R], U8, "a_sc")
         w0_sc = sbuf([P, F], U8, "w0_sc")
         b_sc = sbuf([P, F], U8, "b_sc")
         x_raw = {(r0, r1): sbuf([P, r1 - r0, D], U8, f"x_raw{r0}") for r0, r1 in X_LOADS}
         wr_both = sbuf([P, 2, E], I32, "wr_both")
-        a_both = sbuf([P, 2, R], I32, "a_both")
+        a_in = sbuf([P, 2, R], I32, "a_in")
+        a_codes = sbuf_each(range(2), [P, R], I32, "a_codes")
         w0_first = sbuf_each(range(2), [P, 1, BANK], I32, "w0_first")
         w0_second = sbuf([P, 2, BANK], I32, "w0_second")
         wr_codes = [wr_both[:, g] for g in range(2)]
-        a_codes = [a_both[:, g] for g in range(2)]
         w0_codes = [[w0_first[g][:, 0] for g in range(2)], [w0_second[:, g] for g in range(2)]]
         b_codes = sbuf_each(range(2), [P, 1, BANK], I32, "b_codes")
 
-        nc.vector.memset(zeros[:], 0.0)
-        nc.vector.memset(br_rows[:], 0.0)
-        for plane in (a_sc, wr_sc, w0_sc, b_sc):
-            nc.vector.memset(plane[:].bitcast(I32), 0)
-
-        x_view = x_bytes.rearrange("(p r) k -> p r k", r=TILES)
-        out_view = out.rearrange("(p r) f -> p r f", r=TILES)
+        x_view = x_bytes.rearrange("(r p) k -> p r k", p=P)
+        out_view = out.rearrange("(r p) f -> p r f", p=P)
 
         def load_x(i):
             r0, r1 = X_LOADS[i]
@@ -94,110 +93,114 @@ def tile_rankwisemoloradenserouter_d2p_kernel(
                     in_=scales[:, 4 * quadrant : 4 * quadrant + 4, :].bitcast(I32),
                 )
 
-        make_identity(nc, ident[:])
-        nc.scalar.dma_start(out=x_scale_cols[:], in_=x_scale.unsqueeze(1).to_broadcast([T // P, P // TILES, D // P]))
-        nc.scalar.activation(out=ones[:], in_=zeros[:, :P], func=ACT.Exp)
-        load_x(0)
-        load_x(1)
-        load_x(2)
-        nc.sync.dma_start(out=br_rows[0:1, :], in_=br.unsqueeze(0))
-        load_scales(a_sc, a_scales)
-        load_codes(a_both[:], a_words, 0, R)
-        load_codes(wr_both[:], wr_words, 0, E)
-        load_scales(wr_sc, wr_scales)
-        load_x(3)
-        load_codes(w0_first[0][:], w0_words[0:1], 0, BANK)
-        load_scales(w0_sc, w0_scales)
-        load_codes(w0_first[1][:], w0_words[1:2], 0, BANK)
-        load_codes(w0_second[:], w0_words, BANK, BANK)
-        load_codes(b_codes[0][:], b_words, 0, BANK)
-        load_scales(b_sc, b_scales)
-        load_x(4)
-        load_codes(b_codes[1][:], b_words, BANK, BANK)
+        def load_x_scale():
+            by_half = x_scale.rearrange("r (g q) -> (r g) q", q=4)
+            nc.scalar.dma_start(out=scale_four[:], in_=by_half.unsqueeze(0).to_broadcast([P // 16, 16, 4]))
+
+        def mark_quadrants():
+            nc.vector.tensor_reduce(
+                out=quadrant_of[:], in_=ident[:].rearrange("p (q i) -> p q i", q=4), axis=AX, op=ADD
+            )
+
+        def keep_x_scale():
+            nc.vector.tensor_tensor(
+                out=scale_kept[:],
+                in0=scale_four[:].unsqueeze(1).to_broadcast([P, QUAD, 4]),
+                in1=quadrant_of[:].unsqueeze(1).to_broadcast([P, QUAD, 4]),
+                op=MULT,
+            )
+
+        def spread_x_scale():
+            nc.vector.tensor_reduce(out=scale_rows[:], in_=scale_kept[:], axis=AX, op=ADD)
+
+        def turn_x_scale():
+            nc.vector.transpose(out=scale_cols[:], in_=scale_rows[:])
 
         halves = [(r, g) for r in range(TILES) for g in range(2)]
+        pair_passes = [(h, g) for h in range(PAIRS) for g in range(2)]
         x_wide = sbuf_each(halves, [P, PASS], BF16, "x_wide")
-        x_plain = sbuf_each(SORTED_BY_COPY, [P, PASS], BF16, "x_plain")
-        x_in = sbuf_each(range(len(BY_HALVES), TILES), [P, D], BF16, "x_in")
-        x_in_half = sbuf_each(halves[: 2 * len(BY_HALVES)], [P, PASS], BF16, "x_in_half")
-        x_codes = sbuf_each(range(TILES), [P, 2 * P], U32, "x_codes")
-        x_sc = sbuf_each(range(TILES), [P, 2 * P], U8, "x_sc")
+        x_in = sbuf_each(pair_passes, [P, 2 * PASS], BF16, "x_in")
+        x_codes = sbuf_each(pair_passes, [P, 2 * P], U32, "x_codes")
+        x_sc = sbuf_each(pair_passes, [P, 2 * P], U8, "x_sc")
         logit = sbuf_each(range(PAIRS), [P, 2, E], F32, "logit")
         weight = sbuf_each(range(PAIRS), [P, 2, E], F32, "weight")
-        weight_e = sbuf_each(range(PAIRS), [P, 2, E], F32, "weight_e")
+        gates = sbuf_each(range(TILES), [P, E], F32, "gates")
+        gates_t = sbuf_each(range(PAIRS), [P, 2 * P], F32, "gates_t")
         neg_max = sbuf_each(range(PAIRS), [P, 2], F32, "neg_max")
         total = sbuf_each(range(PAIRS), [P, 2], F32, "total")
         inv_total = sbuf_each(range(PAIRS), [P, 2], F32, "inv_total")
-        z_wide = sbuf_each(range(TILES), [P, R], BF16, "z_wide")
-        z_in = sbuf_each(range(TILES), [P, R], BF16, "z_in")
-        z_codes = sbuf_each(range(TILES), [P, P], U32, "z_codes")
-        z_sc = sbuf_each(range(TILES), [P, P], U8, "z_sc")
+        z_runs = sbuf_each(range(PAIRS), [P, 2, 4 * P], BF16, "z_runs")
+        z_in = sbuf_each(range(PAIRS), [P, 2 * R], BF16, "z_in")
+        z_codes = sbuf_each(range(PAIRS), [P, 2 * P], U32, "z_codes")
+        z_sc = sbuf_each(range(PAIRS), [P, 2 * P], U8, "z_sc")
         y_out = sbuf_each(range(TILES), [P, F], F32, "y_out")
-        xt_ps, zt_ps, l_ps, u_ps, y_ps, br_ps = {}, {}, {}, {}, {}, {}
+        xt_ps, gt_ps, l_ps, u_ps, y_ps, br_ps = {}, {}, {}, {}, {}, {}
         on_scalar, on_vector = nc.scalar.copy, nc.vector.tensor_copy
 
-        def x_block(r, g, j):
+        def tile_cols(r):
+            return slice(P * (r % 2), P * (r % 2) + P)
+
+        def x_half(r, g):
             r0, r1 = [run for run in X_LOADS if run[0] <= r < run[1]][0]
-            c0 = PASS * g + P * j
-            return x_raw[r0, r1][:, r - r0, c0 : c0 + P].bitcast(FP8), x_scale_cols[:, c0 // P : c0 // P + 1]
+            return x_raw[r0, r1][:, r - r0, PASS * g : PASS * g + PASS].bitcast(FP8)
 
         def widen_vector(r, g):
-            runs = x_wide[r, g][:].rearrange("p (s q e) -> p q s e", s=2, e=2)
-            for j in range(BLOCKS):
-                codes, scale = x_block(r, g, j)
-                nc.vector.tensor_scalar(
-                    out=runs[:, 32 * j : 32 * j + 32],
-                    in0=codes.rearrange("p (q s e) -> p q s e", s=2, e=2),
-                    scalar1=scale,
-                    scalar2=None,
-                    op0=MULT,
-                )
-
-        def widen_scalar(r, g, blocks=range(BLOCKS)):
-            dest = x_plain[r, g] if (r, g) in SORTED_BY_COPY else x_wide[r, g]
-            for j in blocks:
-                codes, scale = x_block(r, g, j)
-                nc.scalar.activation(out=dest[:, P * j : P * j + P], in_=codes, func=ACT.Copy, scale=scale)
-
-        def sort_half(r, g):
-            nc.scalar.copy(
-                out=x_wide[r, g][:].bitcast(F32).rearrange("p (s q) -> p s q", s=2),
-                in_=x_plain[r, g][:].bitcast(F32).rearrange("p (q s) -> p s q", s=2),
+            nc.vector.tensor_copy(
+                out=x_wide[r, g][:].rearrange("p (s q e) -> p q s e", s=2, e=2),
+                in_=x_half(r, g).rearrange("p (q s e) -> p q s e", s=2, e=2),
             )
 
-        def transpose_half(r, g, dest):
+        def widen_scalar(r, g):
+            nc.scalar.copy(
+                out=x_wide[r, g][:].rearrange("p (s q e) -> p s q e", s=2, e=2),
+                in_=x_half(r, g).rearrange("p (q s e) -> p s q e", s=2, e=2),
+            )
+
+        def turn_x_half(r, g, dest):
+            xt_ps[r, g] = dest
             words = x_wide[r, g][:].bitcast(F32)
             for s in range(2):
-                run = words[:, s::2] if (r, g) in UNSORTED else words[:, P * s : P * s + P]
-                nc.tensor.transpose(dest[:, s, :], run, ident[:])
+                nc.tensor.transpose(dest[:, s, :], words[:, P * s : P * s + P], ident[:])
 
-        def turn_x_half(r, g, b):
-            xt_ps[r, g] = bank(b, [P, 2, P], f"xt_ps{r}_{g}")
-            transpose_half(r, g, xt_ps[r, g])
+        def turn_x(r, b):
+            dest = bank(b, [P, 2, 2, P], f"xt_ps{r}")
+            for g in range(2):
+                turn_x_half(r, g, dest[:, g])
 
-        def copy_x_half(r, g):
-            nc.scalar.copy(
-                out=x_in_half[r, g][:].bitcast(F32).rearrange("p (n s) -> p n s", s=2),
-                in_=xt_ps[r, g][:].rearrange("p s n -> p n s"),
-            )
+        def scale_views(r, g):
+            dest = x_in[r // 2, g][:, PASS * (r % 2) : PASS * (r % 2) + PASS].rearrange("p (n s e) -> p n s e", s=2, e=2)
+            turned = xt_ps[r, g].bitcast(BF16).rearrange("p s (n e) -> p n s e", e=2)
+            return dest, turned, scale_cols[:, 2 * r + g : 2 * r + g + 1]
+
+        def scale_vector(r, g):
+            dest, turned, scale = scale_views(r, g)
+            nc.vector.tensor_scalar(out=dest, in0=turned, scalar1=scale, scalar2=None, op0=MULT)
+
+        def scale_scalar(r, g):
+            dest, turned, scale = scale_views(r, g)
+            nc.scalar.activation(out=dest, in_=turned, func=ACT.Copy, scale=scale)
 
         def quantize_x_half(r, g):
-            cols = slice(P * g, P * g + P)
-            nc.vector.quantize_mx(out=x_codes[r][:, cols].bitcast(FP8X4), scales=x_sc[r][:, cols], in_=x_in_half[r, g][:])
-
-        def turn_x(r, b, passes=(0, 1)):
-            xt_ps[r] = bank(b, [P, 2, 2, P], f"xt_ps{r}")
-            for g in passes:
-                transpose_half(r, g, xt_ps[r][:, g])
-
-        def copy_x(r, copy):
-            copy(
-                out=x_in[r][:].bitcast(F32).rearrange("p (g n s) -> p g n s", g=2, s=2),
-                in_=xt_ps[r][:].rearrange("p g s n -> p g n s"),
+            h, i = divmod(r, 2)
+            nc.vector.quantize_mx(
+                out=x_codes[h, g][:, tile_cols(r)].bitcast(FP8X4),
+                scales=x_sc[h, g][:, tile_cols(r)],
+                in_=x_in[h, g][:, PASS * i : PASS * i + PASS],
             )
 
-        def quantize_x(r):
-            nc.vector.quantize_mx(out=x_codes[r][:].bitcast(FP8X4), scales=x_sc[r][:], in_=x_in[r][:])
+        def quantize_x(h, g):
+            nc.vector.quantize_mx(out=x_codes[h, g][:].bitcast(FP8X4), scales=x_sc[h, g][:], in_=x_in[h, g][:])
+
+        def order_a_codes(g, copy):
+            copy(
+                out=a_codes[g][:].bitcast(U32).rearrange("p (c e) -> p c e", c=4),
+                in_=a_in[:, g].bitcast(U32).rearrange("p (e c) -> p c e", c=4),
+            )
+
+        def order_a_scales():
+            nc.vector.tensor_copy(
+                out=a_sc[:].rearrange("p (c e) -> p c e", c=4), in_=a_sc_in[:].rearrange("p (e c) -> p c e", c=4)
+            )
 
         def warm_up(count, b):
             scrap = bank(b, [P, BANK], "scrap")
@@ -215,8 +218,8 @@ def tile_rankwisemoloradenserouter_d2p_kernel(
             for g in passes:
                 nc.tensor.matmul_mx(
                     out=dest,
-                    lhsT=x_codes[r][:, P * g : P * g + P].bitcast(FP8X4),
-                    lhsT_scale=x_sc[r][:, P * g : P * g + P],
+                    lhsT=x_codes[r // 2, g][:, tile_cols(r)].bitcast(FP8X4),
+                    lhsT_scale=x_sc[r // 2, g][:, tile_cols(r)],
                     rhs=codes[g][:, c : c + width].bitcast(FP8X4),
                     rhs_scale=plane[4 * g :, c0 : c0 + width],
                     start=(g == 0),
@@ -229,9 +232,20 @@ def tile_rankwisemoloradenserouter_d2p_kernel(
                 l_ps[h] = bank(b, [P, 2, E], f"l_ps{h}")
             x_product(l_ps[h][:, i, :], r, wr_codes, 0, wr_sc, 0, E, True)
 
-        def down(r, b):
-            u_ps[r] = bank(b, [P, R], f"u_ps{r}")
-            x_product(u_ps[r][:], r, a_codes, 0, a_sc, 0, R, True)
+        def down(h, s, b):
+            u_ps[h, s] = bank(b, [P, 2, 2 * P], f"u_ps{h}_{s}")
+            for e in range(2):
+                cols = slice(P * (2 * s + e), P * (2 * s + e) + P)
+                for g in range(2):
+                    nc.tensor.matmul_mx(
+                        out=u_ps[h, s][:, e, :],
+                        lhsT=a_codes[g][:, cols].bitcast(FP8X4),
+                        lhsT_scale=a_sc[4 * g :, cols],
+                        rhs=x_codes[h, g][:].bitcast(FP8X4),
+                        rhs_scale=x_sc[h, g][:],
+                        start=(g == 0),
+                        stop=(g == 1),
+                    )
 
         def base(r, c0, width, b, passes=(0, 1)):
             if 0 in passes:
@@ -243,8 +257,8 @@ def tile_rankwisemoloradenserouter_d2p_kernel(
             f, c = divmod(c0, BANK)
             nc.tensor.matmul_mx(
                 out=y_ps[r, c0][:],
-                lhsT=z_codes[r][:].bitcast(FP8X4),
-                lhsT_scale=z_sc[r][:],
+                lhsT=z_codes[r // 2][:, tile_cols(r)].bitcast(FP8X4),
+                lhsT_scale=z_sc[r // 2][:, tile_cols(r)],
                 rhs=b_codes[f][:, 0, c : c + width].bitcast(FP8X4),
                 rhs_scale=b_sc[:, c0 : c0 + width],
                 start=False,
@@ -265,16 +279,20 @@ def tile_rankwisemoloradenserouter_d2p_kernel(
             copy_y(r, c0, width, copy)
             store_y(r, c0, width)
 
-        def add_bias(h):
+        def add_bias(h, part=slice(0, 2)):
+            count = part.stop - part.start
             nc.vector.tensor_tensor(
-                out=logit[h][:], in0=l_ps[h][:], in1=br_spread[:].unsqueeze(1).to_broadcast([P, 2, E]), op=ADD
+                out=logit[h][:, part],
+                in0=l_ps[h][:, part],
+                in1=br_spread[:].unsqueeze(1).to_broadcast([P, count, E]),
+                op=ADD,
             )
 
-        def row_max(h):
-            nc.vector.tensor_reduce(out=neg_max[h][:], in_=logit[h][:], axis=AX, op=MAX, negate=True)
+        def row_max(h, part=slice(0, 2)):
+            nc.vector.tensor_reduce(out=neg_max[h][:, part], in_=logit[h][:, part], axis=AX, op=MAX, negate=True)
 
-        def exp_and_sum(h):
-            for i in range(2):
+        def exp_and_sum(h, tiles=(0, 1)):
+            for i in tiles:
                 nc.scalar.activation(
                     out=weight[h][:, i, :],
                     in_=logit[h][:, i, :],
@@ -283,205 +301,258 @@ def tile_rankwisemoloradenserouter_d2p_kernel(
                     accum_out=total[h][:, i : i + 1],
                 )
 
-        def normalisers(h, tiles=slice(0, 2)):
-            nc.vector.reciprocal(out=inv_total[h][:, tiles], in_=total[h][:, tiles])
-            nc.vector.tensor_scalar(
-                out=weight_e[h][:, tiles], in0=weight[h][:, tiles], scalar1=float(E), scalar2=None, op0=MULT
-            )
+        def invert_sum(h, part=slice(0, 2)):
+            nc.vector.reciprocal(out=inv_total[h][:, part], in_=total[h][:, part])
 
-        def gate(r, runs=(0, 1)):
+        def normalise(r):
             h, i = divmod(r, 2)
-            for s in runs:
-                nc.vector.scalar_tensor_tensor(
-                    out=z_wide[r][:, 2 * E * s : 2 * E * s + 2 * E].rearrange("p (e c) -> p e c", c=2),
-                    in0=u_ps[r][:].rearrange("p (e s c) -> p s e c", s=2, c=2)[:, s],
-                    scalar=inv_total[h][:, i : i + 1],
-                    in1=weight_e[h][:, i, :].unsqueeze(2).to_broadcast([P, E, 2]),
-                    op0=MULT,
-                    op1=MULT,
-                )
-
-        def turn_z(tiles, b):
-            dest = bank(b, [P, len(tiles), 2, P], f"zt_ps{tiles[0]}")
-            for i, r in enumerate(tiles):
-                zt_ps[r] = dest[:, i]
-                words = z_wide[r][:].bitcast(F32)
-                for s in range(2):
-                    nc.tensor.transpose(zt_ps[r][:, s, :], words[:, P * s : P * s + P], ident[:])
-
-        def copy_z(r):
-            nc.scalar.copy(
-                out=z_in[r][:].bitcast(F32).rearrange("p (n s) -> p n s", s=2),
-                in_=zt_ps[r].rearrange("p s n -> p n s"),
+            nc.vector.tensor_scalar(
+                out=gates[r][:],
+                in0=weight[h][:, i, :],
+                scalar1=inv_total[h][:, i : i + 1],
+                scalar2=float(E),
+                op0=MULT,
+                op1=MULT,
             )
 
-        def quantize_z(r):
-            nc.vector.quantize_mx(out=z_codes[r][:].bitcast(FP8X4), scales=z_sc[r][:], in_=z_in[r][:])
+        def turn_gates(pairs, b):
+            dest = bank(b, [P, len(pairs), 2 * P], f"gt_ps{pairs[0]}")
+            for j, h in enumerate(pairs):
+                gt_ps[h] = dest[:, j]
+                for r in (2 * h, 2 * h + 1):
+                    nc.tensor.transpose(gt_ps[h][:, tile_cols(r)], gates[r][:], ident[:])
 
+        def copy_gates(h):
+            nc.scalar.copy(out=gates_t[h][:], in_=gt_ps[h])
+
+        def gate(h, s, n0=0, n1=2 * P):
+            nc.vector.tensor_tensor(
+                out=z_runs[h][:, s, 2 * n0 : 2 * n1].rearrange("p (n e) -> p n e", e=2),
+                in0=u_ps[h, s][:, :, n0:n1].rearrange("p e n -> p n e"),
+                in1=gates_t[h][:, n0:n1].unsqueeze(2).to_broadcast([P, n1 - n0, 2]),
+                op=MULT,
+            )
+
+        def weave_z(h, copy, n0=0, n1=2 * P):
+            copy(
+                out=z_in[h][:, 4 * n0 : 4 * n1].bitcast(F32).rearrange("p (n s) -> p n s", s=2),
+                in_=z_runs[h][:, :, 2 * n0 : 2 * n1].bitcast(F32).rearrange("p s n -> p n s"),
+            )
+
+        def quantize_z(h, n0=0, n1=2 * P):
+            nc.vector.quantize_mx(
+                out=z_codes[h][:, n0:n1].bitcast(FP8X4), scales=z_sc[h][:, n0:n1], in_=z_in[h][:, 4 * n0 : 4 * n1]
+            )
+
+
+        nc.vector.memset(zeros[:], 0.0)
+        nc.vector.memset(br_rows[:], 0.0)
+        for plane in (wr_sc, w0_sc, a_sc_in, b_sc):
+            nc.vector.memset(plane[:].bitcast(I32), 0)
+        make_identity(nc, ident[:])
+        load_x_scale()
+        nc.scalar.activation(out=ones[:], in_=zeros[:, :P], func=ACT.Exp)
+        load_x(0)
+        load_x(1)
+        load_x(2)
+        nc.sync.dma_start(out=br_rows[0:1, :], in_=br.unsqueeze(0))
+        load_scales(wr_sc, wr_scales)
+        load_codes(wr_both[:], wr_words, 0, E)
+        load_codes(w0_first[0][:], w0_words[0:1], 0, BANK)
+        load_scales(w0_sc, w0_scales)
+        load_codes(w0_first[1][:], w0_words[1:2], 0, BANK)
+        load_x(3)
+        load_scales(a_sc_in, a_scales)
+        load_codes(a_in[:], a_words, 0, R)
+        load_x(4)
+        load_codes(w0_second[:], w0_words, BANK, BANK)
+        load_codes(b_codes[0][:], b_words, 0, BANK)
+        load_scales(b_sc, b_scales)
+        load_codes(b_codes[1][:], b_words, BANK, BANK)
 
         warm_up(4, 7)
+        mark_quadrants()
+        keep_x_scale()
         widen_vector(0, 0)
-        widen_vector(0, 1)
-        widen_scalar(1, 1)
+        spread_x_scale()
+        widen_scalar(0, 1)
         widen_vector(1, 0)
-        for g in range(2):
-            turn_x_half(0, g, g)
-            warm_up(1, 7)
-        turn_x_half(1, 0, 2)
-        turn_x_half(1, 1, 6)
-        widen_scalar(3, 1)
-        for r, g in x_in_half:
-            copy_x_half(r, g)
+        turn_x_scale()
+        widen_scalar(1, 1)
         widen_vector(2, 0)
-        widen_vector(2, 1)
-        widen_vector(3, 0)
-        for r, g in x_in_half:
-            quantize_x_half(r, g)
+        widen_scalar(2, 1)
+        widen_scalar(3, 0)
+        widen_scalar(3, 1)
+        turn_x_half(0, 0, bank(0, [P, 2, P], "xt_a"))
+        turn_x_half(0, 1, bank(1, [P, 2, P], "xt_b"))
+        turn_x(1, 2)
         spread_bias(4)
+        warm_up(1, 7)
         turn_x(2, 3)
-        turn_x(3, 0, (1, 0))
-
-        down(0, 1)
-        router(0, 5)
-        router(1, 5)
+        turn_x_half(3, 0, bank(5, [P, 2, P], "xt_c"))
+        turn_x_half(3, 1, bank(6, [P, 2, P], "xt_d"))
+        warm_up(1, 7)
+        scale_vector(0, 0)
+        scale_vector(0, 1)
+        quantize_x_half(0, 0)
+        scale_vector(1, 0)
+        quantize_x_half(0, 1)
+        scale_vector(1, 1)
+        quantize_x_half(1, 0)
+        scale_vector(2, 0)
+        quantize_x_half(1, 1)
         copy_bias()
-        copy_x(2, on_scalar)
-        copy_x(3, on_vector)
-        down(1, 2)
-        quantize_x(2)
-        add_bias(0)
+        scale_scalar(3, 0)
+        scale_scalar(3, 1)
+        router(0, 0)
+        base(0, 0, BANK, 7, (0,))
+        base(1, 0, BANK, 1, (0,))
+        add_bias(0, FIRST)
+        scale_vector(2, 1)
+        base(0, 0, BANK, 7, (1,))
+        router(1, 0)
+        quantize_x_half(2, 0)
+        row_max(0, FIRST)
+        quantize_x_half(2, 1)
+        add_bias(0, SECOND)
+        quantize_x_half(3, 0)
+        quantize_x_half(3, 1)
+        row_max(0, SECOND)
+        widen_scalar(4, 0)
+        exp_and_sum(0, (0,))
         widen_scalar(4, 1)
-        widen_scalar(5, 0, range(0, BLOCKS // 2))
-        quantize_x(3)
-        row_max(0)
-        widen_vector(4, 0)
-        exp_and_sum(0)
-        widen_scalar(5, 0, range(BLOCKS // 2, BLOCKS))
-        sort_half(4, 1)
-        sort_half(5, 0)
-        widen_scalar(5, 1, range(0, 1))
-        down(2, 3)
+        widen_scalar(5, 0)
+        exp_and_sum(0, (1,))
+        widen_scalar(5, 1)
+        base(1, 0, BANK, 1, (1,))
+        base(2, 0, BANK, 2)
         router(2, 4)
         router(3, 4)
-        down(3, 0)
-        base(0, 0, BANK, 6, (0,))
-        base(1, 0, BANK, 7, (0,))
+        invert_sum(0, FIRST)
+        order_a_scales()
+        normalise(0)
+        invert_sum(0, SECOND)
+        order_a_codes(0, on_vector)
+        normalise(1)
         add_bias(1)
-        normalisers(0)
-        row_max(1)
-        exp_and_sum(1)
-        widen_scalar(5, 1, range(1, BLOCKS))
-        sort_half(5, 1)
-        base(2, 0, BANK, 5, (0,))
-        for r in range(3):
-            base(r, 0, BANK, None, (1,))
-        gate(0)
-        gate(1, (0,))
-        normalisers(1)
-        gate(1, (1,))
+        order_a_codes(1, on_scalar)
 
-        turn_x(4, 4)
-        turn_x(5, 1, (0,))
-        turn_z((0, 1), 2)
-        transpose_half(5, 1, xt_ps[5][:, 1])
-        gate(2)
-        gate(3)
-        copy_x(4, on_scalar)
-        copy_z(0)
-        copy_z(1)
-        copy_x(5, on_scalar)
-        widen_scalar(7, 1)
-        sort_half(7, 1)
-        quantize_x(4)
+        turn_x(4, 3)
+        turn_x(5, 5)
+        turn_gates((0,), 0)
+        scale_vector(4, 0)
+        scale_vector(4, 1)
+        row_max(1)
+        copy_gates(0)
+        exp_and_sum(1)
+        scale_vector(5, 0)
+        scale_vector(5, 1)
+        down(0, 0, 6)
+        down(0, 1, 4)
+        for r in (6, 7):
+            for g in range(2):
+                widen_scalar(r, g)
+        gate(0, 0)
+        invert_sum(1)
+        gate(0, 1, 0, P)
+        normalise(2)
+        normalise(3)
+        gate(0, 1, P, 2 * P)
+        weave_z(0, on_scalar, 0, P)
+        weave_z(0, on_scalar, P, 2 * P)
         base(0, BANK, BANK, 3)
-        base(1, BANK, BANK, 0)
-        router(4, 4)
-        down(4, 2)
-        quantize_z(0)
-        widen_vector(6, 0)
-        quantize_z(1)
-        quantize_x(5)
+        base(1, BANK, BANK, 5)
+        quantize_x(2, 0)
+        quantize_z(0, 0, P)
+        quantize_x(2, 1)
+        quantize_z(0, P, 2 * P)
+
+        turn_x(6, 6)
+        turn_x(7, 4)
+        turn_gates((1,), 0)
+        copy_gates(1)
+        scale_vector(6, 0)
+        scale_vector(6, 1)
+        scale_vector(7, 0)
+        scale_vector(7, 1)
         lora(0, 0, BANK)
         lora(0, BANK, BANK)
-        router(5, 4)
         lora(1, 0, BANK)
         lora(1, BANK, BANK)
-        widen_vector(6, 1)
-        widen_vector(7, 0)
         store(0, 0, BANK, on_scalar)
-        store(0, BANK, BANK, on_vector)
-        store(1, 0, BANK, on_scalar)
+        quantize_x(3, 0)
+        quantize_x(3, 1)
+        router(4, 0)
+        router(5, 0)
+        down(1, 0, 6)
+        store(0, BANK, BANK, on_scalar)
         add_bias(2)
-
-        turn_x(6, 1)
-        turn_x(7, 6)
-        turn_z((2, 3), 3)
+        router(6, 7)
+        router(7, 7)
+        down(1, 1, 4)
+        gate(1, 0, 0, P)
         row_max(2)
-        copy_x(6, on_scalar)
-        copy_x(7, on_vector)
-        down(5, 7)
-        exp_and_sum(2)
-        copy_z(2)
-        copy_z(3)
-        quantize_x(6)
-        quantize_x(7)
-        base(3, 0, BANK, 1)
-        router(6, 4)
-        base(2, BANK, BANK, 6, (0,))
-        router(7, 4)
-        normalisers(2)
-        quantize_z(2)
-        gate(4, (0,))
-        store(1, BANK, BANK, on_scalar)
-        base(2, BANK, BANK, 6, (1,))
         add_bias(3)
-        gate(4, (1,))
+        store(1, 0, BANK, on_scalar)
+        gate(1, 0, P, 2 * P)
         row_max(3)
+        exp_and_sum(2)
+        base(2, BANK, BANK, 3)
+        base(3, 0, BANK, 1)
+        invert_sum(2)
+        gate(1, 1, 0, P)
+        exp_and_sum(3)
+        normalise(4)
+        normalise(5)
+        gate(1, 1, P, 2 * P)
+        invert_sum(3)
+        weave_z(1, on_scalar, 0, P)
+        weave_z(1, on_scalar, P, 2 * P)
+        base(3, BANK, BANK, 0)
+        down(2, 0, 6)
+        down(2, 1, 4)
+        quantize_z(1, 0, P)
+        normalise(6)
+        normalise(7)
+        quantize_z(1, P, 2 * P)
+        store(1, BANK, BANK, on_scalar)
+
+        turn_gates((2, 3), 7)
+        copy_gates(2)
+        copy_gates(3)
         lora(2, 0, BANK)
         lora(2, BANK, BANK)
-        down(6, 3)
-        exp_and_sum(3)
-        quantize_z(3)
-        gate(5)
-        copy_y(2, 0, BANK, on_scalar)
-        down(7, 0)
-        normalisers(3, slice(0, 1))
-        normalisers(3, slice(1, 2))
         lora(3, 0, BANK)
-        copy_y(2, BANK, BANK, on_scalar)
+        lora(3, BANK, BANK)
+        gate(2, 0)
+        gate(2, 1, 0, P)
+        copy_y(2, 0, BANK, on_scalar)
+        gate(2, 1, P, 2 * P)
+        weave_z(2, on_scalar, 0, P)
+        weave_z(2, on_scalar, P, 2 * P)
+        copy_y(2, BANK, BANK, on_vector)
         store_y(2, 0, F)
-        base_and_lora(3, BANK, BANK, 4)
-        gate(6)
-        gate(7)
+        down(3, 0, 5)
+        down(3, 1, 7)
+        quantize_z(2, 0, P)
         store(3, 0, BANK, on_scalar)
-        base(4, 0, BANK, 5)
-
-        turn_z((4,), 7)
-        turn_z((5,), 2)
-        turn_z((6, 7), 3)
-        store(3, BANK, BANK, on_vector)
-        copy_z(4)
-        copy_z(5)
-        base(4, BANK, BANK, 6)
-        base(5, 0, BANK, 1, (0,))
-        quantize_z(4)
-        copy_z(6)
-        quantize_z(5)
-        copy_z(7)
-        lora(4, 0, BANK)
-        lora(4, BANK, BANK)
-        base(5, 0, BANK, 1, (1,))
-        lora(5, 0, BANK)
-        quantize_z(6)
-        quantize_z(7)
+        quantize_z(2, P, 2 * P)
+        store(3, BANK, BANK, on_scalar)
+        gate(3, 0)
+        gate(3, 1)
+        base_and_lora(4, 0, BANK, 2)
+        base_and_lora(4, BANK, BANK, 3)
         store(4, 0, BANK, on_scalar)
+        weave_z(3, on_scalar)
         store(4, BANK, BANK, on_vector)
+        quantize_z(3)
+        base_and_lora(5, 0, BANK, 6)
         store(5, 0, BANK, on_scalar)
-        base_and_lora(5, BANK, BANK, 0)
+        base_and_lora(5, BANK, BANK, 4)
         store(5, BANK, BANK, on_vector)
-        base_and_lora(6, 0, BANK, 4)
+        base_and_lora(6, 0, BANK, 1)
         store(6, 0, BANK, on_scalar)
         pieces = [(6, c0) for c0 in range(BANK, F, QUARTER)] + [(7, c0) for c0 in range(0, F, QUARTER)]
-        for i, ((r, c0), b) in enumerate(zip(pieces, (7, 2, 3, 5, 6, 1))):
+        for i, ((r, c0), b) in enumerate(zip(pieces, (0, 5, 2, 7, 3, 6))):
             base_and_lora(r, c0, QUARTER, b)
             store(r, c0, QUARTER, on_scalar if i % 2 else on_vector)

@@ -55,9 +55,7 @@ def tile_rankwisemoloradenserouter_d2p_kernel(
         ident = sbuf([P, P], F32, "ident")
         br_rows = sbuf([P, E], BF16, "br_rows")
         br_spread = sbuf([P, E], F32, "br_spread")
-        quadrant_of = sbuf([P, 4], F32, "quadrant_of")
-        scale_four = sbuf([P, 4], F32, "scale_four")
-        scale_kept = sbuf([P, QUAD, 4], F32, "scale_kept")
+        scale_one = sbuf([P, 1], F32, "scale_one")
         scale_rows = sbuf([P, QUAD], F32, "scale_rows")
         scale_cols = sbuf([P, QUAD], F32, "scale_cols")
         wr_sc = sbuf([P, E], U8, "wr_sc")
@@ -94,24 +92,11 @@ def tile_rankwisemoloradenserouter_d2p_kernel(
                 )
 
         def load_x_scale():
-            by_half = x_scale.rearrange("r (g q) -> (r g) q", q=4)
-            nc.scalar.dma_start(out=scale_four[:], in_=by_half.unsqueeze(0).to_broadcast([P // 16, 16, 4]))
-
-        def mark_quadrants():
-            nc.vector.tensor_reduce(
-                out=quadrant_of[:], in_=ident[:].rearrange("p (q i) -> p q i", q=4), axis=AX, op=ADD
-            )
-
-        def keep_x_scale():
-            nc.vector.tensor_tensor(
-                out=scale_kept[:],
-                in0=scale_four[:].unsqueeze(1).to_broadcast([P, QUAD, 4]),
-                in1=quadrant_of[:].unsqueeze(1).to_broadcast([P, QUAD, 4]),
-                op=MULT,
-            )
+            by_quadrant = x_scale.rearrange("r (g q) -> q (r g)", q=4)
+            nc.scalar.dma_start(out=scale_one[0:P:2, :], in_=by_quadrant.unsqueeze(2))
 
         def spread_x_scale():
-            nc.vector.tensor_reduce(out=scale_rows[:], in_=scale_kept[:], axis=AX, op=ADD)
+            nc.vector.tensor_copy(out=scale_rows[:], in_=scale_one[:].to_broadcast([P, QUAD]))
 
         def turn_x_scale():
             nc.vector.transpose(out=scale_cols[:], in_=scale_rows[:])
@@ -125,11 +110,10 @@ def tile_rankwisemoloradenserouter_d2p_kernel(
         logit = sbuf_each(range(PAIRS), [P, 2, E], F32, "logit")
         weight = sbuf_each(range(PAIRS), [P, 2, E], F32, "weight")
         gates = sbuf_each(range(TILES), [P, E], F32, "gates")
-        gates_t = sbuf_each(range(PAIRS), [P, 2 * P], F32, "gates_t")
+        u_runs = sbuf_each(range(PAIRS), [P, 2, 4 * P], F32, "u_runs")
         neg_max = sbuf_each(range(PAIRS), [P, 2], F32, "neg_max")
         total = sbuf_each(range(PAIRS), [P, 2], F32, "total")
         inv_total = sbuf_each(range(PAIRS), [P, 2], F32, "inv_total")
-        z_runs = sbuf_each(range(PAIRS), [P, 2, 4 * P], BF16, "z_runs")
         z_in = sbuf_each(range(PAIRS), [P, 2 * R], BF16, "z_in")
         z_codes = sbuf_each(range(PAIRS), [P, 2 * P], U32, "z_codes")
         z_sc = sbuf_each(range(PAIRS), [P, 2 * P], U8, "z_sc")
@@ -156,7 +140,7 @@ def tile_rankwisemoloradenserouter_d2p_kernel(
                 in_=x_half(r, g).rearrange("p (q s e) -> p s q e", s=2, e=2),
             )
 
-        def turn_x_half(r, g, dest):
+        def turn_x_into(r, g, dest):
             xt_ps[r, g] = dest
             words = x_wide[r, g][:].bitcast(F32)
             for s in range(2):
@@ -165,12 +149,15 @@ def tile_rankwisemoloradenserouter_d2p_kernel(
         def turn_x(r, b):
             dest = bank(b, [P, 2, 2, P], f"xt_ps{r}")
             for g in range(2):
-                turn_x_half(r, g, dest[:, g])
+                turn_x_into(r, g, dest[:, g])
+
+        def turn_x_half(r, g, b):
+            turn_x_into(r, g, bank(b, [P, 2, P], f"xt_ps{r}_{g}")[:])
 
         def scale_views(r, g):
             dest = x_in[r // 2, g][:, PASS * (r % 2) : PASS * (r % 2) + PASS].rearrange("p (n s e) -> p n s e", s=2, e=2)
             turned = xt_ps[r, g].bitcast(BF16).rearrange("p s (n e) -> p n s e", e=2)
-            return dest, turned, scale_cols[:, 2 * r + g : 2 * r + g + 1]
+            return dest, turned, scale_cols[:, 4 * r + 2 * g : 4 * r + 2 * g + 1]
 
         def scale_vector(r, g):
             dest, turned, scale = scale_views(r, g)
@@ -226,11 +213,13 @@ def tile_rankwisemoloradenserouter_d2p_kernel(
                     stop=(close and g == 1),
                 )
 
-        def router(r, b):
-            h, i = divmod(r, 2)
-            if i == 0:
-                l_ps[h] = bank(b, [P, 2, E], f"l_ps{h}")
-            x_product(l_ps[h][:, i, :], r, wr_codes, 0, wr_sc, 0, E, True)
+        def open_logits(pairs, b):
+            dest = bank(b, [P, len(pairs), 2, E], f"l_ps{pairs[0]}")
+            for j, h in enumerate(pairs):
+                l_ps[h] = dest[:, j]
+
+        def router(r):
+            x_product(l_ps[r // 2][:, r % 2, :], r, wr_codes, 0, wr_sc, 0, E, True)
 
         def down(h, s, b):
             u_ps[h, s] = bank(b, [P, 2, 2 * P], f"u_ps{h}_{s}")
@@ -279,13 +268,9 @@ def tile_rankwisemoloradenserouter_d2p_kernel(
             copy_y(r, c0, width, copy)
             store_y(r, c0, width)
 
-        def add_bias(h, part=slice(0, 2)):
-            count = part.stop - part.start
+        def add_bias(h):
             nc.vector.tensor_tensor(
-                out=logit[h][:, part],
-                in0=l_ps[h][:, part],
-                in1=br_spread[:].unsqueeze(1).to_broadcast([P, count, E]),
-                op=ADD,
+                out=logit[h][:], in0=l_ps[h], in1=br_spread[:].unsqueeze(1).to_broadcast([P, 2, E]), op=ADD
             )
 
         def row_max(h, part=slice(0, 2)):
@@ -315,55 +300,57 @@ def tile_rankwisemoloradenserouter_d2p_kernel(
                 op1=MULT,
             )
 
-        def turn_gates(pairs, b):
-            dest = bank(b, [P, len(pairs), 2 * P], f"gt_ps{pairs[0]}")
-            for j, h in enumerate(pairs):
-                gt_ps[h] = dest[:, j]
-                for r in (2 * h, 2 * h + 1):
-                    nc.tensor.transpose(gt_ps[h][:, tile_cols(r)], gates[r][:], ident[:])
+        def turn_gates(tiles, b):
+            dest = bank(b, [P, len(tiles), P], f"gt_ps{tiles[0]}")
+            for j, r in enumerate(tiles):
+                gt_ps[r] = dest[:, j]
+                nc.tensor.transpose(gt_ps[r], gates[r][:], ident[:])
 
-        def copy_gates(h):
-            nc.scalar.copy(out=gates_t[h][:], in_=gt_ps[h])
+        def copy_u(h, s, copy):
+            copy(
+                out=u_runs[h][:, s].rearrange("p (n e) -> p n e", e=2),
+                in_=u_ps[h, s][:].rearrange("p e n -> p n e"),
+            )
 
-        def gate(h, s, n0=0, n1=2 * P):
+        def gate(r):
+            h, i = divmod(r, 2)
             nc.vector.tensor_tensor(
-                out=z_runs[h][:, s, 2 * n0 : 2 * n1].rearrange("p (n e) -> p n e", e=2),
-                in0=u_ps[h, s][:, :, n0:n1].rearrange("p e n -> p n e"),
-                in1=gates_t[h][:, n0:n1].unsqueeze(2).to_broadcast([P, n1 - n0, 2]),
+                out=z_in[h][:, R * i : R * i + R].rearrange("p (n s e) -> p n s e", s=2, e=2),
+                in0=gt_ps[r].unsqueeze(2).unsqueeze(3).to_broadcast([P, P, 2, 2]),
+                in1=u_runs[h][:, :, 2 * P * i : 2 * P * i + 2 * P].rearrange("p s (n e) -> p n s e", e=2),
                 op=MULT,
             )
 
-        def weave_z(h, copy, n0=0, n1=2 * P):
-            copy(
-                out=z_in[h][:, 4 * n0 : 4 * n1].bitcast(F32).rearrange("p (n s) -> p n s", s=2),
-                in_=z_runs[h][:, :, 2 * n0 : 2 * n1].bitcast(F32).rearrange("p s n -> p n s"),
-            )
-
-        def quantize_z(h, n0=0, n1=2 * P):
+        def quantize_z(r):
+            h, i = divmod(r, 2)
             nc.vector.quantize_mx(
-                out=z_codes[h][:, n0:n1].bitcast(FP8X4), scales=z_sc[h][:, n0:n1], in_=z_in[h][:, 4 * n0 : 4 * n1]
+                out=z_codes[h][:, tile_cols(r)].bitcast(FP8X4),
+                scales=z_sc[h][:, tile_cols(r)],
+                in_=z_in[h][:, R * i : R * i + R],
             )
 
 
+        nc.gpsimd.memset(scale_one[:], 0.0)
         nc.vector.memset(zeros[:], 0.0)
-        nc.vector.memset(br_rows[:], 0.0)
-        for plane in (wr_sc, w0_sc, a_sc_in, b_sc):
+        for plane in (w0_sc, wr_sc, a_sc_in):
             nc.vector.memset(plane[:].bitcast(I32), 0)
+        nc.vector.memset(br_rows[:], 0.0)
+        nc.vector.memset(b_sc[:].bitcast(I32), 0)
         make_identity(nc, ident[:])
         load_x_scale()
         nc.scalar.activation(out=ones[:], in_=zeros[:, :P], func=ACT.Exp)
         load_x(0)
         load_x(1)
         load_x(2)
-        nc.sync.dma_start(out=br_rows[0:1, :], in_=br.unsqueeze(0))
-        load_scales(wr_sc, wr_scales)
-        load_codes(wr_both[:], wr_words, 0, E)
         load_codes(w0_first[0][:], w0_words[0:1], 0, BANK)
         load_scales(w0_sc, w0_scales)
         load_codes(w0_first[1][:], w0_words[1:2], 0, BANK)
-        load_x(3)
-        load_scales(a_sc_in, a_scales)
+        nc.sync.dma_start(out=br_rows[0:1, :], in_=br.unsqueeze(0))
+        load_codes(wr_both[:], wr_words, 0, E)
+        load_scales(wr_sc, wr_scales)
         load_codes(a_in[:], a_words, 0, R)
+        load_scales(a_sc_in, a_scales)
+        load_x(3)
         load_x(4)
         load_codes(w0_second[:], w0_words, BANK, BANK)
         load_codes(b_codes[0][:], b_words, 0, BANK)
@@ -371,8 +358,6 @@ def tile_rankwisemoloradenserouter_d2p_kernel(
         load_codes(b_codes[1][:], b_words, BANK, BANK)
 
         warm_up(4, 7)
-        mark_quadrants()
-        keep_x_scale()
         widen_vector(0, 0)
         spread_x_scale()
         widen_scalar(0, 1)
@@ -383,176 +368,166 @@ def tile_rankwisemoloradenserouter_d2p_kernel(
         widen_scalar(2, 1)
         widen_scalar(3, 0)
         widen_scalar(3, 1)
-        turn_x_half(0, 0, bank(0, [P, 2, P], "xt_a"))
-        turn_x_half(0, 1, bank(1, [P, 2, P], "xt_b"))
-        turn_x(1, 2)
-        spread_bias(4)
+        turn_x(0, 0)
+        turn_x_half(1, 0, 1)
+        turn_x_half(1, 1, 2)
         warm_up(1, 7)
-        turn_x(2, 3)
-        turn_x_half(3, 0, bank(5, [P, 2, P], "xt_c"))
-        turn_x_half(3, 1, bank(6, [P, 2, P], "xt_d"))
-        warm_up(1, 7)
+        for r in (2, 3):
+            for g in range(2):
+                turn_x_half(r, g, 2 * r + g - 1)
         scale_vector(0, 0)
         scale_vector(0, 1)
         quantize_x_half(0, 0)
         scale_vector(1, 0)
         quantize_x_half(0, 1)
-        scale_vector(1, 1)
-        quantize_x_half(1, 0)
         scale_vector(2, 0)
+        quantize_x_half(1, 0)
+        scale_vector(3, 0)
+        for r in (1, 2, 3):
+            scale_scalar(r, 1)
         quantize_x_half(1, 1)
-        copy_bias()
-        scale_scalar(3, 0)
-        scale_scalar(3, 1)
-        router(0, 0)
-        base(0, 0, BANK, 7, (0,))
-        base(1, 0, BANK, 1, (0,))
-        add_bias(0, FIRST)
-        scale_vector(2, 1)
-        base(0, 0, BANK, 7, (1,))
-        router(1, 0)
         quantize_x_half(2, 0)
-        row_max(0, FIRST)
         quantize_x_half(2, 1)
-        add_bias(0, SECOND)
         quantize_x_half(3, 0)
         quantize_x_half(3, 1)
-        row_max(0, SECOND)
-        widen_scalar(4, 0)
-        exp_and_sum(0, (0,))
+        base(0, 0, BANK, 7)
+        spread_bias(0)
+        base(1, 0, BANK, 1, (0,))
+        open_logits((0,), 5)
+        router(0)
+        base(1, 0, BANK, 1, (1,))
+        router(1)
+        base(2, 0, BANK, 2)
+        open_logits((1,), 4)
+        router(2)
+        router(3)
+        copy_bias()
+        order_a_codes(0, on_vector)
+        order_a_scales()
+        add_bias(0)
+        order_a_codes(1, on_scalar)
         widen_scalar(4, 1)
         widen_scalar(5, 0)
-        exp_and_sum(0, (1,))
         widen_scalar(5, 1)
-        base(1, 0, BANK, 1, (1,))
-        base(2, 0, BANK, 2)
-        router(2, 4)
-        router(3, 4)
-        invert_sum(0, FIRST)
-        order_a_scales()
-        normalise(0)
-        invert_sum(0, SECOND)
-        order_a_codes(0, on_vector)
-        normalise(1)
+        widen_scalar(7, 0)
+        widen_vector(4, 0)
+        row_max(0)
         add_bias(1)
-        order_a_codes(1, on_scalar)
-
-        turn_x(4, 3)
-        turn_x(5, 5)
-        turn_gates((0,), 0)
-        scale_vector(4, 0)
-        scale_vector(4, 1)
+        widen_vector(6, 0)
         row_max(1)
-        copy_gates(0)
+        exp_and_sum(0)
+        down(0, 0, 3)
+        down(0, 1, 0)
+        down(1, 0, 6)
+        down(1, 1, 5)
+        copy_u(0, 0, on_scalar)
+        widen_vector(6, 1)
+        invert_sum(0)
+        widen_vector(7, 1)
         exp_and_sum(1)
-        scale_vector(5, 0)
-        scale_vector(5, 1)
-        down(0, 0, 6)
-        down(0, 1, 4)
-        for r in (6, 7):
-            for g in range(2):
-                widen_scalar(r, g)
-        gate(0, 0)
+        normalise(0)
+        normalise(1)
+        copy_u(1, 0, on_vector)
+        copy_u(0, 1, on_scalar)
         invert_sum(1)
-        gate(0, 1, 0, P)
+        copy_u(1, 1, on_scalar)
+
+        turn_x(4, 4)
+        scale_vector(4, 0)
         normalise(2)
         normalise(3)
-        gate(0, 1, P, 2 * P)
-        weave_z(0, on_scalar, 0, P)
-        weave_z(0, on_scalar, P, 2 * P)
-        base(0, BANK, BANK, 3)
-        base(1, BANK, BANK, 5)
+        turn_x(5, 3)
+        turn_x(6, 0)
+        turn_x(7, 6)
+        turn_gates((0, 1, 2, 3), 5)
+        scale_vector(4, 1)
+        scale_vector(5, 0)
+        scale_vector(5, 1)
+        scale_scalar(6, 0)
+        scale_scalar(6, 1)
+        scale_scalar(7, 0)
+        scale_scalar(7, 1)
+        gate(0)
         quantize_x(2, 0)
-        quantize_z(0, 0, P)
+        quantize_z(0)
+        gate(1)
         quantize_x(2, 1)
-        quantize_z(0, P, 2 * P)
-
-        turn_x(6, 6)
-        turn_x(7, 4)
-        turn_gates((1,), 0)
-        copy_gates(1)
-        scale_vector(6, 0)
-        scale_vector(6, 1)
-        scale_vector(7, 0)
-        scale_vector(7, 1)
-        lora(0, 0, BANK)
-        lora(0, BANK, BANK)
-        lora(1, 0, BANK)
-        lora(1, BANK, BANK)
-        store(0, 0, BANK, on_scalar)
+        quantize_z(1)
         quantize_x(3, 0)
         quantize_x(3, 1)
-        router(4, 0)
-        router(5, 0)
-        down(1, 0, 6)
+        base(0, BANK, BANK, 4)
+        base(1, BANK, BANK, 3)
+        base(2, BANK, BANK, 0)
+        lora(0, 0, BANK)
+        lora(0, BANK, BANK)
+        base(3, 0, BANK, 6)
+        lora(1, 0, BANK)
+        lora(1, BANK, BANK)
+        gate(2)
+        gate(3)
+        quantize_z(2)
+        store(0, 0, BANK, on_scalar)
         store(0, BANK, BANK, on_scalar)
-        add_bias(2)
-        router(6, 7)
-        router(7, 7)
-        down(1, 1, 4)
-        gate(1, 0, 0, P)
-        row_max(2)
-        add_bias(3)
         store(1, 0, BANK, on_scalar)
-        gate(1, 0, P, 2 * P)
+        open_logits((2, 3), 7)
+        for r in range(4, TILES):
+            router(r)
+        add_bias(2)
+        quantize_z(3)
+        add_bias(3)
+        row_max(2)
         row_max(3)
-        exp_and_sum(2)
-        base(2, BANK, BANK, 3)
-        base(3, 0, BANK, 1)
-        invert_sum(2)
-        gate(1, 1, 0, P)
-        exp_and_sum(3)
-        normalise(4)
-        normalise(5)
-        gate(1, 1, P, 2 * P)
-        invert_sum(3)
-        weave_z(1, on_scalar, 0, P)
-        weave_z(1, on_scalar, P, 2 * P)
-        base(3, BANK, BANK, 0)
-        down(2, 0, 6)
-        down(2, 1, 4)
-        quantize_z(1, 0, P)
-        normalise(6)
-        normalise(7)
-        quantize_z(1, P, 2 * P)
         store(1, BANK, BANK, on_scalar)
-
-        turn_gates((2, 3), 7)
-        copy_gates(2)
-        copy_gates(3)
+        down(2, 0, 4)
+        down(2, 1, 1)
+        copy_u(2, 0, on_scalar)
+        exp_and_sum(2)
         lora(2, 0, BANK)
         lora(2, BANK, BANK)
         lora(3, 0, BANK)
-        lora(3, BANK, BANK)
-        gate(2, 0)
-        gate(2, 1, 0, P)
-        copy_y(2, 0, BANK, on_scalar)
-        gate(2, 1, P, 2 * P)
-        weave_z(2, on_scalar, 0, P)
-        weave_z(2, on_scalar, P, 2 * P)
-        copy_y(2, BANK, BANK, on_vector)
-        store_y(2, 0, F)
-        down(3, 0, 5)
+        exp_and_sum(3)
+        copy_y(2, 0, BANK, on_vector)
+        invert_sum(2)
+        invert_sum(3)
+        normalise(4)
+        normalise(5)
+        normalise(6)
+        normalise(7)
+        copy_u(2, 1, on_scalar)
+        down(3, 0, 3)
         down(3, 1, 7)
-        quantize_z(2, 0, P)
-        store(3, 0, BANK, on_scalar)
-        quantize_z(2, P, 2 * P)
+        copy_y(2, BANK, BANK, on_scalar)
+        store_y(2, 0, F)
+        store(3, 0, BANK, on_vector)
+        base(3, BANK, BANK, 2)
+
+        turn_gates((4, 5, 6, 7), 5)
+        gate(4)
+        copy_u(3, 0, on_scalar)
+        copy_u(3, 1, on_scalar)
+        gate(5)
+        quantize_z(4)
+        lora(3, BANK, BANK)
+        base(4, 0, BANK, 4)
+        base(4, BANK, BANK, 1)
+        base(5, 0, BANK, 0)
+        lora(4, 0, BANK)
+        lora(4, BANK, BANK)
+        gate(6)
+        quantize_z(5)
         store(3, BANK, BANK, on_scalar)
-        gate(3, 0)
-        gate(3, 1)
-        base_and_lora(4, 0, BANK, 2)
-        base_and_lora(4, BANK, BANK, 3)
+        gate(7)
+        quantize_z(6)
         store(4, 0, BANK, on_scalar)
-        weave_z(3, on_scalar)
+        quantize_z(7)
         store(4, BANK, BANK, on_vector)
-        quantize_z(3)
-        base_and_lora(5, 0, BANK, 6)
+        lora(5, 0, BANK)
         store(5, 0, BANK, on_scalar)
-        base_and_lora(5, BANK, BANK, 4)
+        base_and_lora(5, BANK, BANK, 6)
         store(5, BANK, BANK, on_vector)
-        base_and_lora(6, 0, BANK, 1)
+        base_and_lora(6, 0, BANK, 3)
         store(6, 0, BANK, on_scalar)
         pieces = [(6, c0) for c0 in range(BANK, F, QUARTER)] + [(7, c0) for c0 in range(0, F, QUARTER)]
-        for i, ((r, c0), b) in enumerate(zip(pieces, (0, 5, 2, 7, 3, 6))):
+        for i, ((r, c0), b) in enumerate(zip(pieces, (7, 2, 5, 4, 1, 0))):
             base_and_lora(r, c0, QUARTER, b)
             store(r, c0, QUARTER, on_scalar if i % 2 else on_vector)

@@ -25,11 +25,14 @@ PAIRS = TILES // 2
 PASS = 512
 BANK = 512
 QUARTER = 256
+EARLY = TILES // 2
 QUAD = 32
+BLOCKS = PASS // P
 
 FIRST, SECOND = slice(0, 1), slice(1, 2)
 
 X_LOADS = ((0, 1), (1, 2), (2, 4), (4, 6), (6, 8))
+UNSORTED = ((1, 1), (3, 1))
 
 
 def tile_rankwisemoloradenserouter_d2p_kernel(
@@ -55,6 +58,7 @@ def tile_rankwisemoloradenserouter_d2p_kernel(
         ident = sbuf([P, P], F32, "ident")
         br_rows = sbuf([P, E], BF16, "br_rows")
         br_spread = sbuf([P, E], F32, "br_spread")
+        x_scale_cols = sbuf([P, D // P], F32, "x_scale_cols")
         scale_one = sbuf([P, 1], F32, "scale_one")
         scale_rows = sbuf([P, QUAD], F32, "scale_rows")
         scale_cols = sbuf([P, QUAD], F32, "scale_cols")
@@ -63,7 +67,7 @@ def tile_rankwisemoloradenserouter_d2p_kernel(
         a_sc = sbuf([P, R], U8, "a_sc")
         w0_sc = sbuf([P, F], U8, "w0_sc")
         b_sc = sbuf([P, F], U8, "b_sc")
-        x_raw = {(r0, r1): sbuf([P, r1 - r0, D], U8, f"x_raw{r0}") for r0, r1 in X_LOADS}
+        x_raw = {(r0, r1): sbuf([P, (r1 - r0) * D], U8, f"x_raw{r0}") for r0, r1 in X_LOADS}
         wr_both = sbuf([P, 2, E], I32, "wr_both")
         a_in = sbuf([P, 2, R], I32, "a_in")
         a_codes = sbuf_each(range(2), [P, R], I32, "a_codes")
@@ -73,12 +77,16 @@ def tile_rankwisemoloradenserouter_d2p_kernel(
         w0_codes = [[w0_first[g][:, 0] for g in range(2)], [w0_second[:, g] for g in range(2)]]
         b_codes = sbuf_each(range(2), [P, 1, BANK], I32, "b_codes")
 
-        x_view = x_bytes.rearrange("(r p) k -> p r k", p=P)
-        out_view = out.rearrange("(r p) f -> p r f", p=P)
+        half_t = T // 2
+        x_early = x_bytes[:half_t].rearrange("(b q r) k -> q b (r k)", b=EARLY, r=EARLY)
+        x_late = x_bytes[half_t:].rearrange("(r p) k -> p r k", p=P)
+        out_early = out[:half_t].rearrange("(b q r) f -> q b (r f)", b=EARLY, r=EARLY)
+        out_late = out[half_t:].rearrange("(r p) f -> p r f", p=P)
 
         def load_x(i):
             r0, r1 = X_LOADS[i]
-            nc.sync.dma_start(out=x_raw[r0, r1][:], in_=x_view[:, r0:r1, :])
+            rows = x_early[:, :, D * r0 : D * r1] if r0 < EARLY else x_late[:, r0 - EARLY : r1 - EARLY, :]
+            nc.sync.dma_start(out=x_raw[r0, r1][:], in_=rows)
 
         def load_codes(tile, words, c0, width):
             rows = words.rearrange("g p n t -> p g (n t)")
@@ -92,13 +100,18 @@ def tile_rankwisemoloradenserouter_d2p_kernel(
                 )
 
         def load_x_scale():
-            by_quadrant = x_scale.rearrange("r (g q) -> q (r g)", q=4)
-            nc.scalar.dma_start(out=scale_one[0:P:2, :], in_=by_quadrant.unsqueeze(2))
+            nc.scalar.dma_start(
+                out=x_scale_cols[:], in_=x_scale[:EARLY].unsqueeze(0).to_broadcast([P // EARLY, EARLY, D // P])
+            )
 
-        def spread_x_scale():
+        def load_late_scale():
+            by_quadrant = x_scale[EARLY:].rearrange("r (g q) -> q (r g)", q=4)
+            nc.sync.dma_start(out=scale_one[0:P:4, :], in_=by_quadrant.unsqueeze(2))
+
+        def spread_late_scale():
             nc.vector.tensor_copy(out=scale_rows[:], in_=scale_one[:].to_broadcast([P, QUAD]))
 
-        def turn_x_scale():
+        def turn_late_scale():
             nc.vector.transpose(out=scale_cols[:], in_=scale_rows[:])
 
         halves = [(r, g) for r in range(TILES) for g in range(2)]
@@ -114,50 +127,63 @@ def tile_rankwisemoloradenserouter_d2p_kernel(
         neg_max = sbuf_each(range(PAIRS), [P, 2], F32, "neg_max")
         total = sbuf_each(range(PAIRS), [P, 2], F32, "total")
         inv_total = sbuf_each(range(PAIRS), [P, 2], F32, "inv_total")
+        weight_e = sbuf_each(range(PAIRS), [P, 2, E], F32, "weight_e")
+        z_wide = sbuf_each(range(TILES), [P, R], BF16, "z_wide")
         z_in = sbuf_each(range(PAIRS), [P, 2 * R], BF16, "z_in")
         z_codes = sbuf_each(range(PAIRS), [P, 2 * P], U32, "z_codes")
         z_sc = sbuf_each(range(PAIRS), [P, 2 * P], U8, "z_sc")
         y_out = sbuf_each(range(TILES), [P, F], F32, "y_out")
-        xt_ps, gt_ps, l_ps, u_ps, y_ps, br_ps = {}, {}, {}, {}, {}, {}
+        xt_ps, zt_ps, gt_ps, l_ps, u_ps, y_ps, br_ps = {}, {}, {}, {}, {}, {}, {}
         on_scalar, on_vector = nc.scalar.copy, nc.vector.tensor_copy
 
         def tile_cols(r):
             return slice(P * (r % 2), P * (r % 2) + P)
 
-        def x_half(r, g):
+        def x_block(r, g, j):
             r0, r1 = [run for run in X_LOADS if run[0] <= r < run[1]][0]
-            return x_raw[r0, r1][:, r - r0, PASS * g : PASS * g + PASS].bitcast(FP8)
+            c0 = D * (r - r0) + PASS * g + P * j
+            col = BLOCKS * g + j
+            return x_raw[r0, r1][:, c0 : c0 + P].bitcast(FP8), x_scale_cols[:, col : col + 1]
 
         def widen_vector(r, g):
+            runs = x_wide[r, g][:].rearrange("p (s q e) -> p q s e", s=2, e=2)
+            for j in range(BLOCKS):
+                codes, scale = x_block(r, g, j)
+                nc.vector.tensor_scalar(
+                    out=runs[:, 32 * j : 32 * j + 32],
+                    in0=codes.rearrange("p (q s e) -> p q s e", s=2, e=2),
+                    scalar1=scale,
+                    scalar2=None,
+                    op0=MULT,
+                )
+
+        def widen_scalar(r, g):
+            for j in range(BLOCKS):
+                codes, scale = x_block(r, g, j)
+                nc.scalar.activation(out=x_wide[r, g][:, P * j : P * j + P], in_=codes, func=ACT.Copy, scale=scale)
+
+        def x_half(r, g):
+            r0, r1 = [run for run in X_LOADS if run[0] <= r < run[1]][0]
+            c0 = D * (r - r0) + PASS * g
+            return x_raw[r0, r1][:, c0 : c0 + PASS].bitcast(FP8)
+
+        def cast_vector(r, g):
             nc.vector.tensor_copy(
                 out=x_wide[r, g][:].rearrange("p (s q e) -> p q s e", s=2, e=2),
                 in_=x_half(r, g).rearrange("p (q s e) -> p q s e", s=2, e=2),
             )
 
-        def widen_scalar(r, g):
+        def cast_scalar(r, g):
             nc.scalar.copy(
                 out=x_wide[r, g][:].rearrange("p (s q e) -> p s q e", s=2, e=2),
                 in_=x_half(r, g).rearrange("p (q s e) -> p s q e", s=2, e=2),
             )
 
-        def turn_x_into(r, g, dest):
-            xt_ps[r, g] = dest
-            words = x_wide[r, g][:].bitcast(F32)
-            for s in range(2):
-                nc.tensor.transpose(dest[:, s, :], words[:, P * s : P * s + P], ident[:])
-
-        def turn_x(r, b):
-            dest = bank(b, [P, 2, 2, P], f"xt_ps{r}")
-            for g in range(2):
-                turn_x_into(r, g, dest[:, g])
-
-        def turn_x_half(r, g, b):
-            turn_x_into(r, g, bank(b, [P, 2, P], f"xt_ps{r}_{g}")[:])
-
         def scale_views(r, g):
-            dest = x_in[r // 2, g][:, PASS * (r % 2) : PASS * (r % 2) + PASS].rearrange("p (n s e) -> p n s e", s=2, e=2)
+            dest = x_in[r // 2, g][:, PASS * (r % 2) : PASS * (r % 2) + PASS]
             turned = xt_ps[r, g].bitcast(BF16).rearrange("p s (n e) -> p n s e", e=2)
-            return dest, turned, scale_cols[:, 4 * r + 2 * g : 4 * r + 2 * g + 1]
+            col = 4 * (2 * (r - EARLY) + g)
+            return dest.rearrange("p (n s e) -> p n s e", s=2, e=2), turned, scale_cols[:, col : col + 1]
 
         def scale_vector(r, g):
             dest, turned, scale = scale_views(r, g)
@@ -166,6 +192,25 @@ def tile_rankwisemoloradenserouter_d2p_kernel(
         def scale_scalar(r, g):
             dest, turned, scale = scale_views(r, g)
             nc.scalar.activation(out=dest, in_=turned, func=ACT.Copy, scale=scale)
+
+        def turn_x_into(r, g, dest):
+            xt_ps[r, g] = dest
+            words = x_wide[r, g][:].bitcast(F32)
+            for s in range(2):
+                run = words[:, s::2] if (r, g) in UNSORTED else words[:, P * s : P * s + P]
+                nc.tensor.transpose(dest[:, s, :], run, ident[:])
+
+        def turn_x(r, b, passes=(0, 1)):
+            dest = bank(b, [P, 2, 2, P], f"xt_ps{r}")
+            for g in passes:
+                turn_x_into(r, g, dest[:, g])
+
+        def turn_x_half(r, g, b):
+            turn_x_into(r, g, bank(b, [P, 2, P], f"xt_ps{r}_{g}")[:])
+
+        def copy_x(r, g, copy):
+            dest = x_in[r // 2, g][:, PASS * (r % 2) : PASS * (r % 2) + PASS]
+            copy(out=dest.bitcast(F32).rearrange("p (n s) -> p n s", s=2), in_=xt_ps[r, g].rearrange("p s n -> p n s"))
 
         def quantize_x_half(r, g):
             h, i = divmod(r, 2)
@@ -180,13 +225,14 @@ def tile_rankwisemoloradenserouter_d2p_kernel(
 
         def order_a_codes(g, copy):
             copy(
-                out=a_codes[g][:].bitcast(U32).rearrange("p (c e) -> p c e", c=4),
-                in_=a_in[:, g].bitcast(U32).rearrange("p (e c) -> p c e", c=4),
+                out=a_codes[g][:].bitcast(U32).rearrange("p (c b i) -> p b c i", c=4, i=4),
+                in_=a_in[:, g].bitcast(U32).rearrange("p (b i c) -> p b c i", c=4, i=4),
             )
 
         def order_a_scales():
             nc.vector.tensor_copy(
-                out=a_sc[:].rearrange("p (c e) -> p c e", c=4), in_=a_sc_in[:].rearrange("p (e c) -> p c e", c=4)
+                out=a_sc[:].rearrange("p (c b i) -> p b c i", c=4, i=16),
+                in_=a_sc_in[:].rearrange("p (b i c) -> p b c i", c=4, i=16),
             )
 
         def warm_up(count, b):
@@ -236,6 +282,10 @@ def tile_rankwisemoloradenserouter_d2p_kernel(
                         stop=(g == 1),
                     )
 
+        def down_tokens(r, b):
+            u_ps[r] = bank(b, [P, R], f"u_ps{r}")
+            x_product(u_ps[r][:], r, [a_in[:, g] for g in range(2)], 0, a_sc_in, 0, R, True)
+
         def base(r, c0, width, b, passes=(0, 1)):
             if 0 in passes:
                 y_ps[r, c0] = bank(b, [P, width], f"y_ps{r}_{c0}")
@@ -262,7 +312,11 @@ def tile_rankwisemoloradenserouter_d2p_kernel(
             copy(out=y_out[r][:, c0 : c0 + width], in_=y_ps[r, c0][:])
 
         def store_y(r, c0, width):
-            nc.sync.dma_start(out=out_view[:, r, c0 : c0 + width], in_=y_out[r][:, c0 : c0 + width])
+            if r < EARLY:
+                dest = out_early[:, :, F * r + c0 : F * r + c0 + width]
+            else:
+                dest = out_late[:, r - EARLY, c0 : c0 + width]
+            nc.sync.dma_start(out=dest, in_=y_out[r][:, c0 : c0 + width])
 
         def store(r, c0, width, copy):
             copy_y(r, c0, width, copy)
@@ -300,6 +354,35 @@ def tile_rankwisemoloradenserouter_d2p_kernel(
                 op1=MULT,
             )
 
+        def scale_weights(h):
+            nc.vector.tensor_scalar(out=weight_e[h][:], in0=weight[h][:], scalar1=float(E), scalar2=None, op0=MULT)
+
+        def gate_tokens(r, runs=(0, 1)):
+            h, i = divmod(r, 2)
+            for s in runs:
+                nc.vector.scalar_tensor_tensor(
+                    out=z_wide[r][:, 2 * E * s : 2 * E * s + 2 * E].rearrange("p (e c) -> p e c", c=2),
+                    in0=u_ps[r][:].rearrange("p (e s c) -> p s e c", s=2, c=2)[:, s],
+                    scalar=inv_total[h][:, i : i + 1],
+                    in1=weight_e[h][:, i, :].unsqueeze(2).to_broadcast([P, E, 2]),
+                    op0=MULT,
+                    op1=MULT,
+                )
+
+        def turn_z(tiles, b):
+            dest = bank(b, [P, len(tiles), 2, P], f"zt_ps{tiles[0]}")
+            for i, r in enumerate(tiles):
+                zt_ps[r] = dest[:, i]
+                words = z_wide[r][:].bitcast(F32)
+                for s in range(2):
+                    nc.tensor.transpose(zt_ps[r][:, s, :], words[:, P * s : P * s + P], ident[:])
+
+        def copy_z(r):
+            dest = z_in[r // 2][:, R * (r % 2) : R * (r % 2) + R]
+            nc.scalar.copy(
+                out=dest.bitcast(F32).rearrange("p (n s) -> p n s", s=2), in_=zt_ps[r].rearrange("p s n -> p n s")
+            )
+
         def turn_gates(tiles, b):
             dest = bank(b, [P, len(tiles), P], f"gt_ps{tiles[0]}")
             for j, r in enumerate(tiles):
@@ -330,27 +413,27 @@ def tile_rankwisemoloradenserouter_d2p_kernel(
             )
 
 
-        nc.gpsimd.memset(scale_one[:], 0.0)
         nc.vector.memset(zeros[:], 0.0)
-        for plane in (w0_sc, wr_sc, a_sc_in):
-            nc.vector.memset(plane[:].bitcast(I32), 0)
         nc.vector.memset(br_rows[:], 0.0)
-        nc.vector.memset(b_sc[:].bitcast(I32), 0)
+        for plane in (a_sc_in, wr_sc, w0_sc, b_sc):
+            nc.vector.memset(plane[:].bitcast(I32), 0)
         make_identity(nc, ident[:])
+        nc.gpsimd.memset(scale_one[:], 0.0)
         load_x_scale()
         nc.scalar.activation(out=ones[:], in_=zeros[:, :P], func=ACT.Exp)
         load_x(0)
         load_x(1)
         load_x(2)
-        load_codes(w0_first[0][:], w0_words[0:1], 0, BANK)
-        load_scales(w0_sc, w0_scales)
-        load_codes(w0_first[1][:], w0_words[1:2], 0, BANK)
         nc.sync.dma_start(out=br_rows[0:1, :], in_=br.unsqueeze(0))
+        load_scales(a_sc_in, a_scales)
+        load_codes(a_in[:], a_words, 0, R)
         load_codes(wr_both[:], wr_words, 0, E)
         load_scales(wr_sc, wr_scales)
-        load_codes(a_in[:], a_words, 0, R)
-        load_scales(a_sc_in, a_scales)
         load_x(3)
+        load_codes(w0_first[0][:], w0_words[0:1], 0, BANK)
+        load_scales(w0_sc, w0_scales)
+        load_late_scale()
+        load_codes(w0_first[1][:], w0_words[1:2], 0, BANK)
         load_x(4)
         load_codes(w0_second[:], w0_words, BANK, BANK)
         load_codes(b_codes[0][:], b_words, 0, BANK)
@@ -359,175 +442,170 @@ def tile_rankwisemoloradenserouter_d2p_kernel(
 
         warm_up(4, 7)
         widen_vector(0, 0)
-        spread_x_scale()
-        widen_scalar(0, 1)
-        widen_vector(1, 0)
-        turn_x_scale()
+        widen_vector(0, 1)
         widen_scalar(1, 1)
-        widen_vector(2, 0)
-        widen_scalar(2, 1)
-        widen_scalar(3, 0)
+        widen_vector(1, 0)
+        for g in range(2):
+            turn_x_half(0, g, g)
+            warm_up(1, 7)
+        turn_x_half(1, 0, 2)
+        turn_x_half(1, 1, 6)
         widen_scalar(3, 1)
-        turn_x(0, 0)
-        turn_x_half(1, 0, 1)
-        turn_x_half(1, 1, 2)
-        warm_up(1, 7)
-        for r in (2, 3):
+        for r in range(2):
             for g in range(2):
-                turn_x_half(r, g, 2 * r + g - 1)
-        scale_vector(0, 0)
-        scale_vector(0, 1)
-        quantize_x_half(0, 0)
-        scale_vector(1, 0)
-        quantize_x_half(0, 1)
-        scale_vector(2, 0)
-        quantize_x_half(1, 0)
-        scale_vector(3, 0)
-        for r in (1, 2, 3):
-            scale_scalar(r, 1)
-        quantize_x_half(1, 1)
-        quantize_x_half(2, 0)
-        quantize_x_half(2, 1)
-        quantize_x_half(3, 0)
-        quantize_x_half(3, 1)
-        base(0, 0, BANK, 7)
-        spread_bias(0)
-        base(1, 0, BANK, 1, (0,))
+                copy_x(r, g, on_scalar)
+        widen_vector(2, 0)
+        widen_vector(2, 1)
+        widen_vector(3, 0)
+        for r in range(2):
+            for g in range(2):
+                quantize_x_half(r, g)
+        spread_bias(4)
+        turn_x(2, 3)
+        turn_x(3, 0, (1, 0))
+
+        down_tokens(0, 1)
         open_logits((0,), 5)
         router(0)
-        base(1, 0, BANK, 1, (1,))
         router(1)
-        base(2, 0, BANK, 2)
+        for g in range(2):
+            copy_x(2, g, on_scalar)
+            copy_x(3, g, on_scalar)
+        copy_bias()
+        order_a_scales()
+        down_tokens(1, 2)
+        quantize_x(1, 0)
+        order_a_codes(0, on_vector)
+        quantize_x(1, 1)
+        order_a_codes(1, on_scalar)
+        add_bias(0)
+        cast_scalar(4, 0)
+        cast_scalar(4, 1)
+        cast_vector(5, 0)
+        row_max(0)
         open_logits((1,), 4)
         router(2)
         router(3)
-        copy_bias()
-        order_a_codes(0, on_vector)
-        order_a_scales()
-        add_bias(0)
-        order_a_codes(1, on_scalar)
-        widen_scalar(4, 1)
-        widen_scalar(5, 0)
-        widen_scalar(5, 1)
-        widen_scalar(7, 0)
-        widen_vector(4, 0)
-        row_max(0)
-        add_bias(1)
-        widen_vector(6, 0)
-        row_max(1)
+        down(1, 0, 3)
+        down(1, 1, 0)
         exp_and_sum(0)
-        down(0, 0, 3)
-        down(0, 1, 0)
-        down(1, 0, 6)
-        down(1, 1, 5)
-        copy_u(0, 0, on_scalar)
-        widen_vector(6, 1)
+        add_bias(1)
+        cast_vector(5, 1)
+        spread_late_scale()
+        copy_u(1, 0, on_scalar)
         invert_sum(0)
-        widen_vector(7, 1)
-        exp_and_sum(1)
-        normalise(0)
-        normalise(1)
-        copy_u(1, 0, on_vector)
-        copy_u(0, 1, on_scalar)
-        invert_sum(1)
+        scale_weights(0)
+        turn_late_scale()
+        row_max(1)
+        base(0, 0, BANK, 6, (0,))
+        base(1, 0, BANK, 7, (0,))
+        base(2, 0, BANK, 5, (0,))
+        for r in range(3):
+            base(r, 0, BANK, None, (1,))
+        gate_tokens(0)
         copy_u(1, 1, on_scalar)
+        exp_and_sum(1)
+        gate_tokens(1)
+        cast_scalar(6, 0)
+        cast_scalar(7, 0)
+        cast_scalar(7, 1)
+        invert_sum(1)
+        cast_vector(6, 1)
 
         turn_x(4, 4)
-        scale_vector(4, 0)
-        normalise(2)
-        normalise(3)
+        turn_z((0, 1), 1)
         turn_x(5, 3)
         turn_x(6, 0)
-        turn_x(7, 6)
-        turn_gates((0, 1, 2, 3), 5)
+        scale_vector(4, 0)
         scale_vector(4, 1)
+        normalise(2)
+        normalise(3)
+        copy_z(0)
+        copy_z(1)
+        turn_x(7, 2)
+        turn_gates((2, 3), 4)
         scale_vector(5, 0)
-        scale_vector(5, 1)
-        scale_scalar(6, 0)
-        scale_scalar(6, 1)
-        scale_scalar(7, 0)
-        scale_scalar(7, 1)
-        gate(0)
-        quantize_x(2, 0)
         quantize_z(0)
-        gate(1)
-        quantize_x(2, 1)
+        scale_vector(5, 1)
         quantize_z(1)
-        quantize_x(3, 0)
-        quantize_x(3, 1)
-        base(0, BANK, BANK, 4)
-        base(1, BANK, BANK, 3)
-        base(2, BANK, BANK, 0)
+        gate(2)
+        base(0, BANK, BANK, 1)
         lora(0, 0, BANK)
         lora(0, BANK, BANK)
-        base(3, 0, BANK, 6)
+        base(1, BANK, BANK, 3)
         lora(1, 0, BANK)
         lora(1, BANK, BANK)
-        gate(2)
-        gate(3)
+        for r in (6, 7):
+            for g in range(2):
+                scale_scalar(r, g)
+        quantize_x(2, 0)
         quantize_z(2)
-        store(0, 0, BANK, on_scalar)
-        store(0, BANK, BANK, on_scalar)
+        quantize_x(2, 1)
+        gate(3)
+        quantize_x(3, 0)
+        quantize_x(3, 1)
+        quantize_z(3)
+        copy_y(0, 0, BANK, on_scalar)
+        copy_y(0, BANK, BANK, on_vector)
+        store_y(0, 0, F)
         store(1, 0, BANK, on_scalar)
-        open_logits((2, 3), 7)
+        base(2, BANK, BANK, 0)
+        open_logits((2, 3), 2)
         for r in range(4, TILES):
             router(r)
+        lora(2, 0, BANK)
+        lora(2, BANK, BANK)
         add_bias(2)
-        quantize_z(3)
         add_bias(3)
         row_max(2)
         row_max(3)
         store(1, BANK, BANK, on_scalar)
         down(2, 0, 4)
-        down(2, 1, 1)
-        copy_u(2, 0, on_scalar)
+        down(2, 1, 6)
+        copy_y(2, 0, BANK, on_scalar)
         exp_and_sum(2)
-        lora(2, 0, BANK)
-        lora(2, BANK, BANK)
-        lora(3, 0, BANK)
         exp_and_sum(3)
-        copy_y(2, 0, BANK, on_vector)
+        copy_y(2, BANK, BANK, on_vector)
+        store_y(2, 0, F)
+        base_and_lora(3, 0, BANK, 1)
         invert_sum(2)
         invert_sum(3)
-        normalise(4)
-        normalise(5)
-        normalise(6)
-        normalise(7)
+        for r in range(4, TILES):
+            normalise(r)
+        copy_u(2, 0, on_scalar)
         copy_u(2, 1, on_scalar)
-        down(3, 0, 3)
-        down(3, 1, 7)
-        copy_y(2, BANK, BANK, on_scalar)
-        store_y(2, 0, F)
+        down(3, 0, 7)
+        down(3, 1, 3)
         store(3, 0, BANK, on_vector)
         base(3, BANK, BANK, 2)
 
-        turn_gates((4, 5, 6, 7), 5)
+        turn_gates((4, 5), 5)
+        turn_gates((6, 7), 0)
         gate(4)
         copy_u(3, 0, on_scalar)
         copy_u(3, 1, on_scalar)
-        gate(5)
         quantize_z(4)
+        gate(5)
         lora(3, BANK, BANK)
         base(4, 0, BANK, 4)
-        base(4, BANK, BANK, 1)
-        base(5, 0, BANK, 0)
+        base(4, BANK, BANK, 6)
         lora(4, 0, BANK)
         lora(4, BANK, BANK)
+        store(3, BANK, BANK, on_scalar)
         gate(6)
         quantize_z(5)
-        store(3, BANK, BANK, on_scalar)
+        store(4, 0, BANK, on_scalar)
+        store(4, BANK, BANK, on_scalar)
         gate(7)
         quantize_z(6)
-        store(4, 0, BANK, on_scalar)
+        base_and_lora(5, 0, BANK, 1)
         quantize_z(7)
-        store(4, BANK, BANK, on_vector)
-        lora(5, 0, BANK)
-        store(5, 0, BANK, on_scalar)
-        base_and_lora(5, BANK, BANK, 6)
-        store(5, BANK, BANK, on_vector)
+        store(5, 0, BANK, on_vector)
+        base_and_lora(5, BANK, BANK, 7)
+        store(5, BANK, BANK, on_scalar)
         base_and_lora(6, 0, BANK, 3)
-        store(6, 0, BANK, on_scalar)
+        store(6, 0, BANK, on_vector)
         pieces = [(6, c0) for c0 in range(BANK, F, QUARTER)] + [(7, c0) for c0 in range(0, F, QUARTER)]
-        for i, ((r, c0), b) in enumerate(zip(pieces, (7, 2, 5, 4, 1, 0))):
+        for i, ((r, c0), b) in enumerate(zip(pieces, (2, 5, 4, 6, 0, 1))):
             base_and_lora(r, c0, QUARTER, b)
-            store(r, c0, QUARTER, on_scalar if i % 2 else on_vector)
+            store(r, c0, QUARTER, on_vector if i % 2 else on_scalar)

@@ -118,8 +118,12 @@ def tile_rankwisemoloradenserouter_d2p_kernel(
         pair_passes = [(h, g) for h in range(PAIRS) for g in range(2)]
         x_wide = sbuf_each(halves, [P, PASS], BF16, "x_wide")
         x_in = sbuf_each(pair_passes, [P, 2 * PASS], BF16, "x_in")
-        x_codes = sbuf_each(pair_passes, [P, 2 * P], U32, "x_codes")
-        x_sc = sbuf_each(pair_passes, [P, 2 * P], U8, "x_sc")
+        quad_passes = [(q, g) for q in range(2) for g in range(2)]
+        x_quad = sbuf_each(quad_passes, [P, 4 * P], U32, "x_codes")
+        x_quad_sc = sbuf_each(quad_passes, [P, 4 * P], U8, "x_sc")
+        x_codes = {(h, g): x_quad[h // 2, g][:, 2 * P * (h % 2) : 2 * P * (h % 2 + 1)] for h, g in pair_passes}
+        x_sc = {(h, g): x_quad_sc[h // 2, g][:, 2 * P * (h % 2) : 2 * P * (h % 2 + 1)] for h, g in pair_passes}
+        u_late = sbuf([P, 4, 4 * P], F32, "u_late")
         logit = sbuf_each(range(PAIRS), [P, 2, E], F32, "logit")
         weight = sbuf_each(range(PAIRS), [P, 2, E], F32, "weight")
         gates = sbuf_each(range(TILES), [P, E], F32, "gates")
@@ -282,6 +286,20 @@ def tile_rankwisemoloradenserouter_d2p_kernel(
                         stop=(g == 1),
                     )
 
+        def down_late(c, b):
+            u_ps["late", c] = bank(b, [P, 4 * P], f"u_ps_late{c}")
+            cols = slice(P * c, P * c + P)
+            for g in range(2):
+                nc.tensor.matmul_mx(
+                    out=u_ps["late", c][:],
+                    lhsT=a_codes[g][:, cols].bitcast(FP8X4),
+                    lhsT_scale=a_sc[4 * g :, cols],
+                    rhs=x_quad[1, g][:].bitcast(FP8X4),
+                    rhs_scale=x_quad_sc[1, g][:],
+                    start=(g == 0),
+                    stop=(g == 1),
+                )
+
         def down_tokens(r, b):
             u_ps[r] = bank(b, [P, R], f"u_ps{r}")
             x_product(u_ps[r][:], r, [a_in[:, g] for g in range(2)], 0, a_sc_in, 0, R, True)
@@ -404,6 +422,19 @@ def tile_rankwisemoloradenserouter_d2p_kernel(
                 op=MULT,
             )
 
+        def copy_u_late(c, copy):
+            copy(out=u_late[:, c], in_=u_ps["late", c][:])
+
+        def gate_late(r):
+            h, i = divmod(r, 2)
+            n0 = P * (r - EARLY)
+            nc.vector.tensor_tensor(
+                out=z_in[h][:, R * i : R * i + R].rearrange("p (m j c) -> p m c j", j=2, c=4),
+                in0=gt_ps[r].rearrange("p (m j) -> p m j", j=2).unsqueeze(2).to_broadcast([P, P // 2, 4, 2]),
+                in1=u_late[:, :, n0 : n0 + P].rearrange("p c (m j) -> p m c j", j=2),
+                op=MULT,
+            )
+
         def quantize_z(r):
             h, i = divmod(r, 2)
             nc.vector.quantize_mx(
@@ -462,21 +493,23 @@ def tile_rankwisemoloradenserouter_d2p_kernel(
                 quantize_x_half(r, g)
         spread_bias(4)
         turn_x(2, 3)
-        turn_x(3, 0, (1, 0))
+        turn_x_half(3, 1, 7)
+        turn_x_half(3, 0, 0)
 
         down_tokens(0, 1)
         open_logits((0,), 5)
         router(0)
         router(1)
-        for g in range(2):
-            copy_x(2, g, on_scalar)
-            copy_x(3, g, on_scalar)
         copy_bias()
+        copy_x(2, 0, on_scalar)
+        copy_x(2, 1, on_scalar)
+        copy_x(3, 1, on_scalar)
+        copy_x(3, 0, on_vector)
         order_a_scales()
         down_tokens(1, 2)
         quantize_x(1, 0)
-        order_a_codes(0, on_vector)
         quantize_x(1, 1)
+        order_a_codes(0, on_scalar)
         order_a_codes(1, on_scalar)
         add_bias(0)
         cast_scalar(4, 0)
@@ -508,9 +541,9 @@ def tile_rankwisemoloradenserouter_d2p_kernel(
         gate_tokens(1)
         cast_scalar(6, 0)
         cast_scalar(7, 0)
-        cast_scalar(7, 1)
         invert_sum(1)
         cast_vector(6, 1)
+        cast_vector(7, 1)
 
         turn_x(4, 4)
         turn_z((0, 1), 1)
@@ -531,9 +564,9 @@ def tile_rankwisemoloradenserouter_d2p_kernel(
         gate(2)
         base(0, BANK, BANK, 1)
         lora(0, 0, BANK)
-        lora(0, BANK, BANK)
         base(1, BANK, BANK, 3)
         lora(1, 0, BANK)
+        lora(0, BANK, BANK)
         lora(1, BANK, BANK)
         for r in (6, 7):
             for g in range(2):
@@ -541,14 +574,14 @@ def tile_rankwisemoloradenserouter_d2p_kernel(
         quantize_x(2, 0)
         quantize_z(2)
         quantize_x(2, 1)
-        gate(3)
         quantize_x(3, 0)
         quantize_x(3, 1)
+        gate(3)
         quantize_z(3)
         copy_y(0, 0, BANK, on_scalar)
+        store(1, 0, BANK, on_scalar)
         copy_y(0, BANK, BANK, on_vector)
         store_y(0, 0, F)
-        store(1, 0, BANK, on_scalar)
         base(2, BANK, BANK, 0)
         open_logits((2, 3), 2)
         for r in range(4, TILES):
@@ -560,43 +593,41 @@ def tile_rankwisemoloradenserouter_d2p_kernel(
         row_max(2)
         row_max(3)
         store(1, BANK, BANK, on_scalar)
-        down(2, 0, 4)
-        down(2, 1, 6)
+        down_late(0, 4)
+        down_late(1, 6)
         copy_y(2, 0, BANK, on_scalar)
         exp_and_sum(2)
         exp_and_sum(3)
         copy_y(2, BANK, BANK, on_vector)
         store_y(2, 0, F)
+        down_late(2, 7)
+        down_late(3, 3)
         base_and_lora(3, 0, BANK, 1)
+        copy_u_late(0, on_vector)
         invert_sum(2)
         invert_sum(3)
         for r in range(4, TILES):
             normalise(r)
-        copy_u(2, 0, on_scalar)
-        copy_u(2, 1, on_scalar)
-        down(3, 0, 7)
-        down(3, 1, 3)
-        store(3, 0, BANK, on_vector)
-        base(3, BANK, BANK, 2)
+        for c in range(1, 4):
+            copy_u_late(c, on_scalar)
+        store(3, 0, BANK, on_scalar)
 
         turn_gates((4, 5), 5)
         turn_gates((6, 7), 0)
-        gate(4)
-        copy_u(3, 0, on_scalar)
-        copy_u(3, 1, on_scalar)
+        gate_late(4)
         quantize_z(4)
-        gate(5)
-        lora(3, BANK, BANK)
+        gate_late(5)
+        quantize_z(5)
+        base_and_lora(3, BANK, BANK, 2)
         base(4, 0, BANK, 4)
         base(4, BANK, BANK, 6)
         lora(4, 0, BANK)
         lora(4, BANK, BANK)
         store(3, BANK, BANK, on_scalar)
-        gate(6)
-        quantize_z(5)
+        gate_late(6)
         store(4, 0, BANK, on_scalar)
         store(4, BANK, BANK, on_scalar)
-        gate(7)
+        gate_late(7)
         quantize_z(6)
         base_and_lora(5, 0, BANK, 1)
         quantize_z(7)

@@ -78,15 +78,15 @@ def tile_rankwisemoloradenserouter_d2p_kernel(
         b_codes = sbuf_each(range(2), [P, 1, BANK], I32, "b_codes")
 
         half_t = T // 2
-        x_early = x_bytes[:half_t].rearrange("(b q r) k -> q b (r k)", b=EARLY, r=EARLY)
+        x_early = x_bytes[:half_t].rearrange("(p r) k -> p r k", r=EARLY)
         x_late = x_bytes[half_t:].rearrange("(r p) k -> p r k", p=P)
-        out_early = out[:half_t].rearrange("(b q r) f -> q b (r f)", b=EARLY, r=EARLY)
+        out_early = out[:half_t].rearrange("(p r) f -> p r f", r=EARLY)
         out_late = out[half_t:].rearrange("(r p) f -> p r f", p=P)
 
         def load_x(i):
             r0, r1 = X_LOADS[i]
-            rows = x_early[:, :, D * r0 : D * r1] if r0 < EARLY else x_late[:, r0 - EARLY : r1 - EARLY, :]
-            nc.sync.dma_start(out=x_raw[r0, r1][:], in_=rows)
+            rows = x_early[:, r0:r1, :] if r0 < EARLY else x_late[:, r0 - EARLY : r1 - EARLY, :]
+            nc.sync.dma_start(out=x_raw[r0, r1][:].rearrange("p (r k) -> p r k", k=D), in_=rows)
 
         def load_codes(tile, words, c0, width):
             rows = words.rearrange("g p n t -> p g (n t)")
@@ -101,7 +101,7 @@ def tile_rankwisemoloradenserouter_d2p_kernel(
 
         def load_x_scale():
             nc.scalar.dma_start(
-                out=x_scale_cols[:], in_=x_scale[:EARLY].unsqueeze(0).to_broadcast([P // EARLY, EARLY, D // P])
+                out=x_scale_cols[:], in_=x_scale[:EARLY].unsqueeze(1).to_broadcast([EARLY, P // EARLY, D // P])
             )
 
         def load_late_scale():
@@ -331,7 +331,7 @@ def tile_rankwisemoloradenserouter_d2p_kernel(
 
         def store_y(r, c0, width):
             if r < EARLY:
-                dest = out_early[:, :, F * r + c0 : F * r + c0 + width]
+                dest = out_early[:, r, c0 : c0 + width]
             else:
                 dest = out_late[:, r - EARLY, c0 : c0 + width]
             nc.sync.dma_start(out=dest, in_=y_out[r][:, c0 : c0 + width])

@@ -27,12 +27,10 @@ BANK = 512
 QUARTER = 256
 EARLY = TILES // 2
 QUAD = 32
-BLOCKS = PASS // P
 
 FIRST, SECOND = slice(0, 1), slice(1, 2)
 
 X_LOADS = ((0, 1), (1, 2), (2, 4), (4, 6), (6, 8))
-UNSORTED = ((1, 1), (3, 1))
 
 
 def tile_rankwisemoloradenserouter_d2p_kernel(
@@ -58,7 +56,6 @@ def tile_rankwisemoloradenserouter_d2p_kernel(
         ident = sbuf([P, P], F32, "ident")
         br_rows = sbuf([P, E], BF16, "br_rows")
         br_spread = sbuf([P, E], F32, "br_spread")
-        x_scale_cols = sbuf([P, D // P], F32, "x_scale_cols")
         scale_one = sbuf([P, 1], F32, "scale_one")
         scale_rows = sbuf([P, QUAD], F32, "scale_rows")
         scale_cols = sbuf([P, QUAD], F32, "scale_cols")
@@ -67,7 +64,7 @@ def tile_rankwisemoloradenserouter_d2p_kernel(
         a_sc = sbuf([P, R], U8, "a_sc")
         w0_sc = sbuf([P, F], U8, "w0_sc")
         b_sc = sbuf([P, F], U8, "b_sc")
-        x_raw = {(r0, r1): sbuf([P, (r1 - r0) * D], U8, f"x_raw{r0}") for r0, r1 in X_LOADS}
+        x_raw = {(r0, r1): sbuf([P, r1 - r0, D], U8, f"x_raw{r0}") for r0, r1 in X_LOADS}
         wr_both = sbuf([P, 2, E], I32, "wr_both")
         a_in = sbuf([P, 2, R], I32, "a_in")
         a_codes = sbuf_each(range(2), [P, R], I32, "a_codes")
@@ -77,16 +74,12 @@ def tile_rankwisemoloradenserouter_d2p_kernel(
         w0_codes = [[w0_first[g][:, 0] for g in range(2)], [w0_second[:, g] for g in range(2)]]
         b_codes = sbuf_each(range(2), [P, 1, BANK], I32, "b_codes")
 
-        half_t = T // 2
-        x_early = x_bytes[:half_t].rearrange("(p r) k -> p r k", r=EARLY)
-        x_late = x_bytes[half_t:].rearrange("(r p) k -> p r k", p=P)
-        out_early = out[:half_t].rearrange("(p r) f -> p r f", r=EARLY)
-        out_late = out[half_t:].rearrange("(r p) f -> p r f", p=P)
+        x_view = x_bytes.rearrange("(r p) k -> p r k", p=P)
+        out_view = out.rearrange("(r p) f -> p r f", p=P)
 
         def load_x(i):
             r0, r1 = X_LOADS[i]
-            rows = x_early[:, r0:r1, :] if r0 < EARLY else x_late[:, r0 - EARLY : r1 - EARLY, :]
-            nc.sync.dma_start(out=x_raw[r0, r1][:].rearrange("p (r k) -> p r k", k=D), in_=rows)
+            nc.sync.dma_start(out=x_raw[r0, r1][:], in_=x_view[:, r0:r1, :])
 
         def load_codes(tile, words, c0, width):
             rows = words.rearrange("g p n t -> p g (n t)")
@@ -100,18 +93,13 @@ def tile_rankwisemoloradenserouter_d2p_kernel(
                 )
 
         def load_x_scale():
-            nc.scalar.dma_start(
-                out=x_scale_cols[:], in_=x_scale[:EARLY].unsqueeze(1).to_broadcast([EARLY, P // EARLY, D // P])
-            )
+            by_quadrant = x_scale.rearrange("r (g q) -> q (r g)", q=4)
+            nc.scalar.dma_start(out=scale_one[0:P:2, :], in_=by_quadrant.unsqueeze(2))
 
-        def load_late_scale():
-            by_quadrant = x_scale[EARLY:].rearrange("r (g q) -> q (r g)", q=4)
-            nc.sync.dma_start(out=scale_one[0:P:4, :], in_=by_quadrant.unsqueeze(2))
-
-        def spread_late_scale():
+        def spread_x_scale():
             nc.vector.tensor_copy(out=scale_rows[:], in_=scale_one[:].to_broadcast([P, QUAD]))
 
-        def turn_late_scale():
+        def turn_x_scale():
             nc.vector.transpose(out=scale_cols[:], in_=scale_rows[:])
 
         halves = [(r, g) for r in range(TILES) for g in range(2)]
@@ -143,33 +131,9 @@ def tile_rankwisemoloradenserouter_d2p_kernel(
         def tile_cols(r):
             return slice(P * (r % 2), P * (r % 2) + P)
 
-        def x_block(r, g, j):
-            r0, r1 = [run for run in X_LOADS if run[0] <= r < run[1]][0]
-            c0 = D * (r - r0) + PASS * g + P * j
-            col = BLOCKS * g + j
-            return x_raw[r0, r1][:, c0 : c0 + P].bitcast(FP8), x_scale_cols[:, col : col + 1]
-
-        def widen_vector(r, g):
-            runs = x_wide[r, g][:].rearrange("p (s q e) -> p q s e", s=2, e=2)
-            for j in range(BLOCKS):
-                codes, scale = x_block(r, g, j)
-                nc.vector.tensor_scalar(
-                    out=runs[:, 32 * j : 32 * j + 32],
-                    in0=codes.rearrange("p (q s e) -> p q s e", s=2, e=2),
-                    scalar1=scale,
-                    scalar2=None,
-                    op0=MULT,
-                )
-
-        def widen_scalar(r, g):
-            for j in range(BLOCKS):
-                codes, scale = x_block(r, g, j)
-                nc.scalar.activation(out=x_wide[r, g][:, P * j : P * j + P], in_=codes, func=ACT.Copy, scale=scale)
-
         def x_half(r, g):
             r0, r1 = [run for run in X_LOADS if run[0] <= r < run[1]][0]
-            c0 = D * (r - r0) + PASS * g
-            return x_raw[r0, r1][:, c0 : c0 + PASS].bitcast(FP8)
+            return x_raw[r0, r1][:, r - r0, PASS * g : PASS * g + PASS].bitcast(FP8)
 
         def cast_vector(r, g):
             nc.vector.tensor_copy(
@@ -186,7 +150,7 @@ def tile_rankwisemoloradenserouter_d2p_kernel(
         def scale_views(r, g):
             dest = x_in[r // 2, g][:, PASS * (r % 2) : PASS * (r % 2) + PASS]
             turned = xt_ps[r, g].bitcast(BF16).rearrange("p s (n e) -> p n s e", e=2)
-            col = 4 * (2 * (r - EARLY) + g)
+            col = 2 * (2 * r + g)
             return dest.rearrange("p (n s e) -> p n s e", s=2, e=2), turned, scale_cols[:, col : col + 1]
 
         def scale_vector(r, g):
@@ -201,8 +165,7 @@ def tile_rankwisemoloradenserouter_d2p_kernel(
             xt_ps[r, g] = dest
             words = x_wide[r, g][:].bitcast(F32)
             for s in range(2):
-                run = words[:, s::2] if (r, g) in UNSORTED else words[:, P * s : P * s + P]
-                nc.tensor.transpose(dest[:, s, :], run, ident[:])
+                nc.tensor.transpose(dest[:, s, :], words[:, P * s : P * s + P], ident[:])
 
         def turn_x(r, b, passes=(0, 1)):
             dest = bank(b, [P, 2, 2, P], f"xt_ps{r}")
@@ -211,10 +174,6 @@ def tile_rankwisemoloradenserouter_d2p_kernel(
 
         def turn_x_half(r, g, b):
             turn_x_into(r, g, bank(b, [P, 2, P], f"xt_ps{r}_{g}")[:])
-
-        def copy_x(r, g, copy):
-            dest = x_in[r // 2, g][:, PASS * (r % 2) : PASS * (r % 2) + PASS]
-            copy(out=dest.bitcast(F32).rearrange("p (n s) -> p n s", s=2), in_=xt_ps[r, g].rearrange("p s n -> p n s"))
 
         def quantize_x_half(r, g):
             h, i = divmod(r, 2)
@@ -233,10 +192,10 @@ def tile_rankwisemoloradenserouter_d2p_kernel(
                 in_=a_in[:, g].bitcast(U32).rearrange("p (b i c) -> p b c i", c=4, i=4),
             )
 
-        def order_a_scales():
+        def order_a_scales(s):
             nc.vector.tensor_copy(
-                out=a_sc[:].rearrange("p (c b i) -> p b c i", c=4, i=16),
-                in_=a_sc_in[:].rearrange("p (b i c) -> p b c i", c=4, i=16),
+                out=a_sc[:].rearrange("p (c b i) -> p b c i", c=4, i=16)[:, :, 2 * s : 2 * s + 2],
+                in_=a_sc_in[:].rearrange("p (b i c) -> p b c i", c=4, i=16)[:, :, 2 * s : 2 * s + 2],
             )
 
         def warm_up(count, b):
@@ -330,10 +289,7 @@ def tile_rankwisemoloradenserouter_d2p_kernel(
             copy(out=y_out[r][:, c0 : c0 + width], in_=y_ps[r, c0][:])
 
         def store_y(r, c0, width):
-            if r < EARLY:
-                dest = out_early[:, r, c0 : c0 + width]
-            else:
-                dest = out_late[:, r - EARLY, c0 : c0 + width]
+            dest = out_view[:, r, c0 : c0 + width]
             nc.sync.dma_start(out=dest, in_=y_out[r][:, c0 : c0 + width])
 
         def store(r, c0, width, copy):
@@ -444,12 +400,12 @@ def tile_rankwisemoloradenserouter_d2p_kernel(
             )
 
 
+        nc.gpsimd.memset(scale_one[:], 0.0)
         nc.vector.memset(zeros[:], 0.0)
         nc.vector.memset(br_rows[:], 0.0)
         for plane in (a_sc_in, wr_sc, w0_sc, b_sc):
             nc.vector.memset(plane[:].bitcast(I32), 0)
         make_identity(nc, ident[:])
-        nc.gpsimd.memset(scale_one[:], 0.0)
         load_x_scale()
         nc.scalar.activation(out=ones[:], in_=zeros[:, :P], func=ACT.Exp)
         load_x(0)
@@ -460,10 +416,9 @@ def tile_rankwisemoloradenserouter_d2p_kernel(
         load_codes(a_in[:], a_words, 0, R)
         load_codes(wr_both[:], wr_words, 0, E)
         load_scales(wr_sc, wr_scales)
-        load_x(3)
         load_codes(w0_first[0][:], w0_words[0:1], 0, BANK)
         load_scales(w0_sc, w0_scales)
-        load_late_scale()
+        load_x(3)
         load_codes(w0_first[1][:], w0_words[1:2], 0, BANK)
         load_x(4)
         load_codes(w0_second[:], w0_words, BANK, BANK)
@@ -472,99 +427,100 @@ def tile_rankwisemoloradenserouter_d2p_kernel(
         load_codes(b_codes[1][:], b_words, BANK, BANK)
 
         warm_up(4, 7)
-        widen_vector(0, 0)
-        widen_vector(0, 1)
-        widen_scalar(1, 1)
-        widen_vector(1, 0)
-        for g in range(2):
-            turn_x_half(0, g, g)
-            warm_up(1, 7)
-        turn_x_half(1, 0, 2)
-        turn_x_half(1, 1, 6)
-        widen_scalar(3, 1)
-        for r in range(2):
+        cast_vector(0, 0)
+        spread_x_scale()
+        cast_scalar(0, 1)
+        cast_vector(1, 0)
+        turn_x_scale()
+        cast_scalar(1, 1)
+        cast_vector(2, 0)
+        cast_scalar(2, 1)
+        cast_scalar(3, 0)
+        cast_scalar(3, 1)
+        turn_x(0, 0)
+        turn_x_half(1, 0, 1)
+        turn_x_half(1, 1, 2)
+        warm_up(1, 7)
+        for r in (2, 3):
             for g in range(2):
-                copy_x(r, g, on_scalar)
-        widen_vector(2, 0)
-        widen_vector(2, 1)
-        widen_vector(3, 0)
-        for r in range(2):
-            for g in range(2):
-                quantize_x_half(r, g)
-        spread_bias(4)
-        turn_x(2, 3)
-        turn_x_half(3, 1, 7)
-        turn_x_half(3, 0, 0)
-
-        down_tokens(0, 1)
-        open_logits((0,), 5)
+                turn_x_half(r, g, 2 * r + g - 1)
+        warm_up(1, 7)
+        scale_vector(0, 0)
+        scale_vector(0, 1)
+        quantize_x_half(0, 0)
+        scale_vector(1, 0)
+        quantize_x_half(0, 1)
+        scale_vector(2, 0)
+        quantize_x_half(1, 0)
+        scale_vector(3, 0)
+        for r in (1, 2, 3):
+            scale_scalar(r, 1)
+        quantize_x_half(1, 1)
+        down_tokens(0, 7)
+        spread_bias(1)
+        open_logits((0,), 0)
         router(0)
         router(1)
-        copy_bias()
-        copy_x(2, 0, on_scalar)
-        copy_x(2, 1, on_scalar)
-        copy_x(3, 1, on_scalar)
-        copy_x(3, 0, on_vector)
-        order_a_scales()
         down_tokens(1, 2)
+        copy_bias()
         quantize_x(1, 0)
         quantize_x(1, 1)
         order_a_codes(0, on_scalar)
         order_a_codes(1, on_scalar)
         add_bias(0)
-        cast_scalar(4, 0)
-        cast_scalar(4, 1)
-        cast_vector(5, 0)
+        order_a_scales(0)
         row_max(0)
-        open_logits((1,), 4)
+        order_a_scales(1)
+        open_logits((1,), 3)
         router(2)
         router(3)
-        down(1, 0, 3)
+        base(0, 0, BANK, 4, (0,))
+        base(1, 0, BANK, 5, (0,))
+        base(2, 0, BANK, 6, (0,))
+        down(1, 0, 1)
         down(1, 1, 0)
-        exp_and_sum(0)
-        add_bias(1)
-        cast_vector(5, 1)
-        spread_late_scale()
-        copy_u(1, 0, on_scalar)
-        invert_sum(0)
-        scale_weights(0)
-        turn_late_scale()
-        row_max(1)
-        base(0, 0, BANK, 6, (0,))
-        base(1, 0, BANK, 7, (0,))
-        base(2, 0, BANK, 5, (0,))
         for r in range(3):
             base(r, 0, BANK, None, (1,))
+        exp_and_sum(0)
+        cast_scalar(4, 0)
+        cast_scalar(4, 1)
+        add_bias(1)
+        cast_vector(5, 0)
+        cast_vector(5, 1)
+        invert_sum(0)
+        scale_weights(0)
+        row_max(1)
+        copy_u(1, 0, on_scalar)
         gate_tokens(0)
-        copy_u(1, 1, on_scalar)
-        exp_and_sum(1)
-        gate_tokens(1)
         cast_scalar(6, 0)
+        exp_and_sum(1)
+        copy_u(1, 1, on_scalar)
+        gate_tokens(1)
         cast_scalar(7, 0)
-        invert_sum(1)
+        cast_scalar(7, 1)
         cast_vector(6, 1)
-        cast_vector(7, 1)
+        invert_sum(1)
 
-        turn_x(4, 4)
-        turn_z((0, 1), 1)
-        turn_x(5, 3)
-        turn_x(6, 0)
+        turn_x(4, 3)
+        turn_x(5, 1)
         scale_vector(4, 0)
-        scale_vector(4, 1)
         normalise(2)
         normalise(3)
+        scale_vector(4, 1)
+        turn_z((0, 1), 7)
+        turn_x(6, 0)
+        turn_x(7, 2)
+        turn_gates((2, 3), 3)
         copy_z(0)
         copy_z(1)
-        turn_x(7, 2)
-        turn_gates((2, 3), 4)
         scale_vector(5, 0)
-        quantize_z(0)
         scale_vector(5, 1)
+        quantize_z(0)
         quantize_z(1)
         gate(2)
-        base(0, BANK, BANK, 1)
+        base(0, BANK, BANK, 7)
         lora(0, 0, BANK)
-        base(1, BANK, BANK, 3)
+        base(1, BANK, BANK, 1)
         lora(1, 0, BANK)
         lora(0, BANK, BANK)
         lora(1, BANK, BANK)
@@ -577,11 +533,9 @@ def tile_rankwisemoloradenserouter_d2p_kernel(
         quantize_x(3, 0)
         quantize_x(3, 1)
         gate(3)
-        quantize_z(3)
-        copy_y(0, 0, BANK, on_scalar)
+        store(0, 0, BANK, on_scalar)
         store(1, 0, BANK, on_scalar)
-        copy_y(0, BANK, BANK, on_vector)
-        store_y(0, 0, F)
+        store(0, BANK, BANK, on_scalar)
         base(2, BANK, BANK, 0)
         open_logits((2, 3), 2)
         for r in range(4, TILES):
@@ -589,38 +543,39 @@ def tile_rankwisemoloradenserouter_d2p_kernel(
         lora(2, 0, BANK)
         lora(2, BANK, BANK)
         add_bias(2)
+        quantize_z(3)
         add_bias(3)
         row_max(2)
         row_max(3)
         store(1, BANK, BANK, on_scalar)
-        down_late(0, 4)
-        down_late(1, 6)
+        down_late(0, 3)
+        down_late(1, 4)
         copy_y(2, 0, BANK, on_scalar)
         exp_and_sum(2)
         exp_and_sum(3)
         copy_y(2, BANK, BANK, on_vector)
         store_y(2, 0, F)
-        down_late(2, 7)
-        down_late(3, 3)
-        base_and_lora(3, 0, BANK, 1)
-        copy_u_late(0, on_vector)
+        down_late(2, 5)
+        down_late(3, 1)
+        base_and_lora(3, 0, BANK, 7)
         invert_sum(2)
         invert_sum(3)
         for r in range(4, TILES):
             normalise(r)
-        for c in range(1, 4):
+        for c in range(3):
             copy_u_late(c, on_scalar)
+        copy_u_late(3, on_vector)
         store(3, 0, BANK, on_scalar)
 
-        turn_gates((4, 5), 5)
+        turn_gates((4, 5), 6)
         turn_gates((6, 7), 0)
         gate_late(4)
         quantize_z(4)
         gate_late(5)
         quantize_z(5)
         base_and_lora(3, BANK, BANK, 2)
-        base(4, 0, BANK, 4)
-        base(4, BANK, BANK, 6)
+        base(4, 0, BANK, 3)
+        base(4, BANK, BANK, 4)
         lora(4, 0, BANK)
         lora(4, BANK, BANK)
         store(3, BANK, BANK, on_scalar)
@@ -629,14 +584,14 @@ def tile_rankwisemoloradenserouter_d2p_kernel(
         store(4, BANK, BANK, on_scalar)
         gate_late(7)
         quantize_z(6)
-        base_and_lora(5, 0, BANK, 1)
+        base_and_lora(5, 0, BANK, 7)
         quantize_z(7)
-        store(5, 0, BANK, on_vector)
-        base_and_lora(5, BANK, BANK, 7)
-        store(5, BANK, BANK, on_scalar)
-        base_and_lora(6, 0, BANK, 3)
-        store(6, 0, BANK, on_vector)
+        store(5, 0, BANK, on_scalar)
+        base_and_lora(5, BANK, BANK, 5)
+        store(5, BANK, BANK, on_vector)
+        base_and_lora(6, 0, BANK, 1)
+        store(6, 0, BANK, on_scalar)
         pieces = [(6, c0) for c0 in range(BANK, F, QUARTER)] + [(7, c0) for c0 in range(0, F, QUARTER)]
-        for i, ((r, c0), b) in enumerate(zip(pieces, (2, 5, 4, 6, 0, 1))):
+        for i, ((r, c0), b) in enumerate(zip(pieces, (2, 6, 3, 4, 0, 7))):
             base_and_lora(r, c0, QUARTER, b)
-            store(r, c0, QUARTER, on_vector if i % 2 else on_scalar)
+            store(r, c0, QUARTER, on_scalar if i % 2 else on_vector)

@@ -416,11 +416,11 @@ def tile_rankwisemoloradenserouter_d2p_kernel(
         load_codes(a_in[:], a_words, 0, R)
         load_codes(wr_both[:], wr_words, 0, E)
         load_scales(wr_sc, wr_scales)
+        load_x(3)
         load_codes(w0_first[0][:], w0_words[0:1], 0, BANK)
         load_scales(w0_sc, w0_scales)
-        load_x(3)
-        load_codes(w0_first[1][:], w0_words[1:2], 0, BANK)
         load_x(4)
+        load_codes(w0_first[1][:], w0_words[1:2], 0, BANK)
         load_codes(w0_second[:], w0_words, BANK, BANK)
         load_codes(b_codes[0][:], b_words, 0, BANK)
         load_scales(b_sc, b_scales)
@@ -444,7 +444,6 @@ def tile_rankwisemoloradenserouter_d2p_kernel(
         for r in (2, 3):
             for g in range(2):
                 turn_x_half(r, g, 2 * r + g - 1)
-        warm_up(1, 7)
         scale_vector(0, 0)
         scale_vector(0, 1)
         quantize_x_half(0, 0)
@@ -452,61 +451,62 @@ def tile_rankwisemoloradenserouter_d2p_kernel(
         quantize_x_half(0, 1)
         scale_vector(2, 0)
         quantize_x_half(1, 0)
-        scale_vector(3, 0)
-        for r in (1, 2, 3):
-            scale_scalar(r, 1)
+        scale_scalar(1, 1)
+        scale_scalar(3, 1)
         quantize_x_half(1, 1)
+        scale_vector(3, 0)
+        scale_vector(2, 1)
         down_tokens(0, 7)
         spread_bias(1)
         open_logits((0,), 0)
         router(0)
         router(1)
         down_tokens(1, 2)
-        copy_bias()
         quantize_x(1, 0)
         quantize_x(1, 1)
+        order_a_scales(0)
         order_a_codes(0, on_scalar)
+        copy_bias()
         order_a_codes(1, on_scalar)
         add_bias(0)
-        order_a_scales(0)
-        row_max(0)
         order_a_scales(1)
+        row_max(0)
         open_logits((1,), 3)
         router(2)
         router(3)
+        down(1, 0, 1)
+        down(1, 1, 0)
         base(0, 0, BANK, 4, (0,))
         base(1, 0, BANK, 5, (0,))
         base(2, 0, BANK, 6, (0,))
-        down(1, 0, 1)
-        down(1, 1, 0)
         for r in range(3):
             base(r, 0, BANK, None, (1,))
-        exp_and_sum(0)
         cast_scalar(4, 0)
         cast_scalar(4, 1)
+        cast_scalar(5, 0)
+        exp_and_sum(0)
         add_bias(1)
-        cast_vector(5, 0)
         cast_vector(5, 1)
+        cast_vector(6, 1)
         invert_sum(0)
         scale_weights(0)
         row_max(1)
         copy_u(1, 0, on_scalar)
+        copy_u(1, 1, on_scalar)
         gate_tokens(0)
         cast_scalar(6, 0)
         exp_and_sum(1)
-        copy_u(1, 1, on_scalar)
         gate_tokens(1)
         cast_scalar(7, 0)
         cast_scalar(7, 1)
-        cast_vector(6, 1)
         invert_sum(1)
 
         turn_x(4, 3)
         turn_x(5, 1)
         scale_vector(4, 0)
+        scale_vector(4, 1)
         normalise(2)
         normalise(3)
-        scale_vector(4, 1)
         turn_z((0, 1), 7)
         turn_x(6, 0)
         turn_x(7, 2)

@@ -419,8 +419,8 @@ def tile_rankwisemoloradenserouter_d2p_kernel(
         load_x(3)
         load_codes(w0_first[0][:], w0_words[0:1], 0, BANK)
         load_scales(w0_sc, w0_scales)
-        load_x(4)
         load_codes(w0_first[1][:], w0_words[1:2], 0, BANK)
+        load_x(4)
         load_codes(w0_second[:], w0_words, BANK, BANK)
         load_codes(b_codes[0][:], b_words, 0, BANK)
         load_scales(b_sc, b_scales)
@@ -444,6 +444,7 @@ def tile_rankwisemoloradenserouter_d2p_kernel(
         for r in (2, 3):
             for g in range(2):
                 turn_x_half(r, g, 2 * r + g - 1)
+        warm_up(1, 7)
         scale_vector(0, 0)
         scale_vector(0, 1)
         quantize_x_half(0, 0)
@@ -487,7 +488,6 @@ def tile_rankwisemoloradenserouter_d2p_kernel(
         exp_and_sum(0)
         add_bias(1)
         cast_vector(5, 1)
-        cast_vector(6, 1)
         invert_sum(0)
         scale_weights(0)
         row_max(1)
@@ -499,6 +499,7 @@ def tile_rankwisemoloradenserouter_d2p_kernel(
         gate_tokens(1)
         cast_scalar(7, 0)
         cast_scalar(7, 1)
+        cast_vector(6, 1)
         invert_sum(1)
 
         turn_x(4, 3)

@@ -514,15 +514,15 @@ def tile_rankwisemoloradenserouter_d2p_kernel(
         turn_gates((2, 3), 3)
         copy_z(0)
         copy_z(1)
-        scale_vector(5, 0)
-        scale_vector(5, 1)
         quantize_z(0)
+        scale_vector(5, 0)
         quantize_z(1)
+        scale_vector(5, 1)
         gate(2)
         base(0, BANK, BANK, 7)
         lora(0, 0, BANK)
-        base(1, BANK, BANK, 1)
         lora(1, 0, BANK)
+        base(1, BANK, BANK, 1)
         lora(0, BANK, BANK)
         lora(1, BANK, BANK)
         for r in (6, 7):

from contextlib import ExitStack

import concourse.mybir as mybir
from concourse.masks import make_identity

T, D, F, E, R = 1024, 1024, 1024, 128, 512
FLOPS = 2 * T * D * (F + E + R) + 2 * T * R * F

F32 = mybir.dt.float32
BF16 = mybir.dt.bfloat16
I32 = mybir.dt.int32
U32 = mybir.dt.uint32
U8 = mybir.dt.uint8
FP8 = mybir.dt.float8_e4m3fn
FP8X4 = mybir.dt.float8_e4m3fn_x4
MULT = mybir.AluOpType.mult
ADD = mybir.AluOpType.add
MAX = mybir.AluOpType.max
AX = mybir.AxisListType.X
ACT = mybir.ActivationFunctionType

P = 128
TILES = T // P
PAIRS = TILES // 2
PASS = 512
BANK = 512
QUARTER = 256
EARLY = TILES // 2
QUAD = 32

FIRST, SECOND = slice(0, 1), slice(1, 2)

X_LOADS = ((0, 1), (1, 2), (2, 4), (4, 6), (6, 8))


def tile_rankwisemoloradenserouter_d2p_kernel(
    tc, x_bytes, x_scale, w0_words, w0_scales, wr_words, wr_scales, br, a_words, a_scales, b_words, b_scales, out
):
    nc = tc.nc
    with ExitStack() as ctx:
        keep = ctx.enter_context(tc.tile_pool(name="keep", bufs=1))
        psum = ctx.enter_context(tc.psum_pool(name="psum", bufs=1))
        ctx.enter_context(tc.manual_schedule())

        def sbuf(shape, dtype, name):
            return keep.tile(shape, dtype, align_bytes=256, name=name)

        def sbuf_each(keys, shape, dtype, name):
            return {key: sbuf(shape, dtype, f"{name}_{i}") for i, key in enumerate(keys)}

        def bank(index, shape, name):
            return psum.tile(shape, F32, tag=f"bank{index}", bufs=1, name=name)

        zeros = sbuf([P, BANK], BF16, "zeros")
        ones = sbuf([P, P], BF16, "ones")
        ident = sbuf([P, P], F32, "ident")
        br_rows = sbuf([P, E], BF16, "br_rows")
        br_spread = sbuf([P, E], F32, "br_spread")
        scale_one = sbuf([P, 1], F32, "scale_one")
        scale_rows = sbuf([P, QUAD], F32, "scale_rows")
        scale_cols = sbuf([P, QUAD], F32, "scale_cols")
        wr_sc = sbuf([P, E], U8, "wr_sc")
        a_sc_in = sbuf([P, R], U8, "a_sc_in")
        a_sc = sbuf([P, R], U8, "a_sc")
        w0_sc = sbuf([P, F], U8, "w0_sc")
        b_sc = sbuf([P, F], U8, "b_sc")
        x_raw = {(r0, r1): sbuf([P, r1 - r0, D], U8, f"x_raw{r0}") for r0, r1 in X_LOADS}
        wr_both = sbuf([P, 2, E], I32, "wr_both")
        a_in = sbuf([P, 2, R], I32, "a_in")
        a_codes = sbuf_each(range(2), [P, R], I32, "a_codes")
        w0_first = sbuf_each(range(2), [P, 1, BANK], I32, "w0_first")
        w0_second = sbuf([P, 2, BANK], I32, "w0_second")
        wr_codes = [wr_both[:, g] for g in range(2)]
        w0_codes = [[w0_first[g][:, 0] for g in range(2)], [w0_second[:, g] for g in range(2)]]
        b_codes = sbuf_each(range(2), [P, 1, BANK], I32, "b_codes")

        x_view = x_bytes.rearrange("(r p) k -> p r k", p=P)
        out_view = out.rearrange("(r p) f -> p r f", p=P)

        def load_x(i):
            r0, r1 = X_LOADS[i]
            nc.sync.dma_start(out=x_raw[r0, r1][:], in_=x_view[:, r0:r1, :])

        def load_codes(tile, words, c0, width):
            rows = words.rearrange("g p n t -> p g (n t)")
            nc.sync.dma_start(out=tile, in_=rows[:, :, 4 * c0 : 4 * (c0 + width)].bitcast(I32))

        def load_scales(plane, scales):
            for quadrant in range(4):
                nc.sync.dma_start(
                    out=plane[32 * quadrant : 32 * quadrant + 4 * scales.shape[0], :].bitcast(I32),
                    in_=scales[:, 4 * quadrant : 4 * quadrant + 4, :].bitcast(I32),
                )

        def load_x_scale():
            by_quadrant = x_scale.rearrange("r (g q) -> q (r g)", q=4)
            nc.scalar.dma_start(out=scale_one[0:P:2, :], in_=by_quadrant.unsqueeze(2))

        def spread_x_scale():
            nc.vector.tensor_copy(out=scale_rows[:], in_=scale_one[:].to_broadcast([P, QUAD]))

        def turn_x_scale():
            nc.vector.transpose(out=scale_cols[:], in_=scale_rows[:])

        halves = [(r, g) for r in range(TILES) for g in range(2)]
        pair_passes = [(h, g) for h in range(PAIRS) for g in range(2)]
        x_wide = sbuf_each(halves, [P, PASS], BF16, "x_wide")
        x_in = sbuf_each(pair_passes, [P, 2 * PASS], BF16, "x_in")
        quad_passes = [(q, g) for q in range(2) for g in range(2)]
        x_quad = sbuf_each(quad_passes, [P, 4 * P], U32, "x_codes")
        x_quad_sc = sbuf_each(quad_passes, [P, 4 * P], U8, "x_sc")
        x_codes = {(h, g): x_quad[h // 2, g][:, 2 * P * (h % 2) : 2 * P * (h % 2 + 1)] for h, g in pair_passes}
        x_sc = {(h, g): x_quad_sc[h // 2, g][:, 2 * P * (h % 2) : 2 * P * (h % 2 + 1)] for h, g in pair_passes}
        u_late = sbuf([P, 4, 4 * P], F32, "u_late")
        logit = sbuf_each(range(PAIRS), [P, 2, E], F32, "logit")
        weight = sbuf_each(range(PAIRS), [P, 2, E], F32, "weight")
        gates = sbuf_each(range(TILES), [P, E], F32, "gates")
        u_runs = sbuf_each(range(PAIRS), [P, 2, 4 * P], F32, "u_runs")
        neg_max = sbuf_each(range(PAIRS), [P, 2], F32, "neg_max")
        total = sbuf_each(range(PAIRS), [P, 2], F32, "total")
        inv_total = sbuf_each(range(PAIRS), [P, 2], F32, "inv_total")
        weight_e = sbuf_each(range(PAIRS), [P, 2, E], F32, "weight_e")
        z_wide = sbuf_each(range(TILES), [P, R], BF16, "z_wide")
        z_in = sbuf_each(range(PAIRS), [P, 2 * R], BF16, "z_in")
        z_codes = sbuf_each(range(PAIRS), [P, 2 * P], U32, "z_codes")
        z_sc = sbuf_each(range(PAIRS), [P, 2 * P], U8, "z_sc")
        y_out = sbuf_each(range(TILES), [P, F], F32, "y_out")
        xt_ps, zt_ps, gt_ps, l_ps, u_ps, y_ps, br_ps = {}, {}, {}, {}, {}, {}, {}
        on_scalar, on_vector = nc.scalar.copy, nc.vector.tensor_copy

        def tile_cols(r):
            return slice(P * (r % 2), P * (r % 2) + P)

        def x_half(r, g):
            r0, r1 = [run for run in X_LOADS if run[0] <= r < run[1]][0]
            return x_raw[r0, r1][:, r - r0, PASS * g : PASS * g + PASS].bitcast(FP8)

        def cast_vector(r, g):
            nc.vector.tensor_copy(
                out=x_wide[r, g][:].rearrange("p (s q e) -> p q s e", s=2, e=2),
                in_=x_half(r, g).rearrange("p (q s e) -> p q s e", s=2, e=2),
            )

        def cast_scalar(r, g):
            nc.scalar.copy(
                out=x_wide[r, g][:].rearrange("p (s q e) -> p s q e", s=2, e=2),
                in_=x_half(r, g).rearrange("p (q s e) -> p s q e", s=2, e=2),
            )

        def scale_views(r, g):
            dest = x_in[r // 2, g][:, PASS * (r % 2) : PASS * (r % 2) + PASS]
            turned = xt_ps[r, g].bitcast(BF16).rearrange("p s (n e) -> p n s e", e=2)
            col = 2 * (2 * r + g)
            return dest.rearrange("p (n s e) -> p n s e", s=2, e=2), turned, scale_cols[:, col : col + 1]

        def scale_vector(r, g):
            dest, turned, scale = scale_views(r, g)
            nc.vector.tensor_scalar(out=dest, in0=turned, scalar1=scale, scalar2=None, op0=MULT)

        def scale_scalar(r, g):
            dest, turned, scale = scale_views(r, g)
            nc.scalar.activation(out=dest, in_=turned, func=ACT.Copy, scale=scale)

        def turn_x_into(r, g, dest):
            xt_ps[r, g] = dest
            words = x_wide[r, g][:].bitcast(F32)
            for s in range(2):
                nc.tensor.transpose(dest[:, s, :], words[:, P * s : P * s + P], ident[:])

        def turn_x(r, b, passes=(0, 1)):
            dest = bank(b, [P, 2, 2, P], f"xt_ps{r}")
            for g in passes:
                turn_x_into(r, g, dest[:, g])

        def turn_x_half(r, g, b):
            turn_x_into(r, g, bank(b, [P, 2, P], f"xt_ps{r}_{g}")[:])

        def quantize_x_half(r, g):
            h, i = divmod(r, 2)
            nc.vector.quantize_mx(
                out=x_codes[h, g][:, tile_cols(r)].bitcast(FP8X4),
                scales=x_sc[h, g][:, tile_cols(r)],
                in_=x_in[h, g][:, PASS * i : PASS * i + PASS],
            )

        def quantize_x(h, g):
            nc.vector.quantize_mx(out=x_codes[h, g][:].bitcast(FP8X4), scales=x_sc[h, g][:], in_=x_in[h, g][:])

        def order_a_codes(g, copy):
            copy(
                out=a_codes[g][:].bitcast(U32).rearrange("p (c b i) -> p b c i", c=4, i=4),
                in_=a_in[:, g].bitcast(U32).rearrange("p (b i c) -> p b c i", c=4, i=4),
            )

        def order_a_scales(s):
            nc.vector.tensor_copy(
                out=a_sc[:].rearrange("p (c b i) -> p b c i", c=4, i=16)[:, :, 2 * s : 2 * s + 2],
                in_=a_sc_in[:].rearrange("p (b i c) -> p b c i", c=4, i=16)[:, :, 2 * s : 2 * s + 2],
            )

        def warm_up(count, b):
            scrap = bank(b, [P, BANK], "scrap")
            for i in range(count):
                nc.tensor.matmul(scrap[:], lhsT=zeros[:, :P], rhs=zeros[:], start=True, stop=True)

        def spread_bias(b):
            br_ps[0] = bank(b, [P, E], "br_ps")
            nc.tensor.matmul(br_ps[0][:], lhsT=ones[:], rhs=br_rows[:], start=True, stop=True)

        def copy_bias():
            nc.scalar.copy(out=br_spread[:], in_=br_ps[0][:])

        def x_product(dest, r, codes, c, plane, c0, width, close, passes=(0, 1)):
            for g in passes:
                nc.tensor.matmul_mx(
                    out=dest,
                    lhsT=x_codes[r // 2, g][:, tile_cols(r)].bitcast(FP8X4),
                    lhsT_scale=x_sc[r // 2, g][:, tile_cols(r)],
                    rhs=codes[g][:, c : c + width].bitcast(FP8X4),
                    rhs_scale=plane[4 * g :, c0 : c0 + width],
                    start=(g == 0),
                    stop=(close and g == 1),
                )

        def open_logits(pairs, b):
            dest = bank(b, [P, len(pairs), 2, E], f"l_ps{pairs[0]}")
            for j, h in enumerate(pairs):
                l_ps[h] = dest[:, j]

        def router(r):
            x_product(l_ps[r // 2][:, r % 2, :], r, wr_codes, 0, wr_sc, 0, E, True)

        def down(h, s, b):
            u_ps[h, s] = bank(b, [P, 2, 2 * P], f"u_ps{h}_{s}")
            for e in range(2):
                cols = slice(P * (2 * s + e), P * (2 * s + e) + P)
                for g in range(2):
                    nc.tensor.matmul_mx(
                        out=u_ps[h, s][:, e, :],
                        lhsT=a_codes[g][:, cols].bitcast(FP8X4),
                        lhsT_scale=a_sc[4 * g :, cols],
                        rhs=x_codes[h, g][:].bitcast(FP8X4),
                        rhs_scale=x_sc[h, g][:],
                        start=(g == 0),
                        stop=(g == 1),
                    )

        def down_late(c, b):
            u_ps["late", c] = bank(b, [P, 4 * P], f"u_ps_late{c}")
            cols = slice(P * c, P * c + P)
            for g in range(2):
                nc.tensor.matmul_mx(
                    out=u_ps["late", c][:],
                    lhsT=a_codes[g][:, cols].bitcast(FP8X4),
                    lhsT_scale=a_sc[4 * g :, cols],
                    rhs=x_quad[1, g][:].bitcast(FP8X4),
                    rhs_scale=x_quad_sc[1, g][:],
                    start=(g == 0),
                    stop=(g == 1),
                )

        def down_tokens(r, b):
            u_ps[r] = bank(b, [P, R], f"u_ps{r}")
            x_product(u_ps[r][:], r, [a_in[:, g] for g in range(2)], 0, a_sc_in, 0, R, True)

        def base(r, c0, width, b, passes=(0, 1)):
            if 0 in passes:
                y_ps[r, c0] = bank(b, [P, width], f"y_ps{r}_{c0}")
            f, c = divmod(c0, BANK)
            x_product(y_ps[r, c0][:], r, w0_codes[f], c, w0_sc, c0, width, False, passes)

        def lora(r, c0, width):
            f, c = divmod(c0, BANK)
            nc.tensor.matmul_mx(
                out=y_ps[r, c0][:],
                lhsT=z_codes[r // 2][:, tile_cols(r)].bitcast(FP8X4),
                lhsT_scale=z_sc[r // 2][:, tile_cols(r)],
                rhs=b_codes[f][:, 0, c : c + width].bitcast(FP8X4),
                rhs_scale=b_sc[:, c0 : c0 + width],
                start=False,
                stop=True,
            )

        def base_and_lora(r, c0, width, b):
            base(r, c0, width, b)
            lora(r, c0, width)

        def copy_y(r, c0, width, copy):
            copy(out=y_out[r][:, c0 : c0 + width], in_=y_ps[r, c0][:])

        def store_y(r, c0, width):
            dest = out_view[:, r, c0 : c0 + width]
            nc.sync.dma_start(out=dest, in_=y_out[r][:, c0 : c0 + width])

        def store(r, c0, width, copy):
            copy_y(r, c0, width, copy)
            store_y(r, c0, width)

        def add_bias(h):
            nc.vector.tensor_tensor(
                out=logit[h][:], in0=l_ps[h], in1=br_spread[:].unsqueeze(1).to_broadcast([P, 2, E]), op=ADD
            )

        def row_max(h, part=slice(0, 2)):
            nc.vector.tensor_reduce(out=neg_max[h][:, part], in_=logit[h][:, part], axis=AX, op=MAX, negate=True)

        def exp_and_sum(h, tiles=(0, 1)):
            for i in tiles:
                nc.scalar.activation(
                    out=weight[h][:, i, :],
                    in_=logit[h][:, i, :],
                    func=ACT.Exp,
                    bias=neg_max[h][:, i : i + 1],
                    accum_out=total[h][:, i : i + 1],
                )

        def invert_sum(h, part=slice(0, 2)):
            nc.vector.reciprocal(out=inv_total[h][:, part], in_=total[h][:, part])

        def normalise(r):
            h, i = divmod(r, 2)
            nc.vector.tensor_scalar(
                out=gates[r][:],
                in0=weight[h][:, i, :],
                scalar1=inv_total[h][:, i : i + 1],
                scalar2=float(E),
                op0=MULT,
                op1=MULT,
            )

        def scale_weights(h):
            nc.vector.tensor_scalar(out=weight_e[h][:], in0=weight[h][:], scalar1=float(E), scalar2=None, op0=MULT)

        def gate_tokens(r, runs=(0, 1)):
            h, i = divmod(r, 2)
            for s in runs:
                nc.vector.scalar_tensor_tensor(
                    out=z_wide[r][:, 2 * E * s : 2 * E * s + 2 * E].rearrange("p (e c) -> p e c", c=2),
                    in0=u_ps[r][:].rearrange("p (e s c) -> p s e c", s=2, c=2)[:, s],
                    scalar=inv_total[h][:, i : i + 1],
                    in1=weight_e[h][:, i, :].unsqueeze(2).to_broadcast([P, E, 2]),
                    op0=MULT,
                    op1=MULT,
                )

        def turn_z(tiles, b):
            dest = bank(b, [P, len(tiles), 2, P], f"zt_ps{tiles[0]}")
            for i, r in enumerate(tiles):
                zt_ps[r] = dest[:, i]
                words = z_wide[r][:].bitcast(F32)
                for s in range(2):
                    nc.tensor.transpose(zt_ps[r][:, s, :], words[:, P * s : P * s + P], ident[:])

        def copy_z(r):
            dest = z_in[r // 2][:, R * (r % 2) : R * (r % 2) + R]
            nc.scalar.copy(
                out=dest.bitcast(F32).rearrange("p (n s) -> p n s", s=2), in_=zt_ps[r].rearrange("p s n -> p n s")
            )

        def turn_gates(tiles, b):
            dest = bank(b, [P, len(tiles), P], f"gt_ps{tiles[0]}")
            for j, r in enumerate(tiles):
                gt_ps[r] = dest[:, j]
                nc.tensor.transpose(gt_ps[r], gates[r][:], ident[:])

        def copy_u(h, s, copy):
            copy(
                out=u_runs[h][:, s].rearrange("p (n e) -> p n e", e=2),
                in_=u_ps[h, s][:].rearrange("p e n -> p n e"),
            )

        def gate(r):
            h, i = divmod(r, 2)
            nc.vector.tensor_tensor(
                out=z_in[h][:, R * i : R * i + R].rearrange("p (n s e) -> p n s e", s=2, e=2),
                in0=gt_ps[r].unsqueeze(2).unsqueeze(3).to_broadcast([P, P, 2, 2]),
                in1=u_runs[h][:, :, 2 * P * i : 2 * P * i + 2 * P].rearrange("p s (n e) -> p n s e", e=2),
                op=MULT,
            )

        def copy_u_late(c, copy):
            copy(out=u_late[:, c], in_=u_ps["late", c][:])

        def gate_late(r):
            h, i = divmod(r, 2)
            n0 = P * (r - EARLY)
            nc.vector.tensor_tensor(
                out=z_in[h][:, R * i : R * i + R].rearrange("p (m j c) -> p m c j", j=2, c=4),
                in0=gt_ps[r].rearrange("p (m j) -> p m j", j=2).unsqueeze(2).to_broadcast([P, P // 2, 4, 2]),
                in1=u_late[:, :, n0 : n0 + P].rearrange("p c (m j) -> p m c j", j=2),
                op=MULT,
            )

        def quantize_z(r):
            h, i = divmod(r, 2)
            nc.vector.quantize_mx(
                out=z_codes[h][:, tile_cols(r)].bitcast(FP8X4),
                scales=z_sc[h][:, tile_cols(r)],
                in_=z_in[h][:, R * i : R * i + R],
            )


        nc.gpsimd.memset(scale_one[:], 0.0)
        nc.vector.memset(zeros[:], 0.0)
        nc.vector.memset(br_rows[:], 0.0)
        for plane in (a_sc_in, wr_sc, w0_sc, b_sc):
            nc.vector.memset(plane[:].bitcast(I32), 0)
        make_identity(nc, ident[:])
        load_x_scale()
        nc.scalar.activation(out=ones[:], in_=zeros[:, :P], func=ACT.Exp)
        load_x(0)
        load_x(1)
        load_x(2)
        nc.sync.dma_start(out=br_rows[0:1, :], in_=br.unsqueeze(0))
        load_scales(a_sc_in, a_scales)
        load_codes(a_in[:], a_words, 0, R)
        load_codes(wr_both[:], wr_words, 0, E)
        load_scales(wr_sc, wr_scales)
        load_x(3)
        load_codes(w0_first[0][:], w0_words[0:1], 0, BANK)
        load_scales(w0_sc, w0_scales)
        load_codes(w0_first[1][:], w0_words[1:2], 0, BANK)
        load_x(4)
        load_codes(w0_second[:], w0_words, BANK, BANK)
        load_codes(b_codes[0][:], b_words, 0, BANK)
        load_scales(b_sc, b_scales)
        load_codes(b_codes[1][:], b_words, BANK, BANK)

        warm_up(4, 7)
        cast_vector(0, 0)
        spread_x_scale()
        cast_scalar(0, 1)
        cast_vector(1, 0)
        turn_x_scale()
        cast_scalar(1, 1)
        cast_vector(2, 0)
        cast_scalar(2, 1)
        cast_scalar(3, 0)
        cast_scalar(3, 1)
        turn_x(0, 0)
        turn_x_half(1, 0, 1)
        turn_x_half(1, 1, 2)
        warm_up(1, 7)
        for r in (2, 3):
            for g in range(2):
                turn_x_half(r, g, 2 * r + g - 1)
        warm_up(1, 7)
        scale_vector(0, 0)
        scale_vector(0, 1)
        quantize_x_half(0, 0)
        scale_vector(1, 0)
        quantize_x_half(0, 1)
        scale_vector(2, 0)
        quantize_x_half(1, 0)
        scale_scalar(1, 1)
        scale_scalar(3, 1)
        quantize_x_half(1, 1)
        scale_vector(3, 0)
        scale_vector(2, 1)
        down_tokens(0, 7)
        spread_bias(1)
        open_logits((0,), 0)
        router(0)
        router(1)
        down_tokens(1, 2)
        quantize_x(1, 0)
        quantize_x(1, 1)
        order_a_scales(0)
        order_a_codes(0, on_scalar)
        copy_bias()
        order_a_codes(1, on_scalar)
        add_bias(0)
        order_a_scales(1)
        row_max(0)
        open_logits((1,), 3)
        router(2)
        router(3)
        down(1, 0, 1)
        down(1, 1, 0)
        base(0, 0, BANK, 4, (0,))
        base(1, 0, BANK, 5, (0,))
        base(2, 0, BANK, 6, (0,))
        for r in range(3):
            base(r, 0, BANK, None, (1,))
        cast_scalar(4, 0)
        cast_scalar(4, 1)
        cast_scalar(5, 0)
        exp_and_sum(0)
        add_bias(1)
        cast_vector(5, 1)
        invert_sum(0)
        scale_weights(0)
        row_max(1)
        copy_u(1, 0, on_scalar)
        copy_u(1, 1, on_scalar)
        gate_tokens(0)
        cast_scalar(6, 0)
        exp_and_sum(1)
        gate_tokens(1)
        cast_scalar(7, 0)
        cast_scalar(7, 1)
        cast_vector(6, 1)
        invert_sum(1)

        turn_x(4, 3)
        turn_x(5, 1)
        scale_vector(4, 0)
        scale_vector(4, 1)
        normalise(2)
        normalise(3)
        turn_z((0, 1), 7)
        turn_x(6, 0)
        turn_x(7, 2)
        turn_gates((2, 3), 3)
        copy_z(0)
        copy_z(1)
        quantize_z(0)
        scale_vector(5, 0)
        quantize_z(1)
        scale_vector(5, 1)
        gate(2)
        base(0, BANK, BANK, 7)
        lora(0, 0, BANK)
        lora(1, 0, BANK)
        base(1, BANK, BANK, 1)
        lora(0, BANK, BANK)
        lora(1, BANK, BANK)
        for r in (6, 7):
            for g in range(2):
                scale_scalar(r, g)
        quantize_x(2, 0)
        quantize_z(2)
        quantize_x(2, 1)
        quantize_x(3, 0)
        quantize_x(3, 1)
        gate(3)
        store(0, 0, BANK, on_scalar)
        store(1, 0, BANK, on_scalar)
        store(0, BANK, BANK, on_scalar)
        base(2, BANK, BANK, 0)
        open_logits((2, 3), 2)
        for r in range(4, TILES):
            router(r)
        lora(2, 0, BANK)
        lora(2, BANK, BANK)
        add_bias(2)
        quantize_z(3)
        add_bias(3)
        row_max(2)
        row_max(3)
        store(1, BANK, BANK, on_scalar)
        down_late(0, 3)
        down_late(1, 4)
        copy_y(2, 0, BANK, on_scalar)
        exp_and_sum(2)
        exp_and_sum(3)
        copy_y(2, BANK, BANK, on_vector)
        store_y(2, 0, F)
        down_late(2, 5)
        down_late(3, 1)
        base_and_lora(3, 0, BANK, 7)
        invert_sum(2)
        invert_sum(3)
        for r in range(4, TILES):
            normalise(r)
        for c in range(3):
            copy_u_late(c, on_scalar)
        copy_u_late(3, on_vector)
        store(3, 0, BANK, on_scalar)

        turn_gates((4, 5), 6)
        turn_gates((6, 7), 0)
        gate_late(4)
        quantize_z(4)
        gate_late(5)
        quantize_z(5)
        base_and_lora(3, BANK, BANK, 2)
        base(4, 0, BANK, 3)
        base(4, BANK, BANK, 4)
        lora(4, 0, BANK)
        lora(4, BANK, BANK)
        store(3, BANK, BANK, on_scalar)
        gate_late(6)
        store(4, 0, BANK, on_scalar)
        store(4, BANK, BANK, on_scalar)
        gate_late(7)
        quantize_z(6)
        base_and_lora(5, 0, BANK, 7)
        quantize_z(7)
        store(5, 0, BANK, on_scalar)
        base_and_lora(5, BANK, BANK, 5)
        store(5, BANK, BANK, on_vector)
        base_and_lora(6, 0, BANK, 1)
        store(6, 0, BANK, on_scalar)
        pieces = [(6, c0) for c0 in range(BANK, F, QUARTER)] + [(7, c0) for c0 in range(0, F, QUARTER)]
        for i, ((r, c0), b) in enumerate(zip(pieces, (2, 6, 3, 4, 0, 7))):
            base_and_lora(r, c0, QUARTER, b)
            store(r, c0, QUARTER, on_scalar if i % 2 else on_vector)
